import numpy as np
import ml_dtypes


def mxq(x, axis, fmt="e4m3"):
    dtype, down = {"e4m3": (ml_dtypes.float8_e4m3fn, 7), "e5m2": (ml_dtypes.float8_e5m2, 14)}[fmt]
    v = np.moveaxis(np.asarray(x, np.float32).astype(ml_dtypes.bfloat16).astype(np.float64), axis, -1)
    blocks = v.reshape(v.shape[:-1] + (-1, 32))
    amax = np.abs(blocks).max(-1, keepdims=True)
    byte = np.maximum(np.where(amax > 0, np.frexp(amax)[1] - 1 + 127, 0) - down, 1)
    scale = np.exp2(byte - 127.0)
    codes = (blocks / scale).astype(np.float32).astype(dtype).astype(np.float64)
    return np.moveaxis((codes * scale).reshape(v.shape), -1, axis)


WIDE = False


def mx_kscale(k):
    if not WIDE:
        return np.ones(k)
    levels = np.array([18, -18])
    if k % 512:
        return np.exp2(np.random.permutation(np.resize(levels, k // 32))).repeat(32)
    a = np.empty((k // 512, 16))
    for p in range(k // 512):
        a[p, :8] = np.random.permutation(np.resize(levels, 8))
        for g in range(8):
            far = levels[np.abs(levels - a[p, g]) >= 10]
            a[p, g + 8] = far[np.random.randint(len(far))]
    return np.exp2(a.ravel()).repeat(32)


def f64(x):
    return np.asarray(x).astype(np.float64)


def striped(idx):
    return np.tile(np.asarray(idx).reshape(-1, 16).T, (8, 1)).astype(np.uint16)


def unstriped(offs):
    return offs[:16].T.reshape(-1).astype(np.int64)


V, K, E, D, DV = 512, 2, 1024, 512, 512


def setup_inputs():
    n = np.random.standard_normal
    v = mx_kscale(DV)[:, None]
    coarse = lambda x: x.astype(np.float32).astype(ml_dtypes.bfloat16).astype(np.float64)
    return {
        "dyT": (coarse(n((DV, V))) * v).astype(np.float32),
        "hE": (np.random.randint(-15, 16, (DV, E)) / 16.0).astype(np.float32),
        "wm": (n((DV, D)) / np.sqrt(DV) / v).astype(np.float32),
        "offs": striped(np.random.randint(0, V, E)),
        "offs2": striped(np.random.permutation(E)),
    }


def reference(dyT, hE, wm, offs, offs2):
    h = f64(hE)
    dz = f64(dyT)[:, unstriped(offs)] * (1.0 - h * h)
    dm = mxq(f64(wm), 0, "e4m3").T @ mxq(dz, 0, "e5m2")
    return dm[:, unstriped(offs2)].reshape(D, V, K).sum(-1)

@@ -1,0 +1,163 @@
+from contextlib import ExitStack
+
+import concourse.mybir as mybir
+
+V, K, E, D, DV = 512, 2, 1024, 512, 512
+FLOPS = 2 * DV * D * E
+
+F32 = mybir.dt.float32
+BF16 = mybir.dt.bfloat16
+U32 = mybir.dt.uint32
+U16 = mybir.dt.uint16
+U8 = mybir.dt.uint8
+E4M3 = mybir.dt.float8_e4m3fn_x4
+E5M2 = mybir.dt.float8_e5m2_x4
+MULT = mybir.AluOpType.mult
+ADD = mybir.AluOpType.add
+COPY = mybir.ActivationFunctionType.Copy
+SQUARE = mybir.ActivationFunctionType.Square
+
+P = 128
+PACK = 4
+N_TILE = 512
+STRIPE = 16
+
+
+def tile_attend_gmp_tnh_kernel(tc, dyT, hE, wm, offs, offs2, out):
+    nc = tc.nc
+    dy_rows = dyT.rearrange("(p t) v -> p t v", t=PACK)
+    h_rows = hE.rearrange("(p t) e -> p t e", t=PACK)
+    w_rows = wm.rearrange("(p t) d -> p t d", t=PACK)
+
+    with ExitStack() as ctx:
+        keep = ctx.enter_context(tc.tile_pool(name="keep", bufs=1))
+        psum = ctx.enter_context(tc.psum_pool(name="psum", bufs=1))
+
+        dst = keep.tile([P, E // STRIPE], U16, name="dst")
+        src = keep.tile([P, E // STRIPE], U16, name="src")
+        dy = [keep.tile([P, V], F32, name=f"dy{t}") for t in range(PACK)]
+        h_lo = [keep.tile([P, 512], F32, name=f"h_lo{t}") for t in range(PACK)]
+        h_hi = [keep.tile([P, 2, 256], F32, name=f"h_hi{i}") for i in range(4)]
+        w_first = keep.tile([P, PACK, P], F32, name="w_first")
+        w_rest = keep.tile([P, PACK, D - P], F32, name="w_rest")
+
+        warm = keep.tile([P, 8], F32, name="warm")
+        nc.vector.memset(warm[:], 0.0)
+        nc.scalar.activation(warm[:], warm[:], SQUARE)
+
+        nc.sync.dma_start(dst[:], offs)
+        nc.sync.dma_start(h_lo[0][:, 0:256], h_rows[:, 0, 0:256])
+        nc.sync.dma_start(dy[0][:], dy_rows[:, 0, :])
+        nc.sync.dma_start(h_lo[0][:, 256:512], h_rows[:, 0, 256:512])
+        for t in range(1, PACK):
+            nc.sync.dma_start(h_lo[t][:], h_rows[:, t, 0:512])
+            nc.sync.dma_start(dy[t][:], dy_rows[:, t, :])
+        for i in range(4):
+            e0, t0 = 512 + 256 * (i // 2), 2 * (i % 2)
+            nc.sync.dma_start(h_hi[i][:], h_rows[:, t0 : t0 + 2, e0 : e0 + 256])
+        nc.sync.dma_start(w_first[:], w_rows[:, :, 0:P])
+        nc.sync.dma_start(src[:], offs2)
+        nc.sync.dma_start(w_rest[:], w_rows[:, :, P:D])
+
+        chunks = [(0, 256), (256, 256), (512, 256), (768, 128), (896, 128)]
+        dz32 = [keep.tile([P, PACK, n], F32, name=f"dz32_{c}") for c, (e0, n) in enumerate(chunks)]
+        dz_codes = [keep.tile([P, N_TILE], U32, name=f"dz_codes{i}", align_bytes=64) for i in range(2)]
+        dz_scales = [keep.tile([P, N_TILE], U8, name=f"dz_scales{i}", align_bytes=64) for i in range(2)]
+        w_codes = [keep.tile([P, P], U32, name=f"w_codes{i}", align_bytes=64) for i in range(4)]
+        w_scales = [keep.tile([P, P], U8, name=f"w_scales{i}", align_bytes=64) for i in range(4)]
+        dm = [keep.tile([P, E], F32, name=f"dm{i}") for i in range(4)]
+        banks = [[psum.tile([P, N_TILE], F32, name=f"bank{i}_{j}") for j in range(2)] for i in range(4)]
+
+        def slope(h, on_vector):
+            nc.scalar.activation(h, h, SQUARE)
+            if on_vector:
+                nc.vector.tensor_scalar(h, h, -1.0, 1.0, MULT, ADD)
+            else:
+                nc.scalar.activation(h, h, COPY, bias=1.0, scale=-1.0)
+
+        def gather_dz(c, t, u):
+            e0, n = chunks[c]
+            nc.vector.tensor_tensor(
+                dz32[c][:, t, :], dy[t][:].indirect(dst[:, e0 // STRIPE : (e0 + n) // STRIPE]), u, MULT
+            )
+
+        def interleave(engine_copy, rows, name, tag):
+            n = rows.shape[2]
+            grouped = keep.tile([P, n * PACK], BF16, name=name, tag=tag, align_bytes=64)
+            engine_copy(
+                grouped[:].rearrange("p (c i t) -> p c t i", i=4, t=PACK),
+                rows.rearrange("p t (c i) -> p c t i", i=4),
+            )
+            return grouped
+
+        def quantize_dz(c, grouped):
+            e0, n = chunks[c]
+            half, c0 = divmod(e0, N_TILE)
+            nc.vector.quantize_mx(
+                dz_codes[half][:, c0 : c0 + n].bitcast(E5M2), dz_scales[half][:, c0 : c0 + n], grouped[:]
+            )
+
+        def quantize_w(i, grouped):
+            nc.vector.quantize_mx(w_codes[i][:].bitcast(E4M3), w_scales[i][:], grouped)
+
+        def product(i, half):
+            nc.tensor.matmul_mx(
+                banks[i][half][:],
+                lhsT=w_codes[i][:].bitcast(E4M3),
+                lhsT_scale=w_scales[i][:],
+                rhs=dz_codes[half][:].bitcast(E5M2),
+                rhs_scale=dz_scales[half][:],
+                start=True,
+                stop=True,
+            )
+            nc.scalar.copy(dm[i][:, half * N_TILE : (half + 1) * N_TILE], banks[i][half][:])
+
+        for t in range(PACK):
+            for c in range(2):
+                u = h_lo[t][:, 256 * c : 256 * (c + 1)]
+                slope(u, t == 0)
+                gather_dz(c, t, u)
+        slope(h_hi[0][:], True)
+        slope(h_hi[1][:], True)
+        for t in range(PACK):
+            gather_dz(2, t, h_hi[t // 2][:, t % 2, :])
+        g0 = interleave(nc.scalar.copy, dz32[0][:], "g0", "g0")
+        slope(h_hi[2][:], False)
+        slope(h_hi[3][:], False)
+        quantize_dz(0, g0)
+        for t in range(PACK):
+            gather_dz(3, t, h_hi[2 + t // 2][:, t % 2, 0:128])
+        g1 = interleave(nc.scalar.copy, dz32[1][:], "g1", "g1")
+        g2 = interleave(nc.scalar.copy, dz32[2][:], "g2", "g2")
+        for t in range(PACK):
+            gather_dz(4, t, h_hi[2 + t // 2][:, t % 2, 128:256])
+        gw0 = interleave(nc.scalar.copy, w_first[:], "gw0", "gw0")
+        g3 = interleave(nc.scalar.copy, dz32[3][:], "g3", "late")
+        quantize_dz(1, g1)
+        g4 = interleave(nc.vector.tensor_copy, dz32[4][:], "g4", "g4")
+        quantize_w(0, gw0[:])
+        quantize_dz(2, g2)
+        quantize_dz(3, g3)
+        quantize_dz(4, g4)
+        product(0, 0)
+        product(0, 1)
+        gw = interleave(nc.vector.tensor_copy, w_rest[:], "gw", "late")
+        for i in range(1, 4):
+            quantize_w(i, gw[:, (i - 1) * N_TILE : i * N_TILE])
+        for i in range(1, 4):
+            product(i, 0)
+            product(i, 1)
+
+        for i in range(4):
+            pieces = [(0, 512), (512, 512)] if i < 3 else [(0, 512), (512, 256), (768, 256)]
+            total = keep.tile([P, V], F32, name=f"total{i}")
+            for j, (c0, n) in enumerate(pieces):
+                picked = keep.tile([P, n], F32, name=f"picked{i}_{j}")
+                nc.vector.tensor_copy(picked[:], dm[i][:].indirect(src[:, c0 // STRIPE : (c0 + n) // STRIPE]))
+                x = slice(c0 // K, (c0 + n) // K)
+                adder = nc.vector if (i, j) == (3, 2) else nc.gpsimd
+                adder.tensor_tensor(total[:, x], picked[:, 0:n:2], picked[:, 1:n:2], ADD)
+                if i == 3:
+                    nc.sync.dma_start(out[i * P : (i + 1) * P, x], total[:, x])
+            if i < 3:
+                nc.sync.dma_start(out[i * P : (i + 1) * P, :], total[:])

@@ -36,8 +36,7 @@ def tile_attend_gmp_tnh_kernel(tc, dyT, hE, wm, offs, offs2, out):
         dst = keep.tile([P, E // STRIPE], U16, name="dst")
         src = keep.tile([P, E // STRIPE], U16, name="src")
         dy = [keep.tile([P, V], F32, name=f"dy{t}") for t in range(PACK)]
-        h_lo = [keep.tile([P, 512], F32, name=f"h_lo{t}") for t in range(PACK)]
-        h_hi = [keep.tile([P, 2, 256], F32, name=f"h_hi{i}") for i in range(4)]
+        h_tiles = []
         w_first = keep.tile([P, PACK, P], F32, name="w_first")
         w_rest = keep.tile([P, PACK, D - P], F32, name="w_rest")
 
@@ -45,40 +44,61 @@ def tile_attend_gmp_tnh_kernel(tc, dyT, hE, wm, offs, offs2, out):
         nc.vector.memset(warm[:], 0.0)
         nc.scalar.activation(warm[:], warm[:], SQUARE)
 
-        nc.sync.dma_start(dst[:], offs)
-        nc.sync.dma_start(h_lo[0][:, 0:256], h_rows[:, 0, 0:256])
-        nc.sync.dma_start(dy[0][:], dy_rows[:, 0, :])
-        nc.sync.dma_start(h_lo[0][:, 256:512], h_rows[:, 0, 256:512])
-        for t in range(1, PACK):
-            nc.sync.dma_start(h_lo[t][:], h_rows[:, t, 0:512])
+        def load_h(t0, t1, e0, e1):
+            tile = keep.tile([P, t1 - t0, e1 - e0], F32, name=f"h{t0}_{e0}")
+            h_tiles.append((t0, t1, e0, e1, tile))
+            nc.sync.dma_start(tile[:], h_rows[:, t0:t1, e0:e1])
+
+        def h_part(t0, t1, e0, e1):
+            for a0, a1, b0, b1, tile in h_tiles:
+                if a0 <= t0 and t1 <= a1 and b0 <= e0 and e1 <= b1:
+                    return tile[:, t0 - a0 : t1 - a0, e0 - b0 : e1 - b0]
+            raise ValueError("no such part")
+
+        def load_dy(t):
             nc.sync.dma_start(dy[t][:], dy_rows[:, t, :])
-        for i in range(4):
-            e0, t0 = 512 + 256 * (i // 2), 2 * (i % 2)
-            nc.sync.dma_start(h_hi[i][:], h_rows[:, t0 : t0 + 2, e0 : e0 + 256])
+
+        load_h(0, 1, 0, 256)
+        load_h(0, 1, 256, 768)
+        load_dy(0)
+        nc.sync.dma_start(dst[:], offs)
+        load_h(1, 2, 0, 256)
+        load_h(1, 2, 256, 768)
+        load_dy(1)
+        for t in range(2, PACK):
+            load_h(t, t + 1, 0, 768)
+            load_dy(t)
+        load_h(0, 2, 768, 1024)
+        load_h(2, 4, 768, 1024)
         nc.sync.dma_start(w_first[:], w_rows[:, :, 0:P])
         nc.sync.dma_start(src[:], offs2)
         nc.sync.dma_start(w_rest[:], w_rows[:, :, P:D])
 
         chunks = [(0, 256), (256, 256), (512, 256), (768, 128), (896, 128)]
         dz32 = [keep.tile([P, PACK, n], F32, name=f"dz32_{c}") for c, (e0, n) in enumerate(chunks)]
-        dz_codes = [keep.tile([P, N_TILE], U32, name=f"dz_codes{i}", align_bytes=64) for i in range(2)]
-        dz_scales = [keep.tile([P, N_TILE], U8, name=f"dz_scales{i}", align_bytes=64) for i in range(2)]
+        dz_codes = keep.tile([P, E], U32, name="dz_codes", align_bytes=64)
+        dz_scales = keep.tile([P, E], U8, name="dz_scales", align_bytes=64)
         w_codes = [keep.tile([P, P], U32, name=f"w_codes{i}", align_bytes=64) for i in range(4)]
         w_scales = [keep.tile([P, P], U8, name=f"w_scales{i}", align_bytes=64) for i in range(4)]
         dm = [keep.tile([P, E], F32, name=f"dm{i}") for i in range(4)]
         banks = [[psum.tile([P, N_TILE], F32, name=f"bank{i}_{j}") for j in range(2)] for i in range(4)]
 
-        def slope(h, on_vector):
-            nc.scalar.activation(h, h, SQUARE)
-            if on_vector:
-                nc.vector.tensor_scalar(h, h, -1.0, 1.0, MULT, ADD)
-            else:
-                nc.scalar.activation(h, h, COPY, bias=1.0, scale=-1.0)
+        def square(t0, t1, e0, e1):
+            nc.scalar.activation(h_part(t0, t1, e0, e1), h_part(t0, t1, e0, e1), SQUARE)
 
-        def gather_dz(c, t, u):
+        def flip_s(t0, t1, e0, e1):
+            nc.scalar.activation(h_part(t0, t1, e0, e1), h_part(t0, t1, e0, e1), COPY, bias=1.0, scale=-1.0)
+
+        def flip_v(t0, t1, e0, e1):
+            nc.vector.tensor_scalar(h_part(t0, t1, e0, e1), h_part(t0, t1, e0, e1), -1.0, 1.0, MULT, ADD)
+
+        def gather_dz(c, t):
             e0, n = chunks[c]
             nc.vector.tensor_tensor(
-                dz32[c][:, t, :], dy[t][:].indirect(dst[:, e0 // STRIPE : (e0 + n) // STRIPE]), u, MULT
+                dz32[c][:, t, :],
+                dy[t][:].indirect(dst[:, e0 // STRIPE : (e0 + n) // STRIPE]),
+                h_part(t, t + 1, e0, e0 + n)[:, 0, :],
+                MULT,
             )
 
         def interleave(engine_copy, rows, name, tag):
@@ -92,58 +112,60 @@ def tile_attend_gmp_tnh_kernel(tc, dyT, hE, wm, offs, offs2, out):
 
         def quantize_dz(c, grouped):
             e0, n = chunks[c]
-            half, c0 = divmod(e0, N_TILE)
-            nc.vector.quantize_mx(
-                dz_codes[half][:, c0 : c0 + n].bitcast(E5M2), dz_scales[half][:, c0 : c0 + n], grouped[:]
-            )
+            nc.vector.quantize_mx(dz_codes[:, e0 : e0 + n].bitcast(E5M2), dz_scales[:, e0 : e0 + n], grouped[:])
 
         def quantize_w(i, grouped):
-            nc.vector.quantize_mx(w_codes[i][:].bitcast(E4M3), w_scales[i][:], grouped)
+            nc.vector.quantize_mx(w_codes[i][:].bitcast(E4M3), w_scales[i][:], grouped[:])
 
-        def product(i, half):
+        def multiply(bank, i, e0):
             nc.tensor.matmul_mx(
-                banks[i][half][:],
+                bank[:],
                 lhsT=w_codes[i][:].bitcast(E4M3),
                 lhsT_scale=w_scales[i][:],
-                rhs=dz_codes[half][:].bitcast(E5M2),
-                rhs_scale=dz_scales[half][:],
+                rhs=dz_codes[:, e0 : e0 + N_TILE].bitcast(E5M2),
+                rhs_scale=dz_scales[:, e0 : e0 + N_TILE],
                 start=True,
                 stop=True,
             )
+
+        def product(i, half):
+            multiply(banks[i][half], i, half * N_TILE)
             nc.scalar.copy(dm[i][:, half * N_TILE : (half + 1) * N_TILE], banks[i][half][:])
 
+        on_vector = [(0, 0), (0, 1), (3, 2)]
         for t in range(PACK):
-            for c in range(2):
-                u = h_lo[t][:, 256 * c : 256 * (c + 1)]
-                slope(u, t == 0)
-                gather_dz(c, t, u)
-        slope(h_hi[0][:], True)
-        slope(h_hi[1][:], True)
-        for t in range(PACK):
-            gather_dz(2, t, h_hi[t // 2][:, t % 2, :])
+            square(t, t + 1, 0, 256)
+            for c in range(3):
+                if c < 2:
+                    square(t, t + 1, 256 * c + 256, 256 * c + 512)
+                (flip_v if (t, c) in on_vector else flip_s)(t, t + 1, 256 * c, 256 * c + 256)
+                gather_dz(c, t)
+
+        square(0, 2, 768, 1024)
+        square(2, 4, 768, 1024)
+        flip_v(0, 2, 768, 1024)
+        flip_v(2, 4, 768, 1024)
         g0 = interleave(nc.scalar.copy, dz32[0][:], "g0", "g0")
-        slope(h_hi[2][:], False)
-        slope(h_hi[3][:], False)
+        g1 = interleave(nc.scalar.copy, dz32[1][:], "g1", "late1")
+        gw0 = interleave(nc.scalar.copy, w_first[:], "gw0", "gw0")
+        for t in range(PACK):
+            gather_dz(3, t)
+        g2 = interleave(nc.scalar.copy, dz32[2][:], "g2", "late2")
         quantize_dz(0, g0)
         for t in range(PACK):
-            gather_dz(3, t, h_hi[2 + t // 2][:, t % 2, 0:128])
-        g1 = interleave(nc.scalar.copy, dz32[1][:], "g1", "g1")
-        g2 = interleave(nc.scalar.copy, dz32[2][:], "g2", "g2")
-        for t in range(PACK):
-            gather_dz(4, t, h_hi[2 + t // 2][:, t % 2, 128:256])
-        gw0 = interleave(nc.scalar.copy, w_first[:], "gw0", "gw0")
-        g3 = interleave(nc.scalar.copy, dz32[3][:], "g3", "late")
+            gather_dz(4, t)
+        g3 = interleave(nc.scalar.copy, dz32[3][:], "g3", "late3")
         quantize_dz(1, g1)
+        quantize_w(0, gw0)
         g4 = interleave(nc.vector.tensor_copy, dz32[4][:], "g4", "g4")
-        quantize_w(0, gw0[:])
         quantize_dz(2, g2)
         quantize_dz(3, g3)
         quantize_dz(4, g4)
         product(0, 0)
         product(0, 1)
-        gw = interleave(nc.vector.tensor_copy, w_rest[:], "gw", "late")
+        gw = [interleave(nc.vector.tensor_copy, w_rest[:, :, (i - 1) * P : i * P], f"gw{i}", f"late{i}") for i in range(1, 4)]
         for i in range(1, 4):
-            quantize_w(i, gw[:, (i - 1) * N_TILE : i * N_TILE])
+            quantize_w(i, gw[i - 1])
         for i in range(1, 4):
             product(i, 0)
             product(i, 1)
@@ -151,13 +173,14 @@ def tile_attend_gmp_tnh_kernel(tc, dyT, hE, wm, offs, offs2, out):
         for i in range(4):
             pieces = [(0, 512), (512, 512)] if i < 3 else [(0, 512), (512, 256), (768, 256)]
             total = keep.tile([P, V], F32, name=f"total{i}")
+            picked = [keep.tile([P, n], F32, name=f"picked{i}_{j}") for j, (c0, n) in enumerate(pieces)]
             for j, (c0, n) in enumerate(pieces):
-                picked = keep.tile([P, n], F32, name=f"picked{i}_{j}")
-                nc.vector.tensor_copy(picked[:], dm[i][:].indirect(src[:, c0 // STRIPE : (c0 + n) // STRIPE]))
-                x = slice(c0 // K, (c0 + n) // K)
-                adder = nc.vector if (i, j) == (3, 2) else nc.gpsimd
-                adder.tensor_tensor(total[:, x], picked[:, 0:n:2], picked[:, 1:n:2], ADD)
-                if i == 3:
-                    nc.sync.dma_start(out[i * P : (i + 1) * P, x], total[:, x])
+                nc.vector.tensor_copy(picked[j][:], dm[i][:].indirect(src[:, c0 // STRIPE : (c0 + n) // STRIPE]))
+                for k in [j - 1, j] if j == len(pieces) - 1 else [j - 1] if j > 0 else []:
+                    c0, n = pieces[k]
+                    x = slice(c0 // K, (c0 + n) // K)
+                    nc.vector.tensor_tensor(total[:, x], picked[k][:, 0:n:2], picked[k][:, 1:n:2], ADD)
+                    if i == 3:
+                        nc.sync.dma_start(out[i * P : (i + 1) * P, x], total[:, x])
             if i < 3:
                 nc.sync.dma_start(out[i * P : (i + 1) * P, :], total[:])

@@ -35,7 +35,7 @@ def tile_attend_gmp_tnh_kernel(tc, dyT, hE, wm, offs, offs2, out):
 
         dst = keep.tile([P, E // STRIPE], U16, name="dst")
         src = keep.tile([P, E // STRIPE], U16, name="src")
-        dy = [keep.tile([P, V], F32, name=f"dy{t}") for t in range(PACK)]
+        dy = [keep.tile([P, V + 32], F32, name=f"dy{t}") for t in range(PACK)]
         h_tiles = []
         w_first = keep.tile([P, PACK, P], F32, name="w_first")
         w_rest = keep.tile([P, PACK, D - P], F32, name="w_rest")
@@ -56,7 +56,8 @@ def tile_attend_gmp_tnh_kernel(tc, dyT, hE, wm, offs, offs2, out):
             raise ValueError("no such part")
 
         def load_dy(t):
-            nc.sync.dma_start(dy[t][:], dy_rows[:, t, :])
+            nc.gpsimd.memset(dy[t][:, V:], 0.0)
+            nc.sync.dma_start(dy[t][:, 0:V], dy_rows[:, t, :])
 
         load_h(0, 1, 0, 256)
         load_h(0, 1, 256, 768)
@@ -74,13 +75,23 @@ def tile_attend_gmp_tnh_kernel(tc, dyT, hE, wm, offs, offs2, out):
         nc.sync.dma_start(src[:], offs2)
         nc.sync.dma_start(w_rest[:], w_rows[:, :, P:D])
 
-        chunks = [(0, 256), (256, 256), (512, 256), (768, 128), (896, 128)]
-        dz32 = [keep.tile([P, PACK, n], F32, name=f"dz32_{c}") for c, (e0, n) in enumerate(chunks)]
+        spans = [(0, 256), (256, 768), (768, 1024)]
+        dz32 = [keep.tile([P, PACK, e1 - e0], F32, name=f"dz32_{e0}") for e0, e1 in spans]
+
+        def dz32_part(e0, e1):
+            for (b0, b1), tile in zip(spans, dz32):
+                if b0 <= e0 and e1 <= b1:
+                    return tile[:, :, e0 - b0 : e1 - b0]
+            raise ValueError("no such part")
+
+        dz16 = keep.tile([P, E * PACK], BF16, name="dz16", align_bytes=64)
         dz_codes = keep.tile([P, E], U32, name="dz_codes", align_bytes=64)
         dz_scales = keep.tile([P, E], U8, name="dz_scales", align_bytes=64)
-        w_codes = [keep.tile([P, P], U32, name=f"w_codes{i}", align_bytes=64) for i in range(4)]
-        w_scales = [keep.tile([P, P], U8, name=f"w_scales{i}", align_bytes=64) for i in range(4)]
-        dm = [keep.tile([P, E], F32, name=f"dm{i}") for i in range(4)]
+        w_codes = keep.tile([P, D], U32, name="w_codes", align_bytes=64)
+        w_scales = keep.tile([P, D], U8, name="w_scales", align_bytes=64)
+        dm = [keep.tile([P, E + 352 if i < 3 else E], F32, name=f"dm{i}") for i in range(4)]
+        for i in range(3):
+            nc.gpsimd.memset(dm[i][:, E:], 0.0)
         banks = [[psum.tile([P, N_TILE], F32, name=f"bank{i}_{j}") for j in range(2)] for i in range(4)]
 
         def square(t0, t1, e0, e1):
@@ -92,36 +103,36 @@ def tile_attend_gmp_tnh_kernel(tc, dyT, hE, wm, offs, offs2, out):
         def flip_v(t0, t1, e0, e1):
             nc.vector.tensor_scalar(h_part(t0, t1, e0, e1), h_part(t0, t1, e0, e1), -1.0, 1.0, MULT, ADD)
 
-        def gather_dz(c, t):
-            e0, n = chunks[c]
+        def gather_dz(t, e0, e1):
             nc.vector.tensor_tensor(
-                dz32[c][:, t, :],
-                dy[t][:].indirect(dst[:, e0 // STRIPE : (e0 + n) // STRIPE]),
-                h_part(t, t + 1, e0, e0 + n)[:, 0, :],
+                dz32_part(e0, e1)[:, t, :],
+                dy[t][:].indirect(dst[:, e0 // STRIPE : e1 // STRIPE]),
+                h_part(t, t + 1, e0, e1)[:, 0, :],
                 MULT,
             )
 
-        def interleave(engine_copy, rows, name, tag):
-            n = rows.shape[2]
-            grouped = keep.tile([P, n * PACK], BF16, name=name, tag=tag, align_bytes=64)
+        def interleave(engine_copy, grouped, rows):
             engine_copy(
-                grouped[:].rearrange("p (c i t) -> p c t i", i=4, t=PACK),
+                grouped.rearrange("p (c i t) -> p c t i", i=4, t=PACK),
                 rows.rearrange("p t (c i) -> p c t i", i=4),
             )
-            return grouped
 
-        def quantize_dz(c, grouped):
-            e0, n = chunks[c]
-            nc.vector.quantize_mx(dz_codes[:, e0 : e0 + n].bitcast(E5M2), dz_scales[:, e0 : e0 + n], grouped[:])
+        def round_dz(engine_copy, e0, e1):
+            interleave(engine_copy, dz16[:, e0 * PACK : e1 * PACK], dz32_part(e0, e1))
 
-        def quantize_w(i, grouped):
-            nc.vector.quantize_mx(w_codes[i][:].bitcast(E4M3), w_scales[i][:], grouped[:])
+        def quantize_dz(e0, e1):
+            nc.vector.quantize_mx(
+                dz_codes[:, e0:e1].bitcast(E5M2), dz_scales[:, e0:e1], dz16[:, e0 * PACK : e1 * PACK]
+            )
+
+        def quantize_w(d0, d1, grouped):
+            nc.vector.quantize_mx(w_codes[:, d0:d1].bitcast(E4M3), w_scales[:, d0:d1], grouped)
 
         def multiply(bank, i, e0):
             nc.tensor.matmul_mx(
                 bank[:],
-                lhsT=w_codes[i][:].bitcast(E4M3),
-                lhsT_scale=w_scales[i][:],
+                lhsT=w_codes[:, i * P : (i + 1) * P].bitcast(E4M3),
+                lhsT_scale=w_scales[:, i * P : (i + 1) * P],
                 rhs=dz_codes[:, e0 : e0 + N_TILE].bitcast(E5M2),
                 rhs_scale=dz_scales[:, e0 : e0 + N_TILE],
                 start=True,
@@ -132,55 +143,64 @@ def tile_attend_gmp_tnh_kernel(tc, dyT, hE, wm, offs, offs2, out):
             multiply(banks[i][half], i, half * N_TILE)
             nc.scalar.copy(dm[i][:, half * N_TILE : (half + 1) * N_TILE], banks[i][half][:])
 
-        on_vector = [(0, 0), (0, 1), (3, 2)]
-        for t in range(PACK):
-            square(t, t + 1, 0, 256)
-            for c in range(3):
-                if c < 2:
-                    square(t, t + 1, 256 * c + 256, 256 * c + 512)
-                (flip_v if (t, c) in on_vector else flip_s)(t, t + 1, 256 * c, 256 * c + 256)
-                gather_dz(c, t)
-
+        square(0, 1, 0, 256)
+        flip_v(0, 1, 0, 256)
+        square(0, 1, 256, 768)
+        gather_dz(0, 0, 256)
+        flip_v(0, 1, 256, 768)
+        gather_dz(0, 256, 768)
+        square(1, 2, 0, 256)
+        square(1, 2, 256, 768)
+        flip_s(1, 2, 0, 256)
+        flip_s(1, 2, 256, 768)
+        gather_dz(1, 0, 256)
+        gather_dz(1, 256, 768)
+        square(2, 3, 0, 256)
+        square(2, 3, 256, 768)
+        flip_s(2, 3, 0, 256)
+        flip_s(2, 3, 256, 768)
+        gather_dz(2, 0, 256)
+        gather_dz(2, 256, 768)
+        square(3, 4, 0, 256)
+        square(3, 4, 256, 768)
+        flip_s(3, 4, 0, 256)
+        flip_s(3, 4, 256, 768)
+        gather_dz(3, 0, 256)
+        gather_dz(3, 256, 768)
+        w16 = keep.tile([P, P * PACK], BF16, name="w16", align_bytes=64)
         square(0, 2, 768, 1024)
         square(2, 4, 768, 1024)
         flip_v(0, 2, 768, 1024)
         flip_v(2, 4, 768, 1024)
-        g0 = interleave(nc.scalar.copy, dz32[0][:], "g0", "g0")
-        g1 = interleave(nc.scalar.copy, dz32[1][:], "g1", "late1")
-        gw0 = interleave(nc.scalar.copy, w_first[:], "gw0", "gw0")
         for t in range(PACK):
-            gather_dz(3, t)
-        g2 = interleave(nc.scalar.copy, dz32[2][:], "g2", "late2")
-        quantize_dz(0, g0)
-        for t in range(PACK):
-            gather_dz(4, t)
-        g3 = interleave(nc.scalar.copy, dz32[3][:], "g3", "late3")
-        quantize_dz(1, g1)
-        quantize_w(0, gw0)
-        g4 = interleave(nc.vector.tensor_copy, dz32[4][:], "g4", "g4")
-        quantize_dz(2, g2)
-        quantize_dz(3, g3)
-        quantize_dz(4, g4)
+            gather_dz(t, 768, 1024)
+        round_dz(nc.scalar.copy, 0, 256)
+        round_dz(nc.scalar.copy, 256, 512)
+        interleave(nc.scalar.copy, w16[:], w_first[:])
+        round_dz(nc.scalar.copy, 512, 768)
+        round_dz(nc.scalar.copy, 768, 896)
+        quantize_dz(0, 512)
+        round_dz(nc.vector.tensor_copy, 896, 1024)
+        quantize_w(0, P, w16[:])
         product(0, 0)
+        quantize_dz(512, 768)
+        quantize_dz(768, 1024)
         product(0, 1)
-        gw = [interleave(nc.vector.tensor_copy, w_rest[:, :, (i - 1) * P : i * P], f"gw{i}", f"late{i}") for i in range(1, 4)]
-        for i in range(1, 4):
-            quantize_w(i, gw[i - 1])
+        w16r = keep.tile([P, (D - P) * PACK], BF16, name="w16r", tag="dz16", align_bytes=64)
+        interleave(nc.vector.tensor_copy, w16r[:], w_rest[:])
+        quantize_w(P, 2 * P, w16r[:, 0:512])
+        quantize_w(2 * P, D, w16r[:, 512:1536])
         for i in range(1, 4):
             product(i, 0)
             product(i, 1)
 
         for i in range(4):
-            pieces = [(0, 512), (512, 512)] if i < 3 else [(0, 512), (512, 256), (768, 256)]
+            pieces = [(0, E)] if i < 3 else [(0, 576), (576, 448)]
             total = keep.tile([P, V], F32, name=f"total{i}")
-            picked = [keep.tile([P, n], F32, name=f"picked{i}_{j}") for j, (c0, n) in enumerate(pieces)]
-            for j, (c0, n) in enumerate(pieces):
-                nc.vector.tensor_copy(picked[j][:], dm[i][:].indirect(src[:, c0 // STRIPE : (c0 + n) // STRIPE]))
-                for k in [j - 1, j] if j == len(pieces) - 1 else [j - 1] if j > 0 else []:
-                    c0, n = pieces[k]
-                    x = slice(c0 // K, (c0 + n) // K)
-                    nc.vector.tensor_tensor(total[:, x], picked[k][:, 0:n:2], picked[k][:, 1:n:2], ADD)
-                    if i == 3:
-                        nc.sync.dma_start(out[i * P : (i + 1) * P, x], total[:, x])
-            if i < 3:
-                nc.sync.dma_start(out[i * P : (i + 1) * P, :], total[:])
+            for c0, n in pieces:
+                picked = keep.tile([P, n], F32, name=f"picked{i}_{c0}")
+                nc.vector.tensor_copy(picked[:], dm[i][:].indirect(src[:, c0 // STRIPE : (c0 + n) // STRIPE]))
+                x = slice(c0 // K, (c0 + n) // K)
+                adder = nc.vector if i == 3 and c0 + n == E else nc.gpsimd
+                adder.tensor_tensor(total[:, x], picked[:, 0:n:2], picked[:, 1:n:2], ADD)
+                nc.sync.dma_start(out[i * P : (i + 1) * P, x], total[:, x])

@@ -29,61 +29,37 @@ def tile_attend_gmp_tnh_kernel(tc, dyT, hE, wm, offs, offs2, out):
     h_rows = hE.rearrange("(p t) e -> p t e", t=PACK)
     w_rows = wm.rearrange("(p t) d -> p t d", t=PACK)
 
+    CH = 256
+    loads = [(0, 0, 2), (1, 0, 2), (0, 2, 4), (1, 2, 4), (2, 0, 4), (3, 0, 4)]
+
     with ExitStack() as ctx:
         keep = ctx.enter_context(tc.tile_pool(name="keep", bufs=1))
         psum = ctx.enter_context(tc.psum_pool(name="psum", bufs=1))
 
         dst = keep.tile([P, E // STRIPE], U16, name="dst")
         src = keep.tile([P, E // STRIPE], U16, name="src")
-        dy = [keep.tile([P, V + 32], F32, name=f"dy{t}") for t in range(PACK)]
-        h_tiles = []
+        dy = keep.tile([P, PACK * V], F32, name="dy")
+        h = {(c, t0): keep.tile([P, t1 - t0, CH], F32, name=f"h{c}_{t0}") for c, t0, t1 in loads}
         w_first = keep.tile([P, PACK, P], F32, name="w_first")
         w_rest = keep.tile([P, PACK, D - P], F32, name="w_rest")
 
-        warm = keep.tile([P, 8], F32, name="warm")
-        nc.vector.memset(warm[:], 0.0)
-        nc.scalar.activation(warm[:], warm[:], SQUARE)
-
-        def load_h(t0, t1, e0, e1):
-            tile = keep.tile([P, t1 - t0, e1 - e0], F32, name=f"h{t0}_{e0}")
-            h_tiles.append((t0, t1, e0, e1, tile))
-            nc.sync.dma_start(tile[:], h_rows[:, t0:t1, e0:e1])
-
-        def h_part(t0, t1, e0, e1):
-            for a0, a1, b0, b1, tile in h_tiles:
-                if a0 <= t0 and t1 <= a1 and b0 <= e0 and e1 <= b1:
-                    return tile[:, t0 - a0 : t1 - a0, e0 - b0 : e1 - b0]
-            raise ValueError("no such part")
+        def load_h(c, t0, t1):
+            nc.sync.dma_start(h[c, t0][:], h_rows[:, t0:t1, c * CH : (c + 1) * CH])
 
         def load_dy(t):
-            nc.gpsimd.memset(dy[t][:, V:], 0.0)
-            nc.sync.dma_start(dy[t][:, 0:V], dy_rows[:, t, :])
+            nc.sync.dma_start(dy[:, t * V : (t + 1) * V], dy_rows[:, t, :])
 
-        load_h(0, 1, 0, 256)
-        load_h(0, 1, 256, 768)
-        load_dy(0)
         nc.sync.dma_start(dst[:], offs)
-        load_h(1, 2, 0, 256)
-        load_h(1, 2, 256, 768)
-        load_dy(1)
-        for t in range(2, PACK):
-            load_h(t, t + 1, 0, 768)
+        for t in range(PACK):
             load_dy(t)
-        load_h(0, 2, 768, 1024)
-        load_h(2, 4, 768, 1024)
+            load_h(*loads[t])
+        load_h(*loads[4])
+        load_h(*loads[5])
         nc.sync.dma_start(w_first[:], w_rows[:, :, 0:P])
         nc.sync.dma_start(src[:], offs2)
         nc.sync.dma_start(w_rest[:], w_rows[:, :, P:D])
 
-        spans = [(0, 256), (256, 768), (768, 1024)]
-        dz32 = [keep.tile([P, PACK, e1 - e0], F32, name=f"dz32_{e0}") for e0, e1 in spans]
-
-        def dz32_part(e0, e1):
-            for (b0, b1), tile in zip(spans, dz32):
-                if b0 <= e0 and e1 <= b1:
-                    return tile[:, :, e0 - b0 : e1 - b0]
-            raise ValueError("no such part")
-
+        g = [keep.tile([P, PACK, CH], F32, name=f"g{c}") for c in range(4)]
         dz16 = keep.tile([P, E * PACK], BF16, name="dz16", align_bytes=64)
         dz_codes = keep.tile([P, E], U32, name="dz_codes", align_bytes=64)
         dz_scales = keep.tile([P, E], U8, name="dz_scales", align_bytes=64)
@@ -92,33 +68,35 @@ def tile_attend_gmp_tnh_kernel(tc, dyT, hE, wm, offs, offs2, out):
         dm = [keep.tile([P, E + 352 if i < 3 else E], F32, name=f"dm{i}") for i in range(4)]
         for i in range(3):
             nc.gpsimd.memset(dm[i][:, E:], 0.0)
-        banks = [[psum.tile([P, N_TILE], F32, name=f"bank{i}_{j}") for j in range(2)] for i in range(4)]
 
-        def square(t0, t1, e0, e1):
-            nc.scalar.activation(h_part(t0, t1, e0, e1), h_part(t0, t1, e0, e1), SQUARE)
+        def gather_dy(c, t, window_end):
+            nc.vector.tensor_copy(
+                g[c][:, t, :], dy[:, t * V : window_end].indirect(dst[:, c * 16 : (c + 1) * 16])
+            )
 
-        def flip_s(t0, t1, e0, e1):
-            nc.scalar.activation(h_part(t0, t1, e0, e1), h_part(t0, t1, e0, e1), COPY, bias=1.0, scale=-1.0)
+        def by_fours(rows):
+            return rows.rearrange("p t (c i) -> p c t i", i=4)
 
-        def flip_v(t0, t1, e0, e1):
-            nc.vector.tensor_scalar(h_part(t0, t1, e0, e1), h_part(t0, t1, e0, e1), -1.0, 1.0, MULT, ADD)
+        def grouped_by_fours(grouped):
+            return grouped.rearrange("p (c i t) -> p c t i", i=4, t=PACK)
 
-        def gather_dz(t, e0, e1):
-            nc.vector.tensor_tensor(
-                dz32_part(e0, e1)[:, t, :],
-                dy[t][:].indirect(dst[:, e0 // STRIPE : e1 // STRIPE]),
-                h_part(t, t + 1, e0, e1)[:, 0, :],
+        def h_part(t0, t1, e0, e1):
+            c = e0 // CH
+            return h[c, t0][:, 0 : t1 - t0, e0 - c * CH : e1 - c * CH]
+
+        def factor(t0, t1, e0, e1):
+            part = h_part(t0, t1, e0, e1)
+            nc.scalar.activation(part, part, SQUARE)
+            nc.scalar.activation(part, part, COPY, bias=1.0, scale=-1.0)
+
+        def form_dz(engine, t0, t1, e0, e1):
+            c = e0 // CH
+            engine.tensor_tensor(
+                grouped_by_fours(dz16[:, e0 * PACK : e1 * PACK])[:, :, t0:t1, :],
+                by_fours(g[c][:, t0:t1, e0 - c * CH : e1 - c * CH]),
+                by_fours(h_part(t0, t1, e0, e1)),
                 MULT,
             )
-
-        def interleave(engine_copy, grouped, rows):
-            engine_copy(
-                grouped.rearrange("p (c i t) -> p c t i", i=4, t=PACK),
-                rows.rearrange("p t (c i) -> p c t i", i=4),
-            )
-
-        def round_dz(engine_copy, e0, e1):
-            interleave(engine_copy, dz16[:, e0 * PACK : e1 * PACK], dz32_part(e0, e1))
 
         def quantize_dz(e0, e1):
             nc.vector.quantize_mx(
@@ -128,7 +106,8 @@ def tile_attend_gmp_tnh_kernel(tc, dyT, hE, wm, offs, offs2, out):
         def quantize_w(d0, d1, grouped):
             nc.vector.quantize_mx(w_codes[:, d0:d1].bitcast(E4M3), w_scales[:, d0:d1], grouped)
 
-        def multiply(bank, i, e0):
+        def product(i, e0, keep_from, bank_tag):
+            bank = psum.tile([P, N_TILE], F32, name=f"bank{i}_{e0}", tag=f"bank{bank_tag}")
             nc.tensor.matmul_mx(
                 bank[:],
                 lhsT=w_codes[:, i * P : (i + 1) * P].bitcast(E4M3),
@@ -138,67 +117,48 @@ def tile_attend_gmp_tnh_kernel(tc, dyT, hE, wm, offs, offs2, out):
                 start=True,
                 stop=True,
             )
+            nc.scalar.copy(dm[i][:, keep_from : e0 + N_TILE], bank[:, keep_from - e0 :])
 
-        def product(i, half):
-            multiply(banks[i][half], i, half * N_TILE)
-            nc.scalar.copy(dm[i][:, half * N_TILE : (half + 1) * N_TILE], banks[i][half][:])
-
-        square(0, 1, 0, 256)
-        flip_v(0, 1, 0, 256)
-        square(0, 1, 256, 768)
-        gather_dz(0, 0, 256)
-        flip_v(0, 1, 256, 768)
-        gather_dz(0, 256, 768)
-        square(1, 2, 0, 256)
-        square(1, 2, 256, 768)
-        flip_s(1, 2, 0, 256)
-        flip_s(1, 2, 256, 768)
-        gather_dz(1, 0, 256)
-        gather_dz(1, 256, 768)
-        square(2, 3, 0, 256)
-        square(2, 3, 256, 768)
-        flip_s(2, 3, 0, 256)
-        flip_s(2, 3, 256, 768)
-        gather_dz(2, 0, 256)
-        gather_dz(2, 256, 768)
-        square(3, 4, 0, 256)
-        square(3, 4, 256, 768)
-        flip_s(3, 4, 0, 256)
-        flip_s(3, 4, 256, 768)
-        gather_dz(3, 0, 256)
-        gather_dz(3, 256, 768)
-        w16 = keep.tile([P, P * PACK], BF16, name="w16", align_bytes=64)
-        square(0, 2, 768, 1024)
-        square(2, 4, 768, 1024)
-        flip_v(0, 2, 768, 1024)
-        flip_v(2, 4, 768, 1024)
         for t in range(PACK):
-            gather_dz(t, 768, 1024)
-        round_dz(nc.scalar.copy, 0, 256)
-        round_dz(nc.scalar.copy, 256, 512)
-        interleave(nc.scalar.copy, w16[:], w_first[:])
-        round_dz(nc.scalar.copy, 512, 768)
-        round_dz(nc.scalar.copy, 768, 896)
+            for c in range(2):
+                gather_dy(c, t, (t + 1) * V)
+        for c in range(2, 4):
+            for t in range(PACK):
+                gather_dy(c, t, PACK * V)
+        on_gpsimd = [(0, 2, 0, 256), (0, 2, 256, 512), (2, 4, 0, 256), (2, 4, 256, 512), (0, 4, 512, 640)]
+        for piece in on_gpsimd:
+            factor(*piece)
+            form_dz(nc.gpsimd, *piece)
+        factor(0, 4, 640, 768)
+        w16 = keep.tile([P, P * PACK], BF16, name="w16", align_bytes=64)
+        nc.scalar.copy(grouped_by_fours(w16[:]), by_fours(w_first[:]))
+        factor(0, 4, 768, 896)
+        factor(0, 4, 896, 1024)
         quantize_dz(0, 512)
-        round_dz(nc.vector.tensor_copy, 896, 1024)
+        form_dz(nc.vector, 0, 4, 640, 768)
         quantize_w(0, P, w16[:])
-        product(0, 0)
+        product(0, 0, 0, 0)
         quantize_dz(512, 768)
-        quantize_dz(768, 1024)
-        product(0, 1)
+        product(0, 256, 512, 1)
+        form_dz(nc.vector, 0, 4, 768, 896)
+        form_dz(nc.vector, 0, 4, 896, 1024)
+        quantize_dz(768, 896)
+        quantize_dz(896, 1024)
+        product(0, 512, 768, 2)
         w16r = keep.tile([P, (D - P) * PACK], BF16, name="w16r", tag="dz16", align_bytes=64)
-        interleave(nc.vector.tensor_copy, w16r[:], w_rest[:])
+        nc.vector.tensor_copy(grouped_by_fours(w16r[:]), by_fours(w_rest[:]))
         quantize_w(P, 2 * P, w16r[:, 0:512])
         quantize_w(2 * P, D, w16r[:, 512:1536])
         for i in range(1, 4):
-            product(i, 0)
-            product(i, 1)
+            for half in range(2):
+                product(i, half * N_TILE, half * N_TILE, (1 + 2 * i + half) % 8)
 
         for i in range(4):
-            pieces = [(0, E)] if i < 3 else [(0, 576), (576, 448)]
+            cuts = [(0, E)] if i < 3 else [(0, 576), (576, 448)]
             total = keep.tile([P, V], F32, name=f"total{i}")
-            for c0, n in pieces:
-                picked = keep.tile([P, n], F32, name=f"picked{i}_{c0}")
+            for c0, n in cuts:
+                tag = "dz16" if i == 0 else f"picked{i}_{c0}"
+                picked = keep.tile([P, n], F32, name=f"picked{i}_{c0}", tag=tag, align_bytes=64)
                 nc.vector.tensor_copy(picked[:], dm[i][:].indirect(src[:, c0 // STRIPE : (c0 + n) // STRIPE]))
                 x = slice(c0 // K, (c0 + n) // K)
                 adder = nc.vector if i == 3 and c0 + n == E else nc.gpsimd

@@ -38,7 +38,10 @@ def tile_attend_gmp_tnh_kernel(tc, dyT, hE, wm, offs, offs2, out):
 
         dst = keep.tile([P, E // STRIPE], U16, name="dst")
         src = keep.tile([P, E // STRIPE], U16, name="src")
-        dy = keep.tile([P, PACK * V], F32, name="dy")
+        PAD = 176
+        dy_at = [0, V + PAD, 2 * V + PAD, 3 * V + 2 * PAD]
+        dy_end = 4 * V + 2 * PAD
+        dy = keep.tile([P, dy_end], F32, name="dy")
         h = {(c, t0): keep.tile([P, t1 - t0, CH], F32, name=f"h{c}_{t0}") for c, t0, t1 in loads}
         w_first = keep.tile([P, PACK, P], F32, name="w_first")
         w_rest = keep.tile([P, PACK, D - P], F32, name="w_rest")
@@ -47,7 +50,7 @@ def tile_attend_gmp_tnh_kernel(tc, dyT, hE, wm, offs, offs2, out):
             nc.sync.dma_start(h[c, t0][:], h_rows[:, t0:t1, c * CH : (c + 1) * CH])
 
         def load_dy(t):
-            nc.sync.dma_start(dy[:, t * V : (t + 1) * V], dy_rows[:, t, :])
+            nc.sync.dma_start(dy[:, dy_at[t] : dy_at[t] + V], dy_rows[:, t, :])
 
         nc.sync.dma_start(dst[:], offs)
         for t in range(PACK):
@@ -59,19 +62,30 @@ def tile_attend_gmp_tnh_kernel(tc, dyT, hE, wm, offs, offs2, out):
         nc.sync.dma_start(src[:], offs2)
         nc.sync.dma_start(w_rest[:], w_rows[:, :, P:D])
 
-        g = [keep.tile([P, PACK, CH], F32, name=f"g{c}") for c in range(4)]
+        g_spans = [(0, 512), (512, 768), (768, 1024)]
+        g = [keep.tile([P, PACK, e1 - e0], F32, name=f"g{e0}") for e0, e1 in g_spans]
+
+        def g_part(t0, t1, e0, e1):
+            for (b0, b1), tile in zip(g_spans, g):
+                if b0 <= e0 and e1 <= b1:
+                    return tile[:, t0:t1, e0 - b0 : e1 - b0]
+            raise ValueError("no such part")
+
         dz16 = keep.tile([P, E * PACK], BF16, name="dz16", align_bytes=64)
         dz_codes = keep.tile([P, E], U32, name="dz_codes", align_bytes=64)
         dz_scales = keep.tile([P, E], U8, name="dz_scales", align_bytes=64)
         w_codes = keep.tile([P, D], U32, name="w_codes", align_bytes=64)
         w_scales = keep.tile([P, D], U8, name="w_scales", align_bytes=64)
         dm = [keep.tile([P, E + 352 if i < 3 else E], F32, name=f"dm{i}") for i in range(4)]
+        for t in (0, 2):
+            nc.vector.memset(dy[:, dy_at[t] + V : dy_at[t + 1]], 0.0)
         for i in range(3):
             nc.gpsimd.memset(dm[i][:, E:], 0.0)
 
-        def gather_dy(c, t, window_end):
+        def gather_dy(t, e0, e1, window_end):
             nc.vector.tensor_copy(
-                g[c][:, t, :], dy[:, t * V : window_end].indirect(dst[:, c * 16 : (c + 1) * 16])
+                g_part(t, t + 1, e0, e1)[:, 0, :],
+                dy[:, dy_at[t] : window_end].indirect(dst[:, e0 // STRIPE : e1 // STRIPE]),
             )
 
         def by_fours(rows):
@@ -90,10 +104,9 @@ def tile_attend_gmp_tnh_kernel(tc, dyT, hE, wm, offs, offs2, out):
             nc.scalar.activation(part, part, COPY, bias=1.0, scale=-1.0)
 
         def form_dz(engine, t0, t1, e0, e1):
-            c = e0 // CH
             engine.tensor_tensor(
                 grouped_by_fours(dz16[:, e0 * PACK : e1 * PACK])[:, :, t0:t1, :],
-                by_fours(g[c][:, t0:t1, e0 - c * CH : e1 - c * CH]),
+                by_fours(g_part(t0, t1, e0, e1)),
                 by_fours(h_part(t0, t1, e0, e1)),
                 MULT,
             )
@@ -119,12 +132,17 @@ def tile_attend_gmp_tnh_kernel(tc, dyT, hE, wm, offs, offs2, out):
             )
             nc.scalar.copy(dm[i][:, keep_from : e0 + N_TILE], bank[:, keep_from - e0 :])
 
+        gather_dy(0, 0, 512, dy_at[1])
+        gather_dy(1, 0, 256, dy_at[2])
+        gather_dy(1, 256, 512, dy_at[2])
+        gather_dy(0, 512, 768, dy_at[2])
+        gather_dy(2, 0, 512, dy_at[3])
+        gather_dy(3, 0, 256, dy_end)
+        gather_dy(3, 256, 512, dy_end)
+        for t in range(1, PACK):
+            gather_dy(t, 512, 768, dy_end)
         for t in range(PACK):
-            for c in range(2):
-                gather_dy(c, t, (t + 1) * V)
-        for c in range(2, 4):
-            for t in range(PACK):
-                gather_dy(c, t, PACK * V)
+            gather_dy(t, 768, 1024, min(dy_end, dy_at[t] + 2048))
         on_gpsimd = [(0, 2, 0, 256), (0, 2, 256, 512), (2, 4, 0, 256), (2, 4, 256, 512), (0, 4, 512, 640)]
         for piece in on_gpsimd:
             factor(*piece)
@@ -154,13 +172,13 @@ def tile_attend_gmp_tnh_kernel(tc, dyT, hE, wm, offs, offs2, out):
                 product(i, half * N_TILE, half * N_TILE, (1 + 2 * i + half) % 8)
 
         for i in range(4):
-            cuts = [(0, E)] if i < 3 else [(0, 576), (576, 448)]
+            cuts = [(0, E)] if i < 3 else [(0, 448), (448, 384), (832, 192)]
             total = keep.tile([P, V], F32, name=f"total{i}")
             for c0, n in cuts:
                 tag = "dz16" if i == 0 else f"picked{i}_{c0}"
                 picked = keep.tile([P, n], F32, name=f"picked{i}_{c0}", tag=tag, align_bytes=64)
                 nc.vector.tensor_copy(picked[:], dm[i][:].indirect(src[:, c0 // STRIPE : (c0 + n) // STRIPE]))
                 x = slice(c0 // K, (c0 + n) // K)
-                adder = nc.vector if i == 3 and c0 + n == E else nc.gpsimd
+                adder = nc.vector if i == 3 and c0 > 0 else nc.gpsimd
                 adder.tensor_tensor(total[:, x], picked[:, 0:n:2], picked[:, 1:n:2], ADD)
                 nc.sync.dma_start(out[i * P : (i + 1) * P, x], total[:, x])

@@ -30,7 +30,7 @@ def tile_attend_gmp_tnh_kernel(tc, dyT, hE, wm, offs, offs2, out):
     w_rows = wm.rearrange("(p t) d -> p t d", t=PACK)
 
     CH = 256
-    loads = [(0, 0, 2), (1, 0, 2), (0, 2, 4), (1, 2, 4), (2, 0, 4), (3, 0, 4)]
+    loads = [(0, 0, 2), (1, 0, 2), (0, 2, 4), (1, 2, 4), (3, 0, 4), (2, 0, 4)]
 
     with ExitStack() as ctx:
         keep = ctx.enter_context(tc.tile_pool(name="keep", bufs=1))
@@ -111,6 +111,14 @@ def tile_attend_gmp_tnh_kernel(tc, dyT, hE, wm, offs, offs2, out):
                 MULT,
             )
 
+        def form_dz_by_edges(t0, t1, e0, e1):
+            nc.gpsimd.tensor_tensor(
+                dz16[:, e0 * PACK : e1 * PACK].rearrange("p (e t) -> p e t", t=PACK)[:, :, t0:t1],
+                g_part(t0, t1, e0, e1).rearrange("p t e -> p e t"),
+                h_part(t0, t1, e0, e1).rearrange("p t e -> p e t"),
+                MULT,
+            )
+
         def quantize_dz(e0, e1):
             nc.vector.quantize_mx(
                 dz_codes[:, e0:e1].bitcast(E5M2), dz_scales[:, e0:e1], dz16[:, e0 * PACK : e1 * PACK]
@@ -135,33 +143,32 @@ def tile_attend_gmp_tnh_kernel(tc, dyT, hE, wm, offs, offs2, out):
         gather_dy(0, 0, 512, dy_at[1])
         gather_dy(1, 0, 256, dy_at[2])
         gather_dy(1, 256, 512, dy_at[2])
-        gather_dy(0, 512, 768, dy_at[2])
+        gather_dy(0, 768, 1024, dy_at[2])
         gather_dy(2, 0, 512, dy_at[3])
         gather_dy(3, 0, 256, dy_end)
         gather_dy(3, 256, 512, dy_end)
         for t in range(1, PACK):
-            gather_dy(t, 512, 768, dy_end)
+            gather_dy(t, 768, 1024, dy_end)
         for t in range(PACK):
-            gather_dy(t, 768, 1024, min(dy_end, dy_at[t] + 2048))
-        on_gpsimd = [(0, 2, 0, 256), (0, 2, 256, 512), (2, 4, 0, 256), (2, 4, 256, 512), (0, 4, 512, 640)]
+            gather_dy(t, 512, 768, min(dy_end, dy_at[t] + 2048))
+        on_gpsimd = [(0, 2, 0, 256), (0, 2, 256, 512), (2, 4, 0, 256), (2, 4, 256, 512), (0, 4, 832, 1024)]
         for piece in on_gpsimd:
             factor(*piece)
-            form_dz(nc.gpsimd, *piece)
-        factor(0, 4, 640, 768)
+            form_dz_by_edges(*piece)
+        factor(0, 4, 512, 640)
         w16 = keep.tile([P, P * PACK], BF16, name="w16", align_bytes=64)
         nc.scalar.copy(grouped_by_fours(w16[:]), by_fours(w_first[:]))
-        factor(0, 4, 768, 896)
-        factor(0, 4, 896, 1024)
+        factor(0, 4, 640, 768)
+        factor(0, 4, 768, 832)
         quantize_dz(0, 512)
-        form_dz(nc.vector, 0, 4, 640, 768)
+        form_dz(nc.vector, 0, 4, 512, 640)
         quantize_w(0, P, w16[:])
         product(0, 0, 0, 0)
+        form_dz(nc.vector, 0, 4, 640, 768)
         quantize_dz(512, 768)
         product(0, 256, 512, 1)
-        form_dz(nc.vector, 0, 4, 768, 896)
-        form_dz(nc.vector, 0, 4, 896, 1024)
-        quantize_dz(768, 896)
-        quantize_dz(896, 1024)
+        form_dz(nc.vector, 0, 4, 768, 832)
+        quantize_dz(768, 1024)
         product(0, 512, 768, 2)
         w16r = keep.tile([P, (D - P) * PACK], BF16, name="w16r", tag="dz16", align_bytes=64)
         nc.vector.tensor_copy(grouped_by_fours(w16r[:]), by_fours(w_rest[:]))

@@ -18,19 +18,31 @@ COPY = mybir.ActivationFunctionType.Copy
 SQUARE = mybir.ActivationFunctionType.Square
 
 P = 128
-PACK = 4
-N_TILE = 512
+PLANES = 4
+N_PASS = 512
+BANKS = 8
 STRIPE = 16
+RUN = 4
+CHUNK = 256
+HALF = CHUNK // 2
+DM_TILES = D // P
+
+DY_PAD = 176
+DM_PAD = 352
+WINDOW_MAX = 8 * CHUNK
+
+LAST_CUTS = [(0, 448), (448, 384), (832, 192)]
 
 
 def tile_attend_gmp_tnh_kernel(tc, dyT, hE, wm, offs, offs2, out):
     nc = tc.nc
-    dy_rows = dyT.rearrange("(p t) v -> p t v", t=PACK)
-    h_rows = hE.rearrange("(p t) e -> p t e", t=PACK)
-    w_rows = wm.rearrange("(p t) d -> p t d", t=PACK)
+    dy_rows = dyT.rearrange("(p t) v -> p t v", t=PLANES)
+    h_rows = hE.rearrange("(p t) e -> p t e", t=PLANES)
+    w_rows = wm.rearrange("(p t) d -> p t d", t=PLANES)
 
-    CH = 256
-    loads = [(0, 0, 2), (1, 0, 2), (0, 2, 4), (1, 2, 4), (3, 0, 4), (2, 0, 4)]
+    edge = [c * CHUNK for c in range(E // CHUNK + 1)]
+    pair_loads = [(c, t0, t0 + 2) for t0 in (0, 2) for c in (0, 1)]
+    whole_loads = [(3, 0, PLANES), (2, 0, PLANES)]
 
     with ExitStack() as ctx:
         keep = ctx.enter_context(tc.tile_pool(name="keep", bufs=1))
@@ -38,154 +50,152 @@ def tile_attend_gmp_tnh_kernel(tc, dyT, hE, wm, offs, offs2, out):
 
         dst = keep.tile([P, E // STRIPE], U16, name="dst")
         src = keep.tile([P, E // STRIPE], U16, name="src")
-        PAD = 176
-        dy_at = [0, V + PAD, 2 * V + PAD, 3 * V + 2 * PAD]
-        dy_end = 4 * V + 2 * PAD
+        dy_at = [0, V + DY_PAD, 2 * V + DY_PAD, 3 * V + 2 * DY_PAD]
+        dy_end = PLANES * V + 2 * DY_PAD
         dy = keep.tile([P, dy_end], F32, name="dy")
-        h = {(c, t0): keep.tile([P, t1 - t0, CH], F32, name=f"h{c}_{t0}") for c, t0, t1 in loads}
-        w_first = keep.tile([P, PACK, P], F32, name="w_first")
-        w_rest = keep.tile([P, PACK, D - P], F32, name="w_rest")
+        h = {
+            (c, t0): keep.tile([P, t1 - t0, CHUNK], F32, name=f"h{c}_{t0}")
+            for c, t0, t1 in pair_loads + whole_loads
+        }
+        w_first = keep.tile([P, PLANES, P], F32, name="w_first")
+        w_rest = keep.tile([P, PLANES, D - P], F32, name="w_rest")
 
         def load_h(c, t0, t1):
-            nc.sync.dma_start(h[c, t0][:], h_rows[:, t0:t1, c * CH : (c + 1) * CH])
-
-        def load_dy(t):
-            nc.sync.dma_start(dy[:, dy_at[t] : dy_at[t] + V], dy_rows[:, t, :])
+            nc.sync.dma_start(h[c, t0][:], h_rows[:, t0:t1, edge[c] : edge[c + 1]])
 
         nc.sync.dma_start(dst[:], offs)
-        for t in range(PACK):
-            load_dy(t)
-            load_h(*loads[t])
-        load_h(*loads[4])
-        load_h(*loads[5])
+        for t in range(PLANES):
+            nc.sync.dma_start(dy[:, dy_at[t] : dy_at[t] + V], dy_rows[:, t, :])
+            load_h(*pair_loads[t])
+        for load in whole_loads:
+            load_h(*load)
         nc.sync.dma_start(w_first[:], w_rows[:, :, 0:P])
         nc.sync.dma_start(src[:], offs2)
         nc.sync.dma_start(w_rest[:], w_rows[:, :, P:D])
 
-        g_spans = [(0, 512), (512, 768), (768, 1024)]
-        g = [keep.tile([P, PACK, e1 - e0], F32, name=f"g{e0}") for e0, e1 in g_spans]
+        gathered_spans = [(edge[0], edge[2]), (edge[2], edge[3]), (edge[3], edge[4])]
+        gathered = [keep.tile([P, PLANES, e1 - e0], F32, name=f"g{e0}") for e0, e1 in gathered_spans]
 
-        def g_part(t0, t1, e0, e1):
-            for (b0, b1), tile in zip(g_spans, g):
-                if b0 <= e0 and e1 <= b1:
-                    return tile[:, t0:t1, e0 - b0 : e1 - b0]
-            raise ValueError("no such part")
+        def gathered_part(t0, t1, e0, e1):
+            i = max(e0 // CHUNK - 1, 0)
+            first = gathered_spans[i][0]
+            return gathered[i][:, t0:t1, e0 - first : e1 - first]
 
-        dz16 = keep.tile([P, E * PACK], BF16, name="dz16", align_bytes=64)
+        dz16 = keep.tile([P, E * PLANES], BF16, name="dz16", align_bytes=64)
         dz_codes = keep.tile([P, E], U32, name="dz_codes", align_bytes=64)
         dz_scales = keep.tile([P, E], U8, name="dz_scales", align_bytes=64)
         w_codes = keep.tile([P, D], U32, name="w_codes", align_bytes=64)
         w_scales = keep.tile([P, D], U8, name="w_scales", align_bytes=64)
-        dm = [keep.tile([P, E + 352 if i < 3 else E], F32, name=f"dm{i}") for i in range(4)]
+        dm = [
+            keep.tile([P, E + DM_PAD if i < DM_TILES - 1 else E], F32, name=f"dm{i}")
+            for i in range(DM_TILES)
+        ]
         for t in (0, 2):
             nc.vector.memset(dy[:, dy_at[t] + V : dy_at[t + 1]], 0.0)
-        for i in range(3):
+        for i in range(DM_TILES - 1):
             nc.gpsimd.memset(dm[i][:, E:], 0.0)
 
         def gather_dy(t, e0, e1, window_end):
             nc.vector.tensor_copy(
-                g_part(t, t + 1, e0, e1)[:, 0, :],
+                gathered_part(t, t + 1, e0, e1)[:, 0, :],
                 dy[:, dy_at[t] : window_end].indirect(dst[:, e0 // STRIPE : e1 // STRIPE]),
             )
 
-        def by_fours(rows):
-            return rows.rearrange("p t (c i) -> p c t i", i=4)
+        def plane_runs(planes):
+            return planes.rearrange("p t (c i) -> p c t i", i=RUN)
 
-        def grouped_by_fours(grouped):
-            return grouped.rearrange("p (c i t) -> p c t i", i=4, t=PACK)
+        def interleaved_runs(interleaved):
+            return interleaved.rearrange("p (c i t) -> p c t i", i=RUN, t=PLANES)
 
         def h_part(t0, t1, e0, e1):
-            c = e0 // CH
-            return h[c, t0][:, 0 : t1 - t0, e0 - c * CH : e1 - c * CH]
+            c = e0 // CHUNK
+            return h[c, t0][:, 0 : t1 - t0, e0 - edge[c] : e1 - edge[c]]
 
-        def factor(t0, t1, e0, e1):
+        def make_factor(t0, t1, e0, e1):
             part = h_part(t0, t1, e0, e1)
             nc.scalar.activation(part, part, SQUARE)
             nc.scalar.activation(part, part, COPY, bias=1.0, scale=-1.0)
 
         def form_dz(engine, t0, t1, e0, e1):
             engine.tensor_tensor(
-                grouped_by_fours(dz16[:, e0 * PACK : e1 * PACK])[:, :, t0:t1, :],
-                by_fours(g_part(t0, t1, e0, e1)),
-                by_fours(h_part(t0, t1, e0, e1)),
-                MULT,
-            )
-
-        def form_dz_by_edges(t0, t1, e0, e1):
-            nc.gpsimd.tensor_tensor(
-                dz16[:, e0 * PACK : e1 * PACK].rearrange("p (e t) -> p e t", t=PACK)[:, :, t0:t1],
-                g_part(t0, t1, e0, e1).rearrange("p t e -> p e t"),
-                h_part(t0, t1, e0, e1).rearrange("p t e -> p e t"),
+                interleaved_runs(dz16[:, e0 * PLANES : e1 * PLANES])[:, :, t0:t1, :],
+                plane_runs(gathered_part(t0, t1, e0, e1)),
+                plane_runs(h_part(t0, t1, e0, e1)),
                 MULT,
             )
 
         def quantize_dz(e0, e1):
             nc.vector.quantize_mx(
-                dz_codes[:, e0:e1].bitcast(E5M2), dz_scales[:, e0:e1], dz16[:, e0 * PACK : e1 * PACK]
+                dz_codes[:, e0:e1].bitcast(E5M2), dz_scales[:, e0:e1], dz16[:, e0 * PLANES : e1 * PLANES]
             )
 
-        def quantize_w(d0, d1, grouped):
-            nc.vector.quantize_mx(w_codes[:, d0:d1].bitcast(E4M3), w_scales[:, d0:d1], grouped)
+        def quantize_w(d0, d1, interleaved):
+            nc.vector.quantize_mx(w_codes[:, d0:d1].bitcast(E4M3), w_scales[:, d0:d1], interleaved)
 
-        def product(i, e0, keep_from, bank_tag):
-            bank = psum.tile([P, N_TILE], F32, name=f"bank{i}_{e0}", tag=f"bank{bank_tag}")
+        def multiply(i, e0, copy_from, bank_number):
+            bank = psum.tile([P, N_PASS], F32, name=f"bank{i}_{e0}", tag=f"bank{bank_number}")
             nc.tensor.matmul_mx(
                 bank[:],
                 lhsT=w_codes[:, i * P : (i + 1) * P].bitcast(E4M3),
                 lhsT_scale=w_scales[:, i * P : (i + 1) * P],
-                rhs=dz_codes[:, e0 : e0 + N_TILE].bitcast(E5M2),
-                rhs_scale=dz_scales[:, e0 : e0 + N_TILE],
+                rhs=dz_codes[:, e0 : e0 + N_PASS].bitcast(E5M2),
+                rhs_scale=dz_scales[:, e0 : e0 + N_PASS],
                 start=True,
                 stop=True,
             )
-            nc.scalar.copy(dm[i][:, keep_from : e0 + N_TILE], bank[:, keep_from - e0 :])
+            nc.scalar.copy(dm[i][:, copy_from : e0 + N_PASS], bank[:, copy_from - e0 :])
 
-        gather_dy(0, 0, 512, dy_at[1])
-        gather_dy(1, 0, 256, dy_at[2])
-        gather_dy(1, 256, 512, dy_at[2])
-        gather_dy(0, 768, 1024, dy_at[2])
-        gather_dy(2, 0, 512, dy_at[3])
-        gather_dy(3, 0, 256, dy_end)
-        gather_dy(3, 256, 512, dy_end)
-        for t in range(1, PACK):
-            gather_dy(t, 768, 1024, dy_end)
-        for t in range(PACK):
-            gather_dy(t, 512, 768, min(dy_end, dy_at[t] + 2048))
-        on_gpsimd = [(0, 2, 0, 256), (0, 2, 256, 512), (2, 4, 0, 256), (2, 4, 256, 512), (0, 4, 832, 1024)]
-        for piece in on_gpsimd:
-            factor(*piece)
-            form_dz_by_edges(*piece)
-        factor(0, 4, 512, 640)
-        w16 = keep.tile([P, P * PACK], BF16, name="w16", align_bytes=64)
-        nc.scalar.copy(grouped_by_fours(w16[:]), by_fours(w_first[:]))
-        factor(0, 4, 640, 768)
-        factor(0, 4, 768, 832)
-        quantize_dz(0, 512)
-        form_dz(nc.vector, 0, 4, 512, 640)
-        quantize_w(0, P, w16[:])
-        product(0, 0, 0, 0)
-        form_dz(nc.vector, 0, 4, 640, 768)
-        quantize_dz(512, 768)
-        product(0, 256, 512, 1)
-        form_dz(nc.vector, 0, 4, 768, 832)
-        quantize_dz(768, 1024)
-        product(0, 512, 768, 2)
-        w16r = keep.tile([P, (D - P) * PACK], BF16, name="w16r", tag="dz16", align_bytes=64)
-        nc.vector.tensor_copy(grouped_by_fours(w16r[:]), by_fours(w_rest[:]))
-        quantize_w(P, 2 * P, w16r[:, 0:512])
-        quantize_w(2 * P, D, w16r[:, 512:1536])
-        for i in range(1, 4):
-            for half in range(2):
-                product(i, half * N_TILE, half * N_TILE, (1 + 2 * i + half) % 8)
+        gather_dy(0, edge[0], edge[2], dy_at[1])
+        gather_dy(1, edge[0], edge[1], dy_at[2])
+        gather_dy(1, edge[1], edge[2], dy_at[2])
+        gather_dy(0, edge[3], edge[4], dy_at[2])
+        gather_dy(2, edge[0], edge[2], dy_at[3])
+        gather_dy(3, edge[0], edge[1], dy_end)
+        gather_dy(3, edge[1], edge[2], dy_end)
+        for t in range(1, PLANES):
+            gather_dy(t, edge[3], edge[4], dy_end)
+        for t in range(PLANES):
+            gather_dy(t, edge[2], edge[3], min(dy_end, dy_at[t] + WINDOW_MAX))
 
-        for i in range(4):
-            cuts = [(0, E)] if i < 3 else [(0, 448), (448, 384), (832, 192)]
+        for c, t0, t1 in pair_loads:
+            make_factor(t0, t1, edge[c], edge[c + 1])
+            form_dz(nc.gpsimd, t0, t1, edge[c], edge[c + 1])
+        make_factor(0, PLANES, E - HALF, E)
+        form_dz(nc.gpsimd, 0, PLANES, E - HALF, E)
+
+        make_factor(0, PLANES, edge[2], edge[2] + HALF)
+        w16_first = keep.tile([P, P * PLANES], BF16, name="w16", align_bytes=64)
+        nc.scalar.copy(interleaved_runs(w16_first[:]), plane_runs(w_first[:]))
+        make_factor(0, PLANES, edge[2] + HALF, edge[3])
+        make_factor(0, PLANES, edge[3], edge[3] + HALF)
+
+        quantize_dz(edge[0], edge[2])
+        form_dz(nc.vector, 0, PLANES, edge[2], edge[2] + HALF)
+        quantize_w(0, P, w16_first[:])
+        multiply(0, edge[0], edge[0], 0)
+        form_dz(nc.vector, 0, PLANES, edge[2] + HALF, edge[3])
+        quantize_dz(edge[2], edge[3])
+        multiply(0, edge[1], edge[2], 1)
+        form_dz(nc.vector, 0, PLANES, edge[3], edge[3] + HALF)
+        quantize_dz(edge[3], edge[4])
+        multiply(0, edge[2], edge[3], 2)
+
+        w16_rest = keep.tile([P, (D - P) * PLANES], BF16, name="w16r", tag="dz16", align_bytes=64)
+        nc.vector.tensor_copy(interleaved_runs(w16_rest[:]), plane_runs(w_rest[:]))
+        quantize_w(P, 2 * P, w16_rest[:, 0 : P * PLANES])
+        quantize_w(2 * P, D, w16_rest[:, P * PLANES :])
+        for i in range(1, DM_TILES):
+            for half in range(E // N_PASS):
+                multiply(i, half * N_PASS, half * N_PASS, (1 + 2 * i + half) % BANKS)
+
+        for i in range(DM_TILES):
+            last = i == DM_TILES - 1
             total = keep.tile([P, V], F32, name=f"total{i}")
-            for c0, n in cuts:
+            for c0, n in LAST_CUTS if last else [(0, E)]:
                 tag = "dz16" if i == 0 else f"picked{i}_{c0}"
                 picked = keep.tile([P, n], F32, name=f"picked{i}_{c0}", tag=tag, align_bytes=64)
                 nc.vector.tensor_copy(picked[:], dm[i][:].indirect(src[:, c0 // STRIPE : (c0 + n) // STRIPE]))
-                x = slice(c0 // K, (c0 + n) // K)
-                adder = nc.vector if i == 3 and c0 > 0 else nc.gpsimd
-                adder.tensor_tensor(total[:, x], picked[:, 0:n:2], picked[:, 1:n:2], ADD)
-                nc.sync.dma_start(out[i * P : (i + 1) * P, x], total[:, x])
+                nodes = slice(c0 // K, (c0 + n) // K)
+                adder = nc.vector if c0 > 0 else nc.gpsimd
+                adder.tensor_tensor(total[:, nodes], picked[:, 0:n:K], picked[:, 1:n:K], ADD)
+                nc.sync.dma_start(out[i * P : (i + 1) * P, nodes], total[:, nodes])

@@ -1,6 +1,7 @@
 from contextlib import ExitStack
 
 import concourse.mybir as mybir
+from concourse.masks import make_identity
 
 V, K, E, D, DV = 512, 2, 1024, 512, 512
 FLOPS = 2 * DV * D * E
@@ -23,6 +24,8 @@ N_PASS = 512
 BANKS = 8
 STRIPE = 16
 RUN = 4
+PAIR = 4
+G_LAST = 896
 CHUNK = 256
 HALF = CHUNK // 2
 DM_TILES = D // P
@@ -42,7 +45,7 @@ def tile_attend_gmp_tnh_kernel(tc, dyT, hE, wm, offs, offs2, out):
 
     edge = [c * CHUNK for c in range(E // CHUNK + 1)]
     pair_loads = [(c, t0, t0 + 2) for t0 in (0, 2) for c in (0, 1)]
-    whole_loads = [(3, 0, PLANES), (2, 0, PLANES)]
+    whole_loads = [(2, 0, PLANES), (3, 0, PLANES)]
 
     with ExitStack() as ctx:
         keep = ctx.enter_context(tc.tile_pool(name="keep", bufs=1))
@@ -95,17 +98,26 @@ def tile_attend_gmp_tnh_kernel(tc, dyT, hE, wm, offs, offs2, out):
         for i in range(DM_TILES - 1):
             nc.gpsimd.memset(dm[i][:, E:], 0.0)
 
+        identity = keep.tile([P, P], F32, name="identity")
+        make_identity(nc, identity[:])
+        minus_one = keep.tile([P, P], F32, name="minus_one")
+        nc.gpsimd.memset(minus_one[:], -1.0)
+        factor_banks = [psum.tile([P, PLANES, HALF], F32, name=f"factor{j}", tag=f"bank{4 + j}") for j in (0, 1)]
+        for bank in factor_banks:
+            for t in range(PLANES):
+                nc.tensor.matmul(bank[:, t, :], minus_one[:], identity[:], start=t == 0, stop=False, is_transpose=True)
+
         def gather_dy(t, e0, e1, window_end):
             nc.vector.tensor_copy(
                 gathered_part(t, t + 1, e0, e1)[:, 0, :],
                 dy[:, dy_at[t] : window_end].indirect(dst[:, e0 // STRIPE : e1 // STRIPE]),
             )
 
-        def plane_runs(planes):
-            return planes.rearrange("p t (c i) -> p c t i", i=RUN)
+        def plane_runs(planes, run=RUN):
+            return planes.rearrange("p t (c i) -> p c t i", i=run)
 
-        def interleaved_runs(interleaved):
-            return interleaved.rearrange("p (c i t) -> p c t i", i=RUN, t=PLANES)
+        def interleaved_runs(interleaved, run=RUN):
+            return interleaved.rearrange("p (c i t) -> p c t i", i=run, t=PLANES)
 
         def h_part(t0, t1, e0, e1):
             c = e0 // CHUNK
@@ -114,14 +126,32 @@ def tile_attend_gmp_tnh_kernel(tc, dyT, hE, wm, offs, offs2, out):
         def make_factor(t0, t1, e0, e1):
             part = h_part(t0, t1, e0, e1)
             nc.scalar.activation(part, part, SQUARE)
-            nc.scalar.activation(part, part, COPY, bias=1.0, scale=-1.0)
+            nc.scalar.activation(part, part, COPY, bias=-1.0)
 
         def form_dz(engine, t0, t1, e0, e1):
             engine.tensor_tensor(
-                interleaved_runs(dz16[:, e0 * PLANES : e1 * PLANES])[:, :, t0:t1, :],
-                plane_runs(gathered_part(t0, t1, e0, e1)),
-                plane_runs(h_part(t0, t1, e0, e1)),
+                interleaved_runs(dz16[:, e0 * PLANES : e1 * PLANES], PAIR)[:, :, t0:t1, :],
+                plane_runs(gathered_part(t0, t1, e0, e1), PAIR),
+                plane_runs(h_part(t0, t1, e0, e1), PAIR),
                 MULT,
+            )
+
+        pairs = [keep.tile([P, 2, CHUNK * 2], BF16, name=f"pairs{c}", align_bytes=64) for c in (0, 1)]
+
+        def form_pair(c, t0):
+            e0, e1 = edge[c], edge[c + 1]
+            nc.gpsimd.tensor_tensor(
+                pairs[c][:, t0 // 2, :].rearrange("p (c i t) -> p c t i", i=RUN, t=2),
+                plane_runs(gathered_part(t0, t0 + 2, e0, e1)),
+                plane_runs(h_part(t0, t0 + 2, e0, e1)),
+                MULT,
+            )
+
+        def weave_pairs(c):
+            words = dz16[:, edge[c] * PLANES : edge[c + 1] * PLANES].bitcast(U32)
+            nc.scalar.copy(
+                words.rearrange("p (c i u) -> p c u i", i=RUN, u=2),
+                pairs[c][:].bitcast(U32).rearrange("p u (c i) -> p c u i", i=RUN),
             )
 
         def quantize_dz(e0, e1):
@@ -143,42 +173,61 @@ def tile_attend_gmp_tnh_kernel(tc, dyT, hE, wm, offs, offs2, out):
                 start=True,
                 stop=True,
             )
-            nc.scalar.copy(dm[i][:, copy_from : e0 + N_PASS], bank[:, copy_from - e0 :])
+            nc.scalar.activation(dm[i][:, copy_from : e0 + N_PASS], bank[:, copy_from - e0 :], COPY, scale=-1.0)
 
         gather_dy(0, edge[0], edge[2], dy_at[1])
         gather_dy(1, edge[0], edge[1], dy_at[2])
         gather_dy(1, edge[1], edge[2], dy_at[2])
-        gather_dy(0, edge[3], edge[4], dy_at[2])
+        gather_dy(0, edge[2], edge[3], dy_at[2])
         gather_dy(2, edge[0], edge[2], dy_at[3])
         gather_dy(3, edge[0], edge[1], dy_end)
         gather_dy(3, edge[1], edge[2], dy_end)
         for t in range(1, PLANES):
-            gather_dy(t, edge[3], edge[4], dy_end)
-        for t in range(PLANES):
-            gather_dy(t, edge[2], edge[3], min(dy_end, dy_at[t] + WINDOW_MAX))
+            gather_dy(t, edge[2], edge[3], dy_end)
+        for t in range(PLANES - 1):
+            gather_dy(t, edge[3], edge[4], min(dy_end, dy_at[t] + WINDOW_MAX))
+        gather_dy(PLANES - 1, E - HALF, E, dy_end)
+        gather_dy(PLANES - 1, edge[3], E - HALF, dy_end)
 
         for c, t0, t1 in pair_loads:
             make_factor(t0, t1, edge[c], edge[c + 1])
-            form_dz(nc.gpsimd, t0, t1, edge[c], edge[c + 1])
-        make_factor(0, PLANES, E - HALF, E)
-        form_dz(nc.gpsimd, 0, PLANES, E - HALF, E)
+            form_pair(c, t0)
+        def make_factor_in_psum(j):
+            e0 = edge[2] + (j + 1) * HALF
+            turned = psum.tile([P, PLANES, P], F32, name=f"turned{j}", tag=f"bank{6 + j}")
+            for t in range(PLANES):
+                nc.tensor.transpose(turned[:, t, :], h_part(0, PLANES, e0, e0 + HALF)[:, t, :], identity[:])
+            squares = keep.tile([P, PLANES, P], F32, name=f"squares{j}")
+            nc.scalar.activation(squares[:], turned[:], SQUARE)
+            for t in range(PLANES):
+                nc.tensor.matmul(
+                    factor_banks[j][:, t, :], squares[:, t, :], identity[:], start=False, stop=t == PLANES - 1, is_transpose=True
+                )
 
         make_factor(0, PLANES, edge[2], edge[2] + HALF)
+        form_dz(nc.gpsimd, 0, PLANES, edge[2], edge[2] + HALF)
+        make_factor_in_psum(0)
+        make_factor(0, PLANES, E - HALF, E)
+        form_dz(nc.gpsimd, 0, PLANES, E - HALF, E)
+        make_factor_in_psum(1)
+        weave_pairs(0)
         w16_first = keep.tile([P, P * PLANES], BF16, name="w16", align_bytes=64)
         nc.scalar.copy(interleaved_runs(w16_first[:]), plane_runs(w_first[:]))
-        make_factor(0, PLANES, edge[2] + HALF, edge[3])
-        make_factor(0, PLANES, edge[3], edge[3] + HALF)
+        weave_pairs(1)
 
-        quantize_dz(edge[0], edge[2])
-        form_dz(nc.vector, 0, PLANES, edge[2], edge[2] + HALF)
+        for j in (0, 1):
+            e0 = edge[2] + (j + 1) * HALF
+            nc.vector.tensor_tensor(
+                interleaved_runs(dz16[:, e0 * PLANES : (e0 + HALF) * PLANES]),
+                plane_runs(gathered_part(0, PLANES, e0, e0 + HALF)),
+                plane_runs(factor_banks[j][:]),
+                MULT,
+            )
         quantize_w(0, P, w16_first[:])
+        quantize_dz(edge[0], edge[2])
         multiply(0, edge[0], edge[0], 0)
-        form_dz(nc.vector, 0, PLANES, edge[2] + HALF, edge[3])
-        quantize_dz(edge[2], edge[3])
-        multiply(0, edge[1], edge[2], 1)
-        form_dz(nc.vector, 0, PLANES, edge[3], edge[3] + HALF)
-        quantize_dz(edge[3], edge[4])
-        multiply(0, edge[2], edge[3], 2)
+        quantize_dz(edge[2], edge[4])
+        multiply(0, edge[2], edge[2], 1)
 
         w16_rest = keep.tile([P, (D - P) * PLANES], BF16, name="w16r", tag="dz16", align_bytes=64)
         nc.vector.tensor_copy(interleaved_runs(w16_rest[:]), plane_runs(w_rest[:]))
@@ -186,7 +235,7 @@ def tile_attend_gmp_tnh_kernel(tc, dyT, hE, wm, offs, offs2, out):
         quantize_w(2 * P, D, w16_rest[:, P * PLANES :])
         for i in range(1, DM_TILES):
             for half in range(E // N_PASS):
-                multiply(i, half * N_PASS, half * N_PASS, (1 + 2 * i + half) % BANKS)
+                multiply(i, half * N_PASS, half * N_PASS, 2 * i + half)
 
         for i in range(DM_TILES):
             last = i == DM_TILES - 1

@@ -25,7 +25,7 @@ BANKS = 8
 STRIPE = 16
 RUN = 4
 PAIR = 4
-G_LAST = 896
+G_END = 704
 CHUNK = 256
 HALF = CHUNK // 2
 DM_TILES = D // P
@@ -44,8 +44,8 @@ def tile_attend_gmp_tnh_kernel(tc, dyT, hE, wm, offs, offs2, out):
     w_rows = wm.rearrange("(p t) d -> p t d", t=PLANES)
 
     edge = [c * CHUNK for c in range(E // CHUNK + 1)]
-    pair_loads = [(c, t0, t0 + 2) for t0 in (0, 2) for c in (0, 1)]
-    whole_loads = [(2, 0, PLANES), (3, 0, PLANES)]
+    pair_loads = [(t0, t0 + 2, edge[c], edge[c + 1]) for t0 in (0, 2) for c in (0, 1)]
+    whole_loads = [(0, PLANES, edge[2], edge[3]), (0, PLANES, edge[3], edge[4])]
 
     with ExitStack() as ctx:
         keep = ctx.enter_context(tc.tile_pool(name="keep", bufs=1))
@@ -57,14 +57,14 @@ def tile_attend_gmp_tnh_kernel(tc, dyT, hE, wm, offs, offs2, out):
         dy_end = PLANES * V + 2 * DY_PAD
         dy = keep.tile([P, dy_end], F32, name="dy")
         h = {
-            (c, t0): keep.tile([P, t1 - t0, CHUNK], F32, name=f"h{c}_{t0}")
-            for c, t0, t1 in pair_loads + whole_loads
+            (t0, t1, e0, e1): keep.tile([P, t1 - t0, e1 - e0], F32, name=f"h{t0}_{e0}")
+            for t0, t1, e0, e1 in pair_loads + whole_loads
         }
         w_first = keep.tile([P, PLANES, P], F32, name="w_first")
         w_rest = keep.tile([P, PLANES, D - P], F32, name="w_rest")
 
-        def load_h(c, t0, t1):
-            nc.sync.dma_start(h[c, t0][:], h_rows[:, t0:t1, edge[c] : edge[c + 1]])
+        def load_h(t0, t1, e0, e1):
+            nc.sync.dma_start(h[t0, t1, e0, e1][:], h_rows[:, t0:t1, e0:e1])
 
         nc.sync.dma_start(dst[:], offs)
         for t in range(PLANES):
@@ -76,16 +76,21 @@ def tile_attend_gmp_tnh_kernel(tc, dyT, hE, wm, offs, offs2, out):
         nc.sync.dma_start(src[:], offs2)
         nc.sync.dma_start(w_rest[:], w_rows[:, :, P:D])
 
-        gathered_spans = [(edge[0], edge[2]), (edge[2], edge[3]), (edge[3], edge[4])]
+        gathered_spans = [(edge[0], edge[3]), (edge[3], edge[4])]
         gathered = [keep.tile([P, PLANES, e1 - e0], F32, name=f"g{e0}") for e0, e1 in gathered_spans]
 
         def gathered_part(t0, t1, e0, e1):
-            i = max(e0 // CHUNK - 1, 0)
+            i = e0 // edge[3]
             first = gathered_spans[i][0]
             return gathered[i][:, t0:t1, e0 - first : e1 - first]
 
         dz16 = keep.tile([P, E * PLANES], BF16, name="dz16", align_bytes=64)
-        dz_codes = keep.tile([P, E], U32, name="dz_codes", align_bytes=64)
+        held = ctx.enter_context(tc.tile_pool(name="held", bufs=1))
+        square_tiles = [
+            keep.tile([P, PLANES, P], F32, name="squares0"),
+            held.tile([P, PLANES, P], F32, name="squares1", align_bytes=64, offset=1024),
+        ]
+        dz_codes = {N_PASS: keep.tile([P, N_PASS], U32, name="dz_codes1", align_bytes=64)}
         dz_scales = keep.tile([P, E], U8, name="dz_scales", align_bytes=64)
         w_codes = keep.tile([P, D], U32, name="w_codes", align_bytes=64)
         w_scales = keep.tile([P, D], U8, name="w_scales", align_bytes=64)
@@ -120,13 +125,17 @@ def tile_attend_gmp_tnh_kernel(tc, dyT, hE, wm, offs, offs2, out):
             return interleaved.rearrange("p (c i t) -> p c t i", i=run, t=PLANES)
 
         def h_part(t0, t1, e0, e1):
-            c = e0 // CHUNK
-            return h[c, t0][:, 0 : t1 - t0, e0 - edge[c] : e1 - edge[c]]
+            key = [k for k in h if k[0] == t0 and k[2] <= e0 < k[3]][0]
+            return h[key][:, 0 : t1 - t0, e0 - key[2] : e1 - key[2]]
 
         def make_factor(t0, t1, e0, e1):
             part = h_part(t0, t1, e0, e1)
-            nc.scalar.activation(part, part, SQUARE)
-            nc.scalar.activation(part, part, COPY, bias=-1.0)
+            half = (t1 - t0) // 2
+            halves = [part[:, 0:half, :], part[:, half:, :]]
+            for planes in halves:
+                nc.scalar.activation(planes, planes, SQUARE)
+            for planes in halves:
+                nc.scalar.activation(planes, planes, COPY, bias=-1.0)
 
         def form_dz(engine, t0, t1, e0, e1):
             engine.tensor_tensor(
@@ -138,12 +147,11 @@ def tile_attend_gmp_tnh_kernel(tc, dyT, hE, wm, offs, offs2, out):
 
         pairs = [keep.tile([P, 2, CHUNK * 2], BF16, name=f"pairs{c}", align_bytes=64) for c in (0, 1)]
 
-        def form_pair(c, t0):
-            e0, e1 = edge[c], edge[c + 1]
+        def form_pair(t0, t1, e0, e1):
             nc.gpsimd.tensor_tensor(
-                pairs[c][:, t0 // 2, :].rearrange("p (c i t) -> p c t i", i=RUN, t=2),
-                plane_runs(gathered_part(t0, t0 + 2, e0, e1)),
-                plane_runs(h_part(t0, t0 + 2, e0, e1)),
+                pairs[e0 // CHUNK][:, t0 // 2, :].rearrange("p (c i t) -> p c t i", i=RUN, t=2),
+                plane_runs(gathered_part(t0, t1, e0, e1)),
+                plane_runs(h_part(t0, t1, e0, e1)),
                 MULT,
             )
 
@@ -156,7 +164,7 @@ def tile_attend_gmp_tnh_kernel(tc, dyT, hE, wm, offs, offs2, out):
 
         def quantize_dz(e0, e1):
             nc.vector.quantize_mx(
-                dz_codes[:, e0:e1].bitcast(E5M2), dz_scales[:, e0:e1], dz16[:, e0 * PLANES : e1 * PLANES]
+                dz_codes[e0][:].bitcast(E5M2), dz_scales[:, e0:e1], dz16[:, e0 * PLANES : e1 * PLANES]
             )
 
         def quantize_w(d0, d1, interleaved):
@@ -168,7 +176,7 @@ def tile_attend_gmp_tnh_kernel(tc, dyT, hE, wm, offs, offs2, out):
                 bank[:],
                 lhsT=w_codes[:, i * P : (i + 1) * P].bitcast(E4M3),
                 lhsT_scale=w_scales[:, i * P : (i + 1) * P],
-                rhs=dz_codes[:, e0 : e0 + N_PASS].bitcast(E5M2),
+                rhs=dz_codes[e0][:].bitcast(E5M2),
                 rhs_scale=dz_scales[:, e0 : e0 + N_PASS],
                 start=True,
                 stop=True,
@@ -186,37 +194,38 @@ def tile_attend_gmp_tnh_kernel(tc, dyT, hE, wm, offs, offs2, out):
             gather_dy(t, edge[2], edge[3], dy_end)
         for t in range(PLANES - 1):
             gather_dy(t, edge[3], edge[4], min(dy_end, dy_at[t] + WINDOW_MAX))
-        gather_dy(PLANES - 1, E - HALF, E, dy_end)
         gather_dy(PLANES - 1, edge[3], E - HALF, dy_end)
+        gather_dy(PLANES - 1, E - HALF, E, dy_end)
 
-        for c, t0, t1 in pair_loads:
-            make_factor(t0, t1, edge[c], edge[c + 1])
-            form_pair(c, t0)
+        for t0, t1, e0, e1 in pair_loads:
+            make_factor(t0, t1, e0, e1)
+            form_pair(t0, t1, e0, e1)
+
         def make_factor_in_psum(j):
-            e0 = edge[2] + (j + 1) * HALF
+            e0 = edge[3] + j * HALF
             turned = psum.tile([P, PLANES, P], F32, name=f"turned{j}", tag=f"bank{6 + j}")
             for t in range(PLANES):
                 nc.tensor.transpose(turned[:, t, :], h_part(0, PLANES, e0, e0 + HALF)[:, t, :], identity[:])
-            squares = keep.tile([P, PLANES, P], F32, name=f"squares{j}")
+            squares = square_tiles[j]
             nc.scalar.activation(squares[:], turned[:], SQUARE)
             for t in range(PLANES):
                 nc.tensor.matmul(
                     factor_banks[j][:, t, :], squares[:, t, :], identity[:], start=False, stop=t == PLANES - 1, is_transpose=True
                 )
 
-        make_factor(0, PLANES, edge[2], edge[2] + HALF)
-        form_dz(nc.gpsimd, 0, PLANES, edge[2], edge[2] + HALF)
+        for e0 in (edge[2], edge[2] + HALF):
+            make_factor(0, PLANES, e0, e0 + HALF)
+            form_dz(nc.gpsimd, 0, PLANES, e0, e0 + HALF)
         make_factor_in_psum(0)
-        make_factor(0, PLANES, E - HALF, E)
-        form_dz(nc.gpsimd, 0, PLANES, E - HALF, E)
         make_factor_in_psum(1)
         weave_pairs(0)
-        w16_first = keep.tile([P, P * PLANES], BF16, name="w16", align_bytes=64)
-        nc.scalar.copy(interleaved_runs(w16_first[:]), plane_runs(w_first[:]))
         weave_pairs(1)
+        w16_first = held.tile([P, P * PLANES], BF16, name="w16", align_bytes=64, offset=256)
+        nc.scalar.copy(interleaved_runs(w16_first[:]), plane_runs(w_first[:]))
+        dz_codes[0] = held.tile([P, N_PASS], U32, name="dz_codes0", align_bytes=64, offset=2304)
 
         for j in (0, 1):
-            e0 = edge[2] + (j + 1) * HALF
+            e0 = edge[3] + j * HALF
             nc.vector.tensor_tensor(
                 interleaved_runs(dz16[:, e0 * PLANES : (e0 + HALF) * PLANES]),
                 plane_runs(gathered_part(0, PLANES, e0, e0 + HALF)),

@@ -20,15 +20,13 @@ SQUARE = mybir.ActivationFunctionType.Square
 
 P = 128
 PLANES = 4
+PAIR = 2
 N_PASS = 512
-BANKS = 8
 STRIPE = 16
 RUN = 4
-PAIR = 4
-G_END = 704
 CHUNK = 256
-HALF = CHUNK // 2
 DM_TILES = D // P
+TURNS = CHUNK // P
 
 DY_PAD = 176
 DM_PAD = 352
@@ -44,11 +42,12 @@ def tile_attend_gmp_tnh_kernel(tc, dyT, hE, wm, offs, offs2, out):
     w_rows = wm.rearrange("(p t) d -> p t d", t=PLANES)
 
     edge = [c * CHUNK for c in range(E // CHUNK + 1)]
-    pair_loads = [(t0, t0 + 2, edge[c], edge[c + 1]) for t0 in (0, 2) for c in (0, 1)]
-    whole_loads = [(0, PLANES, edge[2], edge[3]), (0, PLANES, edge[3], edge[4])]
+    early_products = [(c, t0) for t0 in (0, PAIR) for c in (0, 1)]
+    late_products = [(2, t0) for t0 in (0, PAIR)]
 
     with ExitStack() as ctx:
         keep = ctx.enter_context(tc.tile_pool(name="keep", bufs=1))
+        shared = ctx.enter_context(tc.tile_pool(name="shared", bufs=1))
         psum = ctx.enter_context(tc.psum_pool(name="psum", bufs=1))
 
         dst = keep.tile([P, E // STRIPE], U16, name="dst")
@@ -56,43 +55,25 @@ def tile_attend_gmp_tnh_kernel(tc, dyT, hE, wm, offs, offs2, out):
         dy_at = [0, V + DY_PAD, 2 * V + DY_PAD, 3 * V + 2 * DY_PAD]
         dy_end = PLANES * V + 2 * DY_PAD
         dy = keep.tile([P, dy_end], F32, name="dy")
-        h = {
-            (t0, t1, e0, e1): keep.tile([P, t1 - t0, e1 - e0], F32, name=f"h{t0}_{e0}")
-            for t0, t1, e0, e1 in pair_loads + whole_loads
-        }
+        h_early = {(c, t0): keep.tile([P, PAIR, CHUNK], F32, name=f"h{c}_{t0}") for c, t0 in early_products}
+        h_late = {c: keep.tile([P, PLANES, CHUNK], F32, name=f"h{c}") for c in (2, 3)}
         w_first = keep.tile([P, PLANES, P], F32, name="w_first")
         w_rest = keep.tile([P, PLANES, D - P], F32, name="w_rest")
 
-        def load_h(t0, t1, e0, e1):
-            nc.sync.dma_start(h[t0, t1, e0, e1][:], h_rows[:, t0:t1, e0:e1])
-
         nc.sync.dma_start(dst[:], offs)
-        for t in range(PLANES):
+        for t, (c, t0) in enumerate(early_products):
             nc.sync.dma_start(dy[:, dy_at[t] : dy_at[t] + V], dy_rows[:, t, :])
-            load_h(*pair_loads[t])
-        for load in whole_loads:
-            load_h(*load)
+            nc.sync.dma_start(h_early[c, t0][:], h_rows[:, t0 : t0 + PAIR, edge[c] : edge[c + 1]])
+        for c in h_late:
+            nc.sync.dma_start(h_late[c][:], h_rows[:, :, edge[c] : edge[c + 1]])
         nc.sync.dma_start(w_first[:], w_rows[:, :, 0:P])
         nc.sync.dma_start(src[:], offs2)
         nc.sync.dma_start(w_rest[:], w_rows[:, :, P:D])
 
-        gathered_spans = [(edge[0], edge[3]), (edge[3], edge[4])]
-        gathered = [keep.tile([P, PLANES, e1 - e0], F32, name=f"g{e0}") for e0, e1 in gathered_spans]
-
-        def gathered_part(t0, t1, e0, e1):
-            i = e0 // edge[3]
-            first = gathered_spans[i][0]
-            return gathered[i][:, t0:t1, e0 - first : e1 - first]
-
+        gathered = [keep.tile([P, PLANES, N_PASS], F32, name=f"gathered{half}") for half in range(E // N_PASS)]
+        pairs = [keep.tile([P, PLANES // PAIR, CHUNK * PAIR], BF16, name=f"pairs{c}") for c in range(3)]
         dz16 = keep.tile([P, E * PLANES], BF16, name="dz16", align_bytes=64)
-        held = ctx.enter_context(tc.tile_pool(name="held", bufs=1))
-        square_tiles = [
-            keep.tile([P, PLANES, P], F32, name="squares0"),
-            held.tile([P, PLANES, P], F32, name="squares1", align_bytes=64, offset=1024),
-        ]
-        dz_codes = {N_PASS: keep.tile([P, N_PASS], U32, name="dz_codes1", align_bytes=64)}
         dz_scales = keep.tile([P, E], U8, name="dz_scales", align_bytes=64)
-        w_codes = keep.tile([P, D], U32, name="w_codes", align_bytes=64)
         w_scales = keep.tile([P, D], U8, name="w_scales", align_bytes=64)
         dm = [
             keep.tile([P, E + DM_PAD if i < DM_TILES - 1 else E], F32, name=f"dm{i}")
@@ -107,10 +88,17 @@ def tile_attend_gmp_tnh_kernel(tc, dyT, hE, wm, offs, offs2, out):
         make_identity(nc, identity[:])
         minus_one = keep.tile([P, P], F32, name="minus_one")
         nc.gpsimd.memset(minus_one[:], -1.0)
-        factor_banks = [psum.tile([P, PLANES, HALF], F32, name=f"factor{j}", tag=f"bank{4 + j}") for j in (0, 1)]
+        factor_banks = [
+            psum.tile([P, PLANES, P], F32, name=f"factor{j}", tag=f"bank{4 + j}") for j in range(TURNS)
+        ]
         for bank in factor_banks:
             for t in range(PLANES):
-                nc.tensor.matmul(bank[:, t, :], minus_one[:], identity[:], start=t == 0, stop=False, is_transpose=True)
+                nc.tensor.matmul(
+                    bank[:, t, :], minus_one[:], identity[:], start=t == 0, stop=False, is_transpose=True
+                )
+
+        def gathered_part(t0, t1, e0, e1):
+            return gathered[e0 // N_PASS][:, t0:t1, e0 % N_PASS : e0 % N_PASS + e1 - e0]
 
         def gather_dy(t, e0, e1, window_end):
             nc.vector.tensor_copy(
@@ -118,70 +106,42 @@ def tile_attend_gmp_tnh_kernel(tc, dyT, hE, wm, offs, offs2, out):
                 dy[:, dy_at[t] : window_end].indirect(dst[:, e0 // STRIPE : e1 // STRIPE]),
             )
 
-        def plane_runs(planes, run=RUN):
-            return planes.rearrange("p t (c i) -> p c t i", i=run)
+        def row_runs(rows):
+            return rows.rearrange("p t (c i) -> p c t i", i=RUN)
 
-        def interleaved_runs(interleaved, run=RUN):
-            return interleaved.rearrange("p (c i t) -> p c t i", i=run, t=PLANES)
+        def interleaved_runs(interleaved, rows):
+            return interleaved.rearrange("p (c i t) -> p c t i", i=RUN, t=rows)
 
-        def h_part(t0, t1, e0, e1):
-            key = [k for k in h if k[0] == t0 and k[2] <= e0 < k[3]][0]
-            return h[key][:, 0 : t1 - t0, e0 - key[2] : e1 - key[2]]
-
-        def make_factor(t0, t1, e0, e1):
-            part = h_part(t0, t1, e0, e1)
-            half = (t1 - t0) // 2
-            halves = [part[:, 0:half, :], part[:, half:, :]]
-            for planes in halves:
-                nc.scalar.activation(planes, planes, SQUARE)
-            for planes in halves:
-                nc.scalar.activation(planes, planes, COPY, bias=-1.0)
-
-        def form_dz(engine, t0, t1, e0, e1):
-            engine.tensor_tensor(
-                interleaved_runs(dz16[:, e0 * PLANES : e1 * PLANES], PAIR)[:, :, t0:t1, :],
-                plane_runs(gathered_part(t0, t1, e0, e1), PAIR),
-                plane_runs(h_part(t0, t1, e0, e1), PAIR),
-                MULT,
-            )
-
-        pairs = [keep.tile([P, 2, CHUNK * 2], BF16, name=f"pairs{c}", align_bytes=64) for c in (0, 1)]
-
-        def form_pair(t0, t1, e0, e1):
+        def form_pair(c, t0, h_pair):
+            for t in range(PAIR):
+                nc.scalar.activation(h_pair[:, t, :], h_pair[:, t, :], SQUARE)
+            for t in range(PAIR):
+                nc.scalar.activation(h_pair[:, t, :], h_pair[:, t, :], COPY, bias=-1.0)
             nc.gpsimd.tensor_tensor(
-                pairs[e0 // CHUNK][:, t0 // 2, :].rearrange("p (c i t) -> p c t i", i=RUN, t=2),
-                plane_runs(gathered_part(t0, t1, e0, e1)),
-                plane_runs(h_part(t0, t1, e0, e1)),
+                interleaved_runs(pairs[c][:, t0 // PAIR, :], PAIR),
+                row_runs(gathered_part(t0, t0 + PAIR, edge[c], edge[c + 1])),
+                row_runs(h_pair),
                 MULT,
             )
 
         def weave_pairs(c):
             words = dz16[:, edge[c] * PLANES : edge[c + 1] * PLANES].bitcast(U32)
-            nc.scalar.copy(
-                words.rearrange("p (c i u) -> p c u i", i=RUN, u=2),
-                pairs[c][:].bitcast(U32).rearrange("p u (c i) -> p c u i", i=RUN),
-            )
+            nc.scalar.copy(interleaved_runs(words, PLANES // PAIR), row_runs(pairs[c][:].bitcast(U32)))
 
-        def quantize_dz(e0, e1):
-            nc.vector.quantize_mx(
-                dz_codes[e0][:].bitcast(E5M2), dz_scales[:, e0:e1], dz16[:, e0 * PLANES : e1 * PLANES]
-            )
-
-        def quantize_w(d0, d1, interleaved):
-            nc.vector.quantize_mx(w_codes[:, d0:d1].bitcast(E4M3), w_scales[:, d0:d1], interleaved)
-
-        def multiply(i, e0, copy_from, bank_number):
-            bank = psum.tile([P, N_PASS], F32, name=f"bank{i}_{e0}", tag=f"bank{bank_number}")
-            nc.tensor.matmul_mx(
-                bank[:],
-                lhsT=w_codes[:, i * P : (i + 1) * P].bitcast(E4M3),
-                lhsT_scale=w_scales[:, i * P : (i + 1) * P],
-                rhs=dz_codes[e0][:].bitcast(E5M2),
-                rhs_scale=dz_scales[:, e0 : e0 + N_PASS],
-                start=True,
-                stop=True,
-            )
-            nc.scalar.activation(dm[i][:, copy_from : e0 + N_PASS], bank[:, copy_from - e0 :], COPY, scale=-1.0)
+        def make_factor_in_psum(j, squares):
+            turned = psum.tile([P, PLANES, P], F32, name=f"turned{j}", tag=f"bank{6 + j}")
+            for t in range(PLANES):
+                nc.tensor.transpose(turned[:, t, :], h_late[3][:, t, j * P : (j + 1) * P], identity[:])
+            nc.scalar.activation(squares[:], turned[:], SQUARE)
+            for t in range(PLANES):
+                nc.tensor.matmul(
+                    factor_banks[j][:, t, :],
+                    squares[:, t, :],
+                    identity[:],
+                    start=False,
+                    stop=t == PLANES - 1,
+                    is_transpose=True,
+                )
 
         gather_dy(0, edge[0], edge[2], dy_at[1])
         gather_dy(1, edge[0], edge[1], dy_at[2])
@@ -190,61 +150,82 @@ def tile_attend_gmp_tnh_kernel(tc, dyT, hE, wm, offs, offs2, out):
         gather_dy(2, edge[0], edge[2], dy_at[3])
         gather_dy(3, edge[0], edge[1], dy_end)
         gather_dy(3, edge[1], edge[2], dy_end)
-        for t in range(1, PLANES):
-            gather_dy(t, edge[2], edge[3], dy_end)
-        for t in range(PLANES - 1):
-            gather_dy(t, edge[3], edge[4], min(dy_end, dy_at[t] + WINDOW_MAX))
-        gather_dy(PLANES - 1, edge[3], E - HALF, dy_end)
-        gather_dy(PLANES - 1, E - HALF, E, dy_end)
+        gather_dy(1, edge[2], E, dy_end)
+        gather_dy(2, edge[2], E, dy_end)
+        gather_dy(3, edge[2], E - P, dy_end)
+        gather_dy(0, edge[3], E, WINDOW_MAX)
+        gather_dy(3, E - P, E, dy_end)
 
-        for t0, t1, e0, e1 in pair_loads:
-            make_factor(t0, t1, e0, e1)
-            form_pair(t0, t1, e0, e1)
+        for c, t0 in early_products:
+            form_pair(c, t0, h_early[c, t0][:])
+        for c, t0 in late_products:
+            form_pair(c, t0, h_late[c][:, t0 : t0 + PAIR, :])
 
-        def make_factor_in_psum(j):
-            e0 = edge[3] + j * HALF
-            turned = psum.tile([P, PLANES, P], F32, name=f"turned{j}", tag=f"bank{6 + j}")
-            for t in range(PLANES):
-                nc.tensor.transpose(turned[:, t, :], h_part(0, PLANES, e0, e0 + HALF)[:, t, :], identity[:])
-            squares = square_tiles[j]
-            nc.scalar.activation(squares[:], turned[:], SQUARE)
-            for t in range(PLANES):
-                nc.tensor.matmul(
-                    factor_banks[j][:, t, :], squares[:, t, :], identity[:], start=False, stop=t == PLANES - 1, is_transpose=True
-                )
+        first_squares = keep.tile([P, PLANES, P], F32, name="first_squares")
+        last_squares = shared.tile([P, PLANES, P], F32, name="last_squares", align_bytes=64, offset=0)
+        make_factor_in_psum(0, first_squares)
+        make_factor_in_psum(1, last_squares)
+        w_codes_first = shared.tile([P, P], U32, name="w_codes_first", align_bytes=64, offset=0)
+        w_codes_rest = keep.tile([P, D - P], U32, name="w_codes_rest", align_bytes=64)
+        dz_codes = [
+            shared.tile([P, N_PASS], U32, name="dz_codes0", align_bytes=64, offset=4 * P),
+            keep.tile([P, N_PASS], U32, name="dz_codes1", align_bytes=64),
+        ]
 
-        for e0 in (edge[2], edge[2] + HALF):
-            make_factor(0, PLANES, e0, e0 + HALF)
-            form_dz(nc.gpsimd, 0, PLANES, e0, e0 + HALF)
-        make_factor_in_psum(0)
-        make_factor_in_psum(1)
         weave_pairs(0)
         weave_pairs(1)
-        w16_first = held.tile([P, P * PLANES], BF16, name="w16", align_bytes=64, offset=256)
-        nc.scalar.copy(interleaved_runs(w16_first[:]), plane_runs(w_first[:]))
-        dz_codes[0] = held.tile([P, N_PASS], U32, name="dz_codes0", align_bytes=64, offset=2304)
+        w16_first = keep.tile([P, P * PLANES], BF16, name="w16_first", align_bytes=64)
+        nc.scalar.copy(interleaved_runs(w16_first[:], PLANES), row_runs(w_first[:]))
+        weave_pairs(2)
 
-        for j in (0, 1):
-            e0 = edge[3] + j * HALF
+        for j in range(TURNS):
+            e0 = edge[3] + j * P
             nc.vector.tensor_tensor(
-                interleaved_runs(dz16[:, e0 * PLANES : (e0 + HALF) * PLANES]),
-                plane_runs(gathered_part(0, PLANES, e0, e0 + HALF)),
-                plane_runs(factor_banks[j][:]),
+                interleaved_runs(dz16[:, e0 * PLANES : (e0 + P) * PLANES], PLANES),
+                row_runs(gathered_part(0, PLANES, e0, e0 + P)),
+                row_runs(factor_banks[j][:]),
                 MULT,
             )
-        quantize_w(0, P, w16_first[:])
-        quantize_dz(edge[0], edge[2])
-        multiply(0, edge[0], edge[0], 0)
-        quantize_dz(edge[2], edge[4])
-        multiply(0, edge[2], edge[2], 1)
 
-        w16_rest = keep.tile([P, (D - P) * PLANES], BF16, name="w16r", tag="dz16", align_bytes=64)
-        nc.vector.tensor_copy(interleaved_runs(w16_rest[:]), plane_runs(w_rest[:]))
+        def w_codes(d0, d1):
+            words = w_codes_first[:] if d0 == 0 else w_codes_rest[:, d0 - P : d1 - P]
+            return words.bitcast(E4M3)
+
+        def quantize_w(d0, d1, interleaved):
+            nc.vector.quantize_mx(w_codes(d0, d1), w_scales[:, d0:d1], interleaved)
+
+        def quantize_dz(half):
+            e0, e1 = half * N_PASS, (half + 1) * N_PASS
+            nc.vector.quantize_mx(
+                dz_codes[half][:].bitcast(E5M2), dz_scales[:, e0:e1], dz16[:, e0 * PLANES : e1 * PLANES]
+            )
+
+        def multiply(i, half):
+            edges = slice(half * N_PASS, (half + 1) * N_PASS)
+            bank = psum.tile([P, N_PASS], F32, name=f"pass{i}_{half}", tag=f"bank{2 * i + half}")
+            nc.tensor.matmul_mx(
+                bank[:],
+                lhsT=w_codes(i * P, (i + 1) * P),
+                lhsT_scale=w_scales[:, i * P : (i + 1) * P],
+                rhs=dz_codes[half][:].bitcast(E5M2),
+                rhs_scale=dz_scales[:, edges],
+                start=True,
+                stop=True,
+            )
+            nc.scalar.activation(dm[i][:, edges], bank[:], COPY, scale=-1.0)
+
+        quantize_w(0, P, w16_first[:])
+        for half in range(E // N_PASS):
+            quantize_dz(half)
+            multiply(0, half)
+
+        w16_rest = keep.tile([P, (D - P) * PLANES], BF16, name="w16_rest", tag="dz16", align_bytes=64)
+        nc.vector.tensor_copy(interleaved_runs(w16_rest[:], PLANES), row_runs(w_rest[:]))
         quantize_w(P, 2 * P, w16_rest[:, 0 : P * PLANES])
         quantize_w(2 * P, D, w16_rest[:, P * PLANES :])
         for i in range(1, DM_TILES):
             for half in range(E // N_PASS):
-                multiply(i, half * N_PASS, half * N_PASS, 2 * i + half)
+                multiply(i, half)
 
         for i in range(DM_TILES):
             last = i == DM_TILES - 1

@@ -26,11 +26,21 @@ STRIPE = 16
 RUN = 4
 CHUNK = 256
 DM_TILES = D // P
-TURNS = CHUNK // P
+SPLIT = 832
+PRODUCTS = [(0, 0, CHUNK), (0, CHUNK, N_PASS), (0, N_PASS, SPLIT), (PAIR, 0, N_PASS), (PAIR, N_PASS, SPLIT)]
+H_PIECES = [
+    (0, 0, 0, CHUNK),
+    (0, CHUNK, CHUNK, N_PASS),
+    (0, N_PASS, N_PASS, SPLIT),
+    (PAIR, 0, 0, CHUNK),
+    (PAIR, 0, CHUNK, N_PASS),
+    (PAIR, N_PASS, N_PASS, SPLIT),
+]
+WEAVES = [(0, N_PASS), (N_PASS, SPLIT)]
+TURNS = [(SPLIT, SPLIT + P), (SPLIT + P, E)]
 
-DY_PAD = 176
+DY_PADS = {0: 176, 3: 176}
 DM_PAD = 352
-WINDOW_MAX = 8 * CHUNK
 
 LAST_CUTS = [(0, 448), (448, 384), (832, 192)]
 
@@ -41,10 +51,6 @@ def tile_attend_gmp_tnh_kernel(tc, dyT, hE, wm, offs, offs2, out):
     h_rows = hE.rearrange("(p t) e -> p t e", t=PLANES)
     w_rows = wm.rearrange("(p t) d -> p t d", t=PLANES)
 
-    edge = [c * CHUNK for c in range(E // CHUNK + 1)]
-    early_products = [(c, t0) for t0 in (0, PAIR) for c in (0, 1)]
-    late_products = [(2, t0) for t0 in (0, PAIR)]
-
     with ExitStack() as ctx:
         keep = ctx.enter_context(tc.tile_pool(name="keep", bufs=1))
         shared = ctx.enter_context(tc.tile_pool(name="shared", bufs=1))
@@ -52,26 +58,49 @@ def tile_attend_gmp_tnh_kernel(tc, dyT, hE, wm, offs, offs2, out):
 
         dst = keep.tile([P, E // STRIPE], U16, name="dst")
         src = keep.tile([P, E // STRIPE], U16, name="src")
-        dy_at = [0, V + DY_PAD, 2 * V + DY_PAD, 3 * V + 2 * DY_PAD]
-        dy_end = PLANES * V + 2 * DY_PAD
+        dy_at = {2: 0, 0: V, 1: 2 * V + DY_PADS[0], 3: 3 * V + DY_PADS[0]}
+        dy_end = PLANES * V + sum(DY_PADS.values())
         dy = keep.tile([P, dy_end], F32, name="dy")
-        h_early = {(c, t0): keep.tile([P, PAIR, CHUNK], F32, name=f"h{c}_{t0}") for c, t0 in early_products}
-        h_late = {c: keep.tile([P, PLANES, CHUNK], F32, name=f"h{c}") for c in (2, 3)}
+        h_pair = {
+            (t0, e0): keep.tile([P, PAIR, e1 - e0], F32, name=f"h{t0}_{e0}") for t0, e0, e1 in PRODUCTS
+        }
+        h_turn = [keep.tile([P, PLANES * (e1 - e0)], F32, name=f"h_turn{e0}") for e0, e1 in TURNS]
         w_first = keep.tile([P, PLANES, P], F32, name="w_first")
         w_rest = keep.tile([P, PLANES, D - P], F32, name="w_rest")
 
-        nc.sync.dma_start(dst[:], offs)
-        for t, (c, t0) in enumerate(early_products):
+        def h_piece(t0, first, e0, e1):
+            return h_pair[t0, first][:, :, e0 - first : e1 - first]
+
+        def load_dy(t):
             nc.sync.dma_start(dy[:, dy_at[t] : dy_at[t] + V], dy_rows[:, t, :])
-            nc.sync.dma_start(h_early[c, t0][:], h_rows[:, t0 : t0 + PAIR, edge[c] : edge[c + 1]])
-        for c in h_late:
-            nc.sync.dma_start(h_late[c][:], h_rows[:, :, edge[c] : edge[c + 1]])
+
+        def load_h(t0, first, e0, e1):
+            nc.sync.dma_start(h_piece(t0, first, e0, e1), h_rows[:, t0 : t0 + PAIR, e0:e1])
+
+        nc.sync.dma_start(dst[:], offs)
+        load_dy(0)
+        load_h(*H_PIECES[0])
+        load_dy(1)
+        load_h(*H_PIECES[1])
+        load_h(*H_PIECES[2])
+        load_dy(2)
+        load_dy(3)
+        for piece in H_PIECES[3:]:
+            load_h(*piece)
+        for j, (e0, e1) in enumerate(TURNS):
+            nc.sync.dma_start(h_turn[j][:].rearrange("p (t e) -> p t e", t=PLANES), h_rows[:, :, e0:e1])
         nc.sync.dma_start(w_first[:], w_rows[:, :, 0:P])
         nc.sync.dma_start(src[:], offs2)
         nc.sync.dma_start(w_rest[:], w_rows[:, :, P:D])
 
         gathered = [keep.tile([P, PLANES, N_PASS], F32, name=f"gathered{half}") for half in range(E // N_PASS)]
-        pairs = [keep.tile([P, PLANES // PAIR, CHUNK * PAIR], BF16, name=f"pairs{c}") for c in range(3)]
+
+        def gathered_part(t0, t1, e0, e1):
+            return gathered[e0 // N_PASS][:, t0:t1, e0 % N_PASS : e0 % N_PASS + e1 - e0]
+
+        pairs = {
+            e0: keep.tile([P, PLANES // PAIR, (e1 - e0) * PAIR], BF16, name=f"pairs{e0}") for e0, e1 in WEAVES
+        }
         dz16 = keep.tile([P, E * PLANES], BF16, name="dz16", align_bytes=64)
         dz_scales = keep.tile([P, E], U8, name="dz_scales", align_bytes=64)
         w_scales = keep.tile([P, D], U8, name="w_scales", align_bytes=64)
@@ -79,8 +108,8 @@ def tile_attend_gmp_tnh_kernel(tc, dyT, hE, wm, offs, offs2, out):
             keep.tile([P, E + DM_PAD if i < DM_TILES - 1 else E], F32, name=f"dm{i}")
             for i in range(DM_TILES)
         ]
-        for t in (0, 2):
-            nc.vector.memset(dy[:, dy_at[t] + V : dy_at[t + 1]], 0.0)
+        for t, pad in DY_PADS.items():
+            nc.vector.memset(dy[:, dy_at[t] + V : dy_at[t] + V + pad], 0.0)
         for i in range(DM_TILES - 1):
             nc.gpsimd.memset(dm[i][:, E:], 0.0)
 
@@ -88,17 +117,15 @@ def tile_attend_gmp_tnh_kernel(tc, dyT, hE, wm, offs, offs2, out):
         make_identity(nc, identity[:])
         minus_one = keep.tile([P, P], F32, name="minus_one")
         nc.gpsimd.memset(minus_one[:], -1.0)
+        blocks = [range(0, PLANES * (e1 - e0), P) for e0, e1 in TURNS]
         factor_banks = [
-            psum.tile([P, PLANES, P], F32, name=f"factor{j}", tag=f"bank{4 + j}") for j in range(TURNS)
+            psum.tile([P, N_PASS], F32, name=f"factor{j}", tag=f"bank{4 + j}") for j in range(len(TURNS))
         ]
-        for bank in factor_banks:
-            for t in range(PLANES):
+        for j, bank in enumerate(factor_banks):
+            for c0 in blocks[j]:
                 nc.tensor.matmul(
-                    bank[:, t, :], minus_one[:], identity[:], start=t == 0, stop=False, is_transpose=True
+                    bank[:, c0 : c0 + P], minus_one[:], identity[:], start=c0 == 0, stop=False, is_transpose=True
                 )
-
-        def gathered_part(t0, t1, e0, e1):
-            return gathered[e0 // N_PASS][:, t0:t1, e0 % N_PASS : e0 % N_PASS + e1 - e0]
 
         def gather_dy(t, e0, e1, window_end):
             nc.vector.tensor_copy(
@@ -112,57 +139,68 @@ def tile_attend_gmp_tnh_kernel(tc, dyT, hE, wm, offs, offs2, out):
         def interleaved_runs(interleaved, rows):
             return interleaved.rearrange("p (c i t) -> p c t i", i=RUN, t=rows)
 
-        def form_pair(c, t0, h_pair):
-            for t in range(PAIR):
-                nc.scalar.activation(h_pair[:, t, :], h_pair[:, t, :], SQUARE)
-            for t in range(PAIR):
-                nc.scalar.activation(h_pair[:, t, :], h_pair[:, t, :], COPY, bias=-1.0)
+        def make_factor(parts):
+            for part in parts:
+                nc.scalar.activation(part, part, SQUARE)
+            for part in parts:
+                nc.scalar.activation(part, part, COPY, bias=-1.0)
+
+        def multiply_pair(t0, e0, e1):
+            first = max(w0 for w0, w1 in WEAVES if w0 <= e0)
             nc.gpsimd.tensor_tensor(
-                interleaved_runs(pairs[c][:, t0 // PAIR, :], PAIR),
-                row_runs(gathered_part(t0, t0 + PAIR, edge[c], edge[c + 1])),
-                row_runs(h_pair),
+                interleaved_runs(pairs[first][:, t0 // PAIR, (e0 - first) * PAIR : (e1 - first) * PAIR], PAIR),
+                row_runs(gathered_part(t0, t0 + PAIR, e0, e1)),
+                row_runs(h_pair[t0, e0][:]),
                 MULT,
             )
 
-        def weave_pairs(c):
-            words = dz16[:, edge[c] * PLANES : edge[c + 1] * PLANES].bitcast(U32)
-            nc.scalar.copy(interleaved_runs(words, PLANES // PAIR), row_runs(pairs[c][:].bitcast(U32)))
+        def weave_pairs(e0, e1):
+            words = dz16[:, e0 * PLANES : e1 * PLANES].bitcast(U32)
+            nc.scalar.copy(interleaved_runs(words, PLANES // PAIR), row_runs(pairs[e0][:].bitcast(U32)))
 
         def make_factor_in_psum(j, squares):
-            turned = psum.tile([P, PLANES, P], F32, name=f"turned{j}", tag=f"bank{6 + j}")
-            for t in range(PLANES):
-                nc.tensor.transpose(turned[:, t, :], h_late[3][:, t, j * P : (j + 1) * P], identity[:])
-            nc.scalar.activation(squares[:], turned[:], SQUARE)
-            for t in range(PLANES):
+            turned = psum.tile([P, N_PASS], F32, name=f"turned{j}", tag=f"bank{6 + j}")
+            width = blocks[j].stop
+            for c0 in blocks[j]:
+                nc.tensor.transpose(turned[:, c0 : c0 + P], h_turn[j][:, c0 : c0 + P], identity[:])
+            nc.scalar.activation(squares[:, 0:width], turned[:, 0:width], SQUARE)
+            for c0 in blocks[j]:
                 nc.tensor.matmul(
-                    factor_banks[j][:, t, :],
-                    squares[:, t, :],
+                    factor_banks[j][:, c0 : c0 + P],
+                    squares[:, c0 : c0 + P],
                     identity[:],
                     start=False,
-                    stop=t == PLANES - 1,
+                    stop=c0 + P == width,
                     is_transpose=True,
                 )
 
-        gather_dy(0, edge[0], edge[2], dy_at[1])
-        gather_dy(1, edge[0], edge[1], dy_at[2])
-        gather_dy(1, edge[1], edge[2], dy_at[2])
-        gather_dy(0, edge[2], edge[3], dy_at[2])
-        gather_dy(2, edge[0], edge[2], dy_at[3])
-        gather_dy(3, edge[0], edge[1], dy_end)
-        gather_dy(3, edge[1], edge[2], dy_end)
-        gather_dy(1, edge[2], E, dy_end)
-        gather_dy(2, edge[2], E, dy_end)
-        gather_dy(3, edge[2], E - P, dy_end)
-        gather_dy(0, edge[3], E, WINDOW_MAX)
-        gather_dy(3, E - P, E, dy_end)
+        def plane_end(t):
+            return dy_at[t] + V + DY_PADS.get(t, 0)
 
-        for c, t0 in early_products:
-            form_pair(c, t0, h_early[c, t0][:])
-        for c, t0 in late_products:
-            form_pair(c, t0, h_late[c][:, t0 : t0 + PAIR, :])
+        half, split, last = N_PASS, TURNS[0][0], TURNS[1][0]
+        gather_dy(0, 0, half, plane_end(0))
+        gather_dy(1, 0, CHUNK, dy_at[1] + V)
+        gather_dy(1, CHUNK, half, dy_at[1] + V)
+        gather_dy(0, half, split, dy_at[1] + V)
+        gather_dy(1, half, split, dy_at[1] + V)
+        gather_dy(2, 0, half, plane_end(0))
+        gather_dy(3, 0, half, dy_end)
+        gather_dy(2, half, E, dy_end)
+        gather_dy(3, half, last, dy_end)
+        gather_dy(0, split, E, dy_at[0] + 8 * (E - split))
+        gather_dy(1, split, E, dy_end)
+        gather_dy(3, last, E, dy_at[3] + V)
 
-        first_squares = keep.tile([P, PLANES, P], F32, name="first_squares")
-        last_squares = shared.tile([P, PLANES, P], F32, name="last_squares", align_bytes=64, offset=0)
+        pieces = [h_piece(*piece) for piece in H_PIECES]
+        make_factor([pieces[0][:, t, :] for t in range(PAIR)])
+        make_factor(pieces[1:3])
+        make_factor(pieces[3:5])
+        make_factor(pieces[5:6])
+        for product in PRODUCTS:
+            multiply_pair(*product)
+
+        first_squares = keep.tile([P, N_PASS], F32, name="first_squares")
+        last_squares = shared.tile([P, blocks[1].stop], F32, name="last_squares", align_bytes=64, offset=0)
         make_factor_in_psum(0, first_squares)
         make_factor_in_psum(1, last_squares)
         w_codes_first = shared.tile([P, P], U32, name="w_codes_first", align_bytes=64, offset=0)
@@ -172,18 +210,16 @@ def tile_attend_gmp_tnh_kernel(tc, dyT, hE, wm, offs, offs2, out):
             keep.tile([P, N_PASS], U32, name="dz_codes1", align_bytes=64),
         ]
 
-        weave_pairs(0)
-        weave_pairs(1)
         w16_first = keep.tile([P, P * PLANES], BF16, name="w16_first", align_bytes=64)
         nc.scalar.copy(interleaved_runs(w16_first[:], PLANES), row_runs(w_first[:]))
-        weave_pairs(2)
+        for e0, e1 in WEAVES:
+            weave_pairs(e0, e1)
 
-        for j in range(TURNS):
-            e0 = edge[3] + j * P
+        for j, (e0, e1) in enumerate(TURNS):
             nc.vector.tensor_tensor(
-                interleaved_runs(dz16[:, e0 * PLANES : (e0 + P) * PLANES], PLANES),
-                row_runs(gathered_part(0, PLANES, e0, e0 + P)),
-                row_runs(factor_banks[j][:]),
+                interleaved_runs(dz16[:, e0 * PLANES : e1 * PLANES], PLANES),
+                row_runs(gathered_part(0, PLANES, e0, e1)),
+                row_runs(factor_banks[j][:, 0 : blocks[j].stop].rearrange("p (t e) -> p t e", t=PLANES)),
                 MULT,
             )
 

@@ -26,21 +26,17 @@ STRIPE = 16
 RUN = 4
 CHUNK = 256
 DM_TILES = D // P
-SPLIT = 832
-PRODUCTS = [(0, 0, CHUNK), (0, CHUNK, N_PASS), (0, N_PASS, SPLIT), (PAIR, 0, N_PASS), (PAIR, N_PASS, SPLIT)]
-H_PIECES = [
-    (0, 0, 0, CHUNK),
-    (0, CHUNK, CHUNK, N_PASS),
-    (0, N_PASS, N_PASS, SPLIT),
-    (PAIR, 0, 0, CHUNK),
-    (PAIR, 0, CHUNK, N_PASS),
-    (PAIR, N_PASS, N_PASS, SPLIT),
-]
-WEAVES = [(0, N_PASS), (N_PASS, SPLIT)]
-TURNS = [(SPLIT, SPLIT + P), (SPLIT + P, E)]
+HALF = N_PASS
 
-DY_PADS = {0: 176, 3: 176}
+SPLIT = 832
+PRODUCTS = [(0, 0, CHUNK), (0, CHUNK, HALF), (0, HALF, SPLIT), (PAIR, 0, HALF), (PAIR, HALF, SPLIT)]
+WEAVES = [(0, HALF), (HALF, SPLIT)]
+LAST = SPLIT + P
+TURNS = [(SPLIT, LAST), (LAST, E)]
+
+DY_PAD = 176
 DM_PAD = 352
+WINDOW_PER_ENTRY = 8
 
 LAST_CUTS = [(0, 448), (448, 384), (832, 192)]
 
@@ -58,8 +54,8 @@ def tile_attend_gmp_tnh_kernel(tc, dyT, hE, wm, offs, offs2, out):
 
         dst = keep.tile([P, E // STRIPE], U16, name="dst")
         src = keep.tile([P, E // STRIPE], U16, name="src")
-        dy_at = {2: 0, 0: V, 1: 2 * V + DY_PADS[0], 3: 3 * V + DY_PADS[0]}
-        dy_end = PLANES * V + sum(DY_PADS.values())
+        dy_at = {2: 0, 0: V, 1: 2 * V + DY_PAD, 3: 3 * V + DY_PAD}
+        dy_end = PLANES * V + 2 * DY_PAD
         dy = keep.tile([P, dy_end], F32, name="dy")
         h_pair = {
             (t0, e0): keep.tile([P, PAIR, e1 - e0], F32, name=f"h{t0}_{e0}") for t0, e0, e1 in PRODUCTS
@@ -68,25 +64,26 @@ def tile_attend_gmp_tnh_kernel(tc, dyT, hE, wm, offs, offs2, out):
         w_first = keep.tile([P, PLANES, P], F32, name="w_first")
         w_rest = keep.tile([P, PLANES, D - P], F32, name="w_rest")
 
-        def h_piece(t0, first, e0, e1):
-            return h_pair[t0, first][:, :, e0 - first : e1 - first]
-
         def load_dy(t):
             nc.sync.dma_start(dy[:, dy_at[t] : dy_at[t] + V], dy_rows[:, t, :])
 
         def load_h(t0, first, e0, e1):
-            nc.sync.dma_start(h_piece(t0, first, e0, e1), h_rows[:, t0 : t0 + PAIR, e0:e1])
+            nc.sync.dma_start(h_pair[t0, first][:, :, e0 - first : e1 - first], h_rows[:, t0 : t0 + PAIR, e0:e1])
 
-        nc.sync.dma_start(dst[:], offs)
+        def load_h_second_half(t0):
+            load_h(t0, HALF, HALF, HALF + CHUNK)
+            load_h(t0, HALF, HALF + CHUNK, SPLIT)
+
         load_dy(0)
-        load_h(*H_PIECES[0])
+        nc.sync.dma_start(dst[:], offs)
+        load_h(0, 0, 0, CHUNK)
         load_dy(1)
-        load_h(*H_PIECES[1])
-        load_h(*H_PIECES[2])
-        load_dy(2)
-        load_dy(3)
-        for piece in H_PIECES[3:]:
-            load_h(*piece)
+        load_h(0, CHUNK, CHUNK, HALF)
+        load_h_second_half(0)
+        for t in range(PAIR, PLANES):
+            load_dy(t)
+            nc.sync.dma_start(h_pair[PAIR, 0][:, t - PAIR, :], h_rows[:, t, 0:HALF])
+        load_h_second_half(PAIR)
         for j, (e0, e1) in enumerate(TURNS):
             nc.sync.dma_start(h_turn[j][:].rearrange("p (t e) -> p t e", t=PLANES), h_rows[:, :, e0:e1])
         nc.sync.dma_start(w_first[:], w_rows[:, :, 0:P])
@@ -108,8 +105,8 @@ def tile_attend_gmp_tnh_kernel(tc, dyT, hE, wm, offs, offs2, out):
             keep.tile([P, E + DM_PAD if i < DM_TILES - 1 else E], F32, name=f"dm{i}")
             for i in range(DM_TILES)
         ]
-        for t, pad in DY_PADS.items():
-            nc.vector.memset(dy[:, dy_at[t] + V : dy_at[t] + V + pad], 0.0)
+        for t in (0, 3):
+            nc.vector.memset(dy[:, dy_at[t] + V : dy_at[t] + V + DY_PAD], 0.0)
         for i in range(DM_TILES - 1):
             nc.gpsimd.memset(dm[i][:, E:], 0.0)
 
@@ -146,7 +143,7 @@ def tile_attend_gmp_tnh_kernel(tc, dyT, hE, wm, offs, offs2, out):
                 nc.scalar.activation(part, part, COPY, bias=-1.0)
 
         def multiply_pair(t0, e0, e1):
-            first = max(w0 for w0, w1 in WEAVES if w0 <= e0)
+            first = e0 - e0 % HALF
             nc.gpsimd.tensor_tensor(
                 interleaved_runs(pairs[first][:, t0 // PAIR, (e0 - first) * PAIR : (e1 - first) * PAIR], PAIR),
                 row_runs(gathered_part(t0, t0 + PAIR, e0, e1)),
@@ -174,28 +171,27 @@ def tile_attend_gmp_tnh_kernel(tc, dyT, hE, wm, offs, offs2, out):
                     is_transpose=True,
                 )
 
-        def plane_end(t):
-            return dy_at[t] + V + DY_PADS.get(t, 0)
+        gather_dy(0, 0, HALF, dy_at[1])
+        gather_dy(0, HALF, HALF + P, dy_at[1])
+        gather_dy(1, 0, CHUNK, dy_at[3])
+        gather_dy(1, CHUNK, HALF, dy_at[3])
+        gather_dy(0, HALF + P, SPLIT, dy_at[3])
+        gather_dy(1, HALF, SPLIT, dy_at[3])
+        gather_dy(2, 0, HALF, dy_at[1])
+        gather_dy(3, 0, HALF, dy_end)
+        gather_dy(2, HALF, E, dy_end)
+        gather_dy(3, HALF, LAST, dy_end)
+        gather_dy(0, SPLIT, E, dy_at[0] + WINDOW_PER_ENTRY * (E - SPLIT))
+        gather_dy(1, SPLIT, E, dy_end)
+        gather_dy(3, LAST, E, dy_at[3] + V)
 
-        half, split, last = N_PASS, TURNS[0][0], TURNS[1][0]
-        gather_dy(0, 0, half, plane_end(0))
-        gather_dy(1, 0, CHUNK, dy_at[1] + V)
-        gather_dy(1, CHUNK, half, dy_at[1] + V)
-        gather_dy(0, half, split, dy_at[1] + V)
-        gather_dy(1, half, split, dy_at[1] + V)
-        gather_dy(2, 0, half, plane_end(0))
-        gather_dy(3, 0, half, dy_end)
-        gather_dy(2, half, E, dy_end)
-        gather_dy(3, half, last, dy_end)
-        gather_dy(0, split, E, dy_at[0] + 8 * (E - split))
-        gather_dy(1, split, E, dy_end)
-        gather_dy(3, last, E, dy_at[3] + V)
-
-        pieces = [h_piece(*piece) for piece in H_PIECES]
-        make_factor([pieces[0][:, t, :] for t in range(PAIR)])
-        make_factor(pieces[1:3])
-        make_factor(pieces[3:5])
-        make_factor(pieces[5:6])
+        for t0, e0, e1 in PRODUCTS:
+            planes = [h_pair[t0, e0][:, t, :] for t in range(PAIR)]
+            if e1 - e0 == HALF:
+                for plane in planes:
+                    make_factor([plane[:, 0:CHUNK], plane[:, CHUNK:HALF]])
+            else:
+                make_factor(planes)
         for product in PRODUCTS:
             multiply_pair(*product)
 

@@ -28,15 +28,15 @@ CHUNK = 256
 DM_TILES = D // P
 HALF = N_PASS
 
-SPLIT = 832
-PRODUCTS = [(0, 0, CHUNK), (0, CHUNK, HALF), (0, HALF, SPLIT), (PAIR, 0, HALF), (PAIR, HALF, SPLIT)]
-WEAVES = [(0, HALF), (HALF, SPLIT)]
-LAST = SPLIT + P
-TURNS = [(SPLIT, LAST), (LAST, E)]
+TAIL = E - CHUNK
+LAST = TAIL + P
+PRODUCTS = [(t0, e0, e0 + CHUNK) for t0 in (0, PAIR) for e0 in range(0, TAIL, CHUNK)] + [(0, TAIL, LAST)]
+WEAVES = [(0, HALF), (HALF, TAIL), (TAIL, LAST)]
+TURNS = [(PAIR, TAIL), (0, LAST)]
 
 DY_PAD = 176
 DM_PAD = 352
-WINDOW_PER_ENTRY = 8
+REACH = 64
 
 LAST_CUTS = [(0, 448), (448, 384), (832, 192)]
 
@@ -57,35 +57,36 @@ def tile_attend_gmp_tnh_kernel(tc, dyT, hE, wm, offs, offs2, out):
         dy_at = {2: 0, 0: V, 1: 2 * V + DY_PAD, 3: 3 * V + DY_PAD}
         dy_end = PLANES * V + 2 * DY_PAD
         dy = keep.tile([P, dy_end], F32, name="dy")
-        h_pair = {
-            (t0, e0): keep.tile([P, PAIR, e1 - e0], F32, name=f"h{t0}_{e0}") for t0, e0, e1 in PRODUCTS
-        }
-        h_turn = [keep.tile([P, PLANES * (e1 - e0)], F32, name=f"h_turn{e0}") for e0, e1 in TURNS]
+        h_spans = [(0, e0, CHUNK) for e0 in range(0, TAIL, CHUNK)] + [(PAIR, 0, HALF), (PAIR, HALF, CHUNK), (PAIR, TAIL, CHUNK)]
+        h = {(t0, e0): keep.tile([P, PAIR, n], F32, name=f"h{t0}_{e0}") for t0, e0, n in h_spans}
+        late = 4 * (P + N_PASS)
+        h[0, TAIL] = shared.tile([P, PAIR, CHUNK], F32, name="h_last", align_bytes=64, offset=late)
         w_first = keep.tile([P, PLANES, P], F32, name="w_first")
         w_rest = keep.tile([P, PLANES, D - P], F32, name="w_rest")
 
         def load_dy(t):
             nc.sync.dma_start(dy[:, dy_at[t] : dy_at[t] + V], dy_rows[:, t, :])
 
-        def load_h(t0, first, e0, e1):
-            nc.sync.dma_start(h_pair[t0, first][:, :, e0 - first : e1 - first], h_rows[:, t0 : t0 + PAIR, e0:e1])
+        def load_h(t0, e0):
+            nc.sync.dma_start(h[t0, e0][:], h_rows[:, t0 : t0 + PAIR, e0 : e0 + CHUNK])
 
-        def load_h_second_half(t0):
-            load_h(t0, HALF, HALF, HALF + CHUNK)
-            load_h(t0, HALF, HALF + CHUNK, SPLIT)
+        def h_part(t0, t1, e0, e1):
+            pair = t0 - t0 % PAIR
+            first = max(start for t, start in h if t == pair and start <= e0)
+            return h[pair, first][:, t0 - pair : t1 - pair, e0 - first : e1 - first]
 
         load_dy(0)
         nc.sync.dma_start(dst[:], offs)
-        load_h(0, 0, 0, CHUNK)
+        load_h(0, 0)
         load_dy(1)
-        load_h(0, CHUNK, CHUNK, HALF)
-        load_h_second_half(0)
+        load_h(0, CHUNK)
+        load_h(0, HALF)
         for t in range(PAIR, PLANES):
             load_dy(t)
-            nc.sync.dma_start(h_pair[PAIR, 0][:, t - PAIR, :], h_rows[:, t, 0:HALF])
-        load_h_second_half(PAIR)
-        for j, (e0, e1) in enumerate(TURNS):
-            nc.sync.dma_start(h_turn[j][:].rearrange("p (t e) -> p t e", t=PLANES), h_rows[:, :, e0:e1])
+            nc.sync.dma_start(h[PAIR, 0][:, t - PAIR, :], h_rows[:, t, 0:HALF])
+        load_h(PAIR, HALF)
+        load_h(PAIR, TAIL)
+        load_h(0, TAIL)
         nc.sync.dma_start(w_first[:], w_rows[:, :, 0:P])
         nc.sync.dma_start(src[:], offs2)
         nc.sync.dma_start(w_rest[:], w_rows[:, :, P:D])
@@ -98,7 +99,6 @@ def tile_attend_gmp_tnh_kernel(tc, dyT, hE, wm, offs, offs2, out):
         pairs = {
             e0: keep.tile([P, PLANES // PAIR, (e1 - e0) * PAIR], BF16, name=f"pairs{e0}") for e0, e1 in WEAVES
         }
-        dz16 = keep.tile([P, E * PLANES], BF16, name="dz16", align_bytes=64)
         dz_scales = keep.tile([P, E], U8, name="dz_scales", align_bytes=64)
         w_scales = keep.tile([P, D], U8, name="w_scales", align_bytes=64)
         dm = [
@@ -114,7 +114,7 @@ def tile_attend_gmp_tnh_kernel(tc, dyT, hE, wm, offs, offs2, out):
         make_identity(nc, identity[:])
         minus_one = keep.tile([P, P], F32, name="minus_one")
         nc.gpsimd.memset(minus_one[:], -1.0)
-        blocks = [range(0, PLANES * (e1 - e0), P) for e0, e1 in TURNS]
+        blocks = [range(0, (PLANES - t0) * P, P) for t0, e0 in TURNS]
         factor_banks = [
             psum.tile([P, N_PASS], F32, name=f"factor{j}", tag=f"bank{4 + j}") for j in range(len(TURNS))
         ]
@@ -136,19 +136,19 @@ def tile_attend_gmp_tnh_kernel(tc, dyT, hE, wm, offs, offs2, out):
         def interleaved_runs(interleaved, rows):
             return interleaved.rearrange("p (c i t) -> p c t i", i=RUN, t=rows)
 
-        def make_factor(parts):
-            for part in parts:
-                nc.scalar.activation(part, part, SQUARE)
+        def make_factor(parts, sources):
+            for part, source in zip(parts, sources):
+                nc.scalar.activation(part, source, SQUARE)
             for part in parts:
                 nc.scalar.activation(part, part, COPY, bias=-1.0)
 
-        def multiply_pair(t0, e0, e1):
-            first = e0 - e0 % HALF
+        def pair_runs(t0, e0, e1):
+            first = max(start for start in pairs if start <= e0)
+            return interleaved_runs(pairs[first][:, t0 // PAIR, (e0 - first) * PAIR : (e1 - first) * PAIR], PAIR)
+
+        def multiply_pair(t0, e0, e1, factor):
             nc.gpsimd.tensor_tensor(
-                interleaved_runs(pairs[first][:, t0 // PAIR, (e0 - first) * PAIR : (e1 - first) * PAIR], PAIR),
-                row_runs(gathered_part(t0, t0 + PAIR, e0, e1)),
-                row_runs(h_pair[t0, e0][:]),
-                MULT,
+                pair_runs(t0, e0, e1), row_runs(gathered_part(t0, t0 + PAIR, e0, e1)), row_runs(factor), MULT
             )
 
         def weave_pairs(e0, e1):
@@ -158,8 +158,10 @@ def tile_attend_gmp_tnh_kernel(tc, dyT, hE, wm, offs, offs2, out):
         def make_factor_in_psum(j, squares):
             turned = psum.tile([P, N_PASS], F32, name=f"turned{j}", tag=f"bank{6 + j}")
             width = blocks[j].stop
-            for c0 in blocks[j]:
-                nc.tensor.transpose(turned[:, c0 : c0 + P], h_turn[j][:, c0 : c0 + P], identity[:])
+            t0, e0 = TURNS[j]
+            for c0 in reversed(blocks[j]):
+                t = t0 + c0 // P
+                nc.tensor.transpose(turned[:, c0 : c0 + P], h_part(t, t + 1, e0, e0 + P)[:, 0, :], identity[:])
             nc.scalar.activation(squares[:, 0:width], turned[:, 0:width], SQUARE)
             for c0 in blocks[j]:
                 nc.tensor.matmul(
@@ -175,30 +177,35 @@ def tile_attend_gmp_tnh_kernel(tc, dyT, hE, wm, offs, offs2, out):
         gather_dy(0, HALF, HALF + P, dy_at[1])
         gather_dy(1, 0, CHUNK, dy_at[3])
         gather_dy(1, CHUNK, HALF, dy_at[3])
-        gather_dy(0, HALF + P, SPLIT, dy_at[3])
-        gather_dy(1, HALF, SPLIT, dy_at[3])
+        gather_dy(0, HALF + P, E, dy_at[1] + REACH)
+        gather_dy(1, HALF, TAIL, dy_at[3])
         gather_dy(2, 0, HALF, dy_at[1])
-        gather_dy(3, 0, HALF, dy_end)
+        gather_dy(3, 0, CHUNK, dy_end)
+        gather_dy(3, CHUNK, HALF, dy_end)
         gather_dy(2, HALF, E, dy_end)
         gather_dy(3, HALF, LAST, dy_end)
-        gather_dy(0, SPLIT, E, dy_at[0] + WINDOW_PER_ENTRY * (E - SPLIT))
-        gather_dy(1, SPLIT, E, dy_end)
+        gather_dy(1, TAIL, E, dy_end)
         gather_dy(3, LAST, E, dy_at[3] + V)
 
-        for t0, e0, e1 in PRODUCTS:
-            planes = [h_pair[t0, e0][:, t, :] for t in range(PAIR)]
-            if e1 - e0 == HALF:
-                for plane in planes:
-                    make_factor([plane[:, 0:CHUNK], plane[:, CHUNK:HALF]])
-            else:
-                make_factor(planes)
-        for product in PRODUCTS:
-            multiply_pair(*product)
+        def planes_of(t0, e0, e1):
+            return [h_part(t, t + 1, e0, e1)[:, 0, :] for t in range(t0, t0 + PAIR)]
 
-        first_squares = keep.tile([P, N_PASS], F32, name="first_squares")
+        for e0 in range(0, TAIL, CHUNK):
+            make_factor(planes_of(0, e0, e0 + CHUNK), planes_of(0, e0, e0 + CHUNK))
+        for t in range(PAIR, PLANES):
+            halves = [h_part(t, t + 1, e0, e0 + CHUNK)[:, 0, :] for e0 in range(0, HALF, CHUNK)]
+            make_factor(halves, halves)
+        make_factor(planes_of(PAIR, HALF, TAIL), planes_of(PAIR, HALF, TAIL))
+
+        first_squares = keep.tile([P, blocks[0].stop], F32, name="first_squares")
         last_squares = shared.tile([P, blocks[1].stop], F32, name="last_squares", align_bytes=64, offset=0)
+        last_factor = keep.tile([P, PAIR, P], F32, name="last_factor")
         make_factor_in_psum(0, first_squares)
+        make_factor([last_factor[:]], [h_part(0, PAIR, TAIL, LAST)])
         make_factor_in_psum(1, last_squares)
+        for t0, e0, e1 in PRODUCTS:
+            multiply_pair(t0, e0, e1, last_factor[:] if e0 == TAIL else h_part(t0, t0 + PAIR, e0, e1))
+
         w_codes_first = shared.tile([P, P], U32, name="w_codes_first", align_bytes=64, offset=0)
         w_codes_rest = keep.tile([P, D - P], U32, name="w_codes_rest", align_bytes=64)
         dz_codes = [
@@ -206,18 +213,21 @@ def tile_attend_gmp_tnh_kernel(tc, dyT, hE, wm, offs, offs2, out):
             keep.tile([P, N_PASS], U32, name="dz_codes1", align_bytes=64),
         ]
 
-        w16_first = keep.tile([P, P * PLANES], BF16, name="w16_first", align_bytes=64)
+        w16_first = shared.tile([P, P * PLANES], BF16, name="w16_first", align_bytes=64, offset=late)
+        dz16_at = late + 2 * P * PLANES
+        dz16 = shared.tile([P, E * PLANES], BF16, name="dz16", align_bytes=64, offset=dz16_at)
         nc.scalar.copy(interleaved_runs(w16_first[:], PLANES), row_runs(w_first[:]))
-        for e0, e1 in WEAVES:
-            weave_pairs(e0, e1)
 
-        for j, (e0, e1) in enumerate(TURNS):
+        for j, (t0, e0) in enumerate(TURNS):
+            whole = interleaved_runs(dz16[:, e0 * PLANES : (e0 + P) * PLANES], PLANES)
             nc.vector.tensor_tensor(
-                interleaved_runs(dz16[:, e0 * PLANES : e1 * PLANES], PLANES),
-                row_runs(gathered_part(0, PLANES, e0, e1)),
-                row_runs(factor_banks[j][:, 0 : blocks[j].stop].rearrange("p (t e) -> p t e", t=PLANES)),
+                whole if t0 == 0 else pair_runs(t0, e0, e0 + P),
+                row_runs(gathered_part(t0, PLANES, e0, e0 + P)),
+                row_runs(factor_banks[j][:, 0 : blocks[j].stop].rearrange("p (t e) -> p t e", e=P)),
                 MULT,
             )
+        for e0, e1 in WEAVES:
+            weave_pairs(e0, e1)
 
         def w_codes(d0, d1):
             words = w_codes_first[:] if d0 == 0 else w_codes_rest[:, d0 - P : d1 - P]
@@ -251,7 +261,7 @@ def tile_attend_gmp_tnh_kernel(tc, dyT, hE, wm, offs, offs2, out):
             quantize_dz(half)
             multiply(0, half)
 
-        w16_rest = keep.tile([P, (D - P) * PLANES], BF16, name="w16_rest", tag="dz16", align_bytes=64)
+        w16_rest = shared.tile([P, (D - P) * PLANES], BF16, name="w16_rest", align_bytes=64, offset=dz16_at)
         nc.vector.tensor_copy(interleaved_runs(w16_rest[:], PLANES), row_runs(w_rest[:]))
         quantize_w(P, 2 * P, w16_rest[:, 0 : P * PLANES])
         quantize_w(2 * P, D, w16_rest[:, P * PLANES :])
@@ -263,8 +273,10 @@ def tile_attend_gmp_tnh_kernel(tc, dyT, hE, wm, offs, offs2, out):
             last = i == DM_TILES - 1
             total = keep.tile([P, V], F32, name=f"total{i}")
             for c0, n in LAST_CUTS if last else [(0, E)]:
-                tag = "dz16" if i == 0 else f"picked{i}_{c0}"
-                picked = keep.tile([P, n], F32, name=f"picked{i}_{c0}", tag=tag, align_bytes=64)
+                if i == 0:
+                    picked = shared.tile([P, n], F32, name="picked0", align_bytes=64, offset=dz16_at)
+                else:
+                    picked = keep.tile([P, n], F32, name=f"picked{i}_{c0}")
                 nc.vector.tensor_copy(picked[:], dm[i][:].indirect(src[:, c0 // STRIPE : (c0 + n) // STRIPE]))
                 nodes = slice(c0 // K, (c0 + n) // K)
                 adder = nc.vector if c0 > 0 else nc.gpsimd

@@ -26,13 +26,14 @@ STRIPE = 16
 RUN = 4
 CHUNK = 256
 DM_TILES = D // P
-HALF = N_PASS
+HALF = E // 2
 
-TAIL = E - CHUNK
-LAST = TAIL + P
-PRODUCTS = [(t0, e0, e0 + CHUNK) for t0 in (0, PAIR) for e0 in range(0, TAIL, CHUNK)] + [(0, TAIL, LAST)]
-WEAVES = [(0, HALF), (HALF, TAIL), (TAIL, LAST)]
-TURNS = [(PAIR, TAIL), (0, LAST)]
+SPLIT = E - CHUNK
+LAST = SPLIT + P
+CHUNKS = range(0, SPLIT, CHUNK)
+PRODUCTS = [(t0, e0) for t0 in (0, PAIR) for e0 in CHUNKS]
+TURNS = [SPLIT, LAST]
+PASS_CHUNKS = [(0, SPLIT), (CHUNK, 2 * CHUNK)]
 
 DY_PAD = 176
 DM_PAD = 352
@@ -57,10 +58,9 @@ def tile_attend_gmp_tnh_kernel(tc, dyT, hE, wm, offs, offs2, out):
         dy_at = {2: 0, 0: V, 1: 2 * V + DY_PAD, 3: 3 * V + DY_PAD}
         dy_end = PLANES * V + 2 * DY_PAD
         dy = keep.tile([P, dy_end], F32, name="dy")
-        h_spans = [(0, e0, CHUNK) for e0 in range(0, TAIL, CHUNK)] + [(PAIR, 0, HALF), (PAIR, HALF, CHUNK), (PAIR, TAIL, CHUNK)]
-        h = {(t0, e0): keep.tile([P, PAIR, n], F32, name=f"h{t0}_{e0}") for t0, e0, n in h_spans}
-        late = 4 * (P + N_PASS)
-        h[0, TAIL] = shared.tile([P, PAIR, CHUNK], F32, name="h_last", align_bytes=64, offset=late)
+        h = {key: keep.tile([P, PAIR, CHUNK], F32, name=f"h{key[0]}_{key[1]}") for key in PRODUCTS + [(PAIR, SPLIT)]}
+        late = 4 * (P + 2 * N_PASS)
+        h[0, SPLIT] = shared.tile([P, PAIR, CHUNK], F32, name="h_last", align_bytes=64, offset=late)
         w_first = keep.tile([P, PLANES, P], F32, name="w_first")
         w_rest = keep.tile([P, PLANES, D - P], F32, name="w_rest")
 
@@ -70,23 +70,19 @@ def tile_attend_gmp_tnh_kernel(tc, dyT, hE, wm, offs, offs2, out):
         def load_h(t0, e0):
             nc.sync.dma_start(h[t0, e0][:], h_rows[:, t0 : t0 + PAIR, e0 : e0 + CHUNK])
 
-        def h_part(t0, t1, e0, e1):
-            pair = t0 - t0 % PAIR
-            first = max(start for t, start in h if t == pair and start <= e0)
-            return h[pair, first][:, t0 - pair : t1 - pair, e0 - first : e1 - first]
-
         load_dy(0)
         nc.sync.dma_start(dst[:], offs)
         load_h(0, 0)
         load_dy(1)
         load_h(0, CHUNK)
-        load_h(0, HALF)
-        for t in range(PAIR, PLANES):
-            load_dy(t)
-            nc.sync.dma_start(h[PAIR, 0][:, t - PAIR, :], h_rows[:, t, 0:HALF])
-        load_h(PAIR, HALF)
-        load_h(PAIR, TAIL)
-        load_h(0, TAIL)
+        load_h(0, 2 * CHUNK)
+        load_dy(2)
+        load_h(PAIR, 0)
+        load_dy(3)
+        load_h(PAIR, CHUNK)
+        load_h(PAIR, 2 * CHUNK)
+        load_h(PAIR, SPLIT)
+        load_h(0, SPLIT)
         nc.sync.dma_start(w_first[:], w_rows[:, :, 0:P])
         nc.sync.dma_start(src[:], offs2)
         nc.sync.dma_start(w_rest[:], w_rows[:, :, P:D])
@@ -96,9 +92,11 @@ def tile_attend_gmp_tnh_kernel(tc, dyT, hE, wm, offs, offs2, out):
         def gathered_part(t0, t1, e0, e1):
             return gathered[e0 // N_PASS][:, t0:t1, e0 % N_PASS : e0 % N_PASS + e1 - e0]
 
-        pairs = {
-            e0: keep.tile([P, PLANES // PAIR, (e1 - e0) * PAIR], BF16, name=f"pairs{e0}") for e0, e1 in WEAVES
-        }
+        def place(e):
+            first = e - e % CHUNK
+            return [e0 for chunks in PASS_CHUNKS for e0 in chunks].index(first) * CHUNK + e - first
+
+        pairs = {e0: keep.tile([P, PLANES // PAIR, CHUNK * PAIR], BF16, name=f"pairs{e0}") for e0 in CHUNKS}
         dz_scales = keep.tile([P, E], U8, name="dz_scales", align_bytes=64)
         w_scales = keep.tile([P, D], U8, name="w_scales", align_bytes=64)
         dm = [
@@ -114,12 +112,12 @@ def tile_attend_gmp_tnh_kernel(tc, dyT, hE, wm, offs, offs2, out):
         make_identity(nc, identity[:])
         minus_one = keep.tile([P, P], F32, name="minus_one")
         nc.gpsimd.memset(minus_one[:], -1.0)
-        blocks = [range(0, (PLANES - t0) * P, P) for t0, e0 in TURNS]
+        blocks = range(0, N_PASS, P)
         factor_banks = [
             psum.tile([P, N_PASS], F32, name=f"factor{j}", tag=f"bank{4 + j}") for j in range(len(TURNS))
         ]
-        for j, bank in enumerate(factor_banks):
-            for c0 in blocks[j]:
+        for bank in factor_banks:
+            for c0 in blocks:
                 nc.tensor.matmul(
                     bank[:, c0 : c0 + P], minus_one[:], identity[:], start=c0 == 0, stop=False, is_transpose=True
                 )
@@ -136,40 +134,43 @@ def tile_attend_gmp_tnh_kernel(tc, dyT, hE, wm, offs, offs2, out):
         def interleaved_runs(interleaved, rows):
             return interleaved.rearrange("p (c i t) -> p c t i", i=RUN, t=rows)
 
-        def make_factor(parts, sources):
-            for part, source in zip(parts, sources):
-                nc.scalar.activation(part, source, SQUARE)
+        def make_factor(parts):
+            for part in parts:
+                nc.scalar.activation(part, part, SQUARE)
             for part in parts:
                 nc.scalar.activation(part, part, COPY, bias=-1.0)
 
-        def pair_runs(t0, e0, e1):
-            first = max(start for start in pairs if start <= e0)
-            return interleaved_runs(pairs[first][:, t0 // PAIR, (e0 - first) * PAIR : (e1 - first) * PAIR], PAIR)
-
-        def multiply_pair(t0, e0, e1, factor):
+        def multiply_pair(t0, e0):
             nc.gpsimd.tensor_tensor(
-                pair_runs(t0, e0, e1), row_runs(gathered_part(t0, t0 + PAIR, e0, e1)), row_runs(factor), MULT
+                interleaved_runs(pairs[e0][:, t0 // PAIR, :], PAIR),
+                row_runs(gathered_part(t0, t0 + PAIR, e0, e0 + CHUNK)),
+                row_runs(h[t0, e0][:]),
+                MULT,
             )
 
-        def weave_pairs(e0, e1):
-            words = dz16[:, e0 * PLANES : e1 * PLANES].bitcast(U32)
+        def dz_part(e0, e1):
+            return dz16[:, place(e0) * PLANES : (place(e0) + e1 - e0) * PLANES]
+
+        def weave_pairs(e0):
+            words = dz_part(e0, e0 + CHUNK).bitcast(U32)
             nc.scalar.copy(interleaved_runs(words, PLANES // PAIR), row_runs(pairs[e0][:].bitcast(U32)))
 
-        def make_factor_in_psum(j, squares):
-            turned = psum.tile([P, N_PASS], F32, name=f"turned{j}", tag=f"bank{6 + j}")
-            width = blocks[j].stop
-            t0, e0 = TURNS[j]
-            for c0 in reversed(blocks[j]):
-                t = t0 + c0 // P
-                nc.tensor.transpose(turned[:, c0 : c0 + P], h_part(t, t + 1, e0, e0 + P)[:, 0, :], identity[:])
-            nc.scalar.activation(squares[:, 0:width], turned[:, 0:width], SQUARE)
-            for c0 in blocks[j]:
+        def turn(t0):
+            turned = psum.tile([P, N_PASS], F32, name=f"turned{t0}", tag=f"bank{6 + t0 // PAIR}")
+            for c0 in blocks:
+                j, t = divmod(c0 // P, PAIR)
+                nc.tensor.transpose(turned[:, c0 : c0 + P], h[t0, SPLIT][:, t, j * P : (j + 1) * P], identity[:])
+            return turned
+
+        def turn_back(squares, t0, j):
+            for t in range(PAIR):
+                c0 = (j * PAIR + t) * P
                 nc.tensor.matmul(
-                    factor_banks[j][:, c0 : c0 + P],
+                    factor_banks[j][:, (t0 + t) * P : (t0 + t + 1) * P],
                     squares[:, c0 : c0 + P],
                     identity[:],
                     start=False,
-                    stop=c0 + P == width,
+                    stop=t0 == 0 and t == PAIR - 1,
                     is_transpose=True,
                 )
 
@@ -178,39 +179,37 @@ def tile_attend_gmp_tnh_kernel(tc, dyT, hE, wm, offs, offs2, out):
         gather_dy(1, 0, CHUNK, dy_at[3])
         gather_dy(1, CHUNK, HALF, dy_at[3])
         gather_dy(0, HALF + P, E, dy_at[1] + REACH)
-        gather_dy(1, HALF, TAIL, dy_at[3])
+        gather_dy(1, HALF, SPLIT, dy_at[3])
         gather_dy(2, 0, HALF, dy_at[1])
         gather_dy(3, 0, CHUNK, dy_end)
         gather_dy(3, CHUNK, HALF, dy_end)
         gather_dy(2, HALF, E, dy_end)
         gather_dy(3, HALF, LAST, dy_end)
-        gather_dy(1, TAIL, E, dy_end)
+        gather_dy(1, SPLIT, E, dy_end)
         gather_dy(3, LAST, E, dy_at[3] + V)
 
-        def planes_of(t0, e0, e1):
-            return [h_part(t, t + 1, e0, e1)[:, 0, :] for t in range(t0, t0 + PAIR)]
+        for product in PRODUCTS:
+            make_factor([h[product][:, t, :] for t in range(PAIR)])
+        for product in PRODUCTS:
+            multiply_pair(*product)
 
-        for e0 in range(0, TAIL, CHUNK):
-            make_factor(planes_of(0, e0, e0 + CHUNK), planes_of(0, e0, e0 + CHUNK))
-        for t in range(PAIR, PLANES):
-            halves = [h_part(t, t + 1, e0, e0 + CHUNK)[:, 0, :] for e0 in range(0, HALF, CHUNK)]
-            make_factor(halves, halves)
-        make_factor(planes_of(PAIR, HALF, TAIL), planes_of(PAIR, HALF, TAIL))
+        first_squares = keep.tile([P, N_PASS], F32, name="first_squares")
+        last_squares = shared.tile([P, N_PASS], F32, name="last_squares", align_bytes=64, offset=2 * N_PASS)
+        turned = turn(PAIR)
+        nc.scalar.activation(first_squares[:], turned[:], SQUARE)
+        turned = turn(0)
+        for j in range(len(TURNS)):
+            turn_back(first_squares, PAIR, j)
+        for j in range(len(TURNS)):
+            columns = slice(j * PAIR * P, (j + 1) * PAIR * P)
+            nc.scalar.activation(last_squares[:, columns], turned[:, columns], SQUARE)
+            turn_back(last_squares, 0, j)
 
-        first_squares = keep.tile([P, blocks[0].stop], F32, name="first_squares")
-        last_squares = shared.tile([P, blocks[1].stop], F32, name="last_squares", align_bytes=64, offset=0)
-        last_factor = keep.tile([P, PAIR, P], F32, name="last_factor")
-        make_factor_in_psum(0, first_squares)
-        make_factor([last_factor[:]], [h_part(0, PAIR, TAIL, LAST)])
-        make_factor_in_psum(1, last_squares)
-        for t0, e0, e1 in PRODUCTS:
-            multiply_pair(t0, e0, e1, last_factor[:] if e0 == TAIL else h_part(t0, t0 + PAIR, e0, e1))
-
-        w_codes_first = shared.tile([P, P], U32, name="w_codes_first", align_bytes=64, offset=0)
+        w_codes_first = shared.tile([P, P], U32, name="w_codes_first", align_bytes=64, offset=4 * N_PASS)
         w_codes_rest = keep.tile([P, D - P], U32, name="w_codes_rest", align_bytes=64)
         dz_codes = [
-            shared.tile([P, N_PASS], U32, name="dz_codes0", align_bytes=64, offset=4 * P),
-            keep.tile([P, N_PASS], U32, name="dz_codes1", align_bytes=64),
+            shared.tile([P, N_PASS], U32, name="dz_codes0", align_bytes=64, offset=0),
+            shared.tile([P, N_PASS], U32, name="dz_codes1", align_bytes=64, offset=4 * (N_PASS + P)),
         ]
 
         w16_first = shared.tile([P, P * PLANES], BF16, name="w16_first", align_bytes=64, offset=late)
@@ -218,16 +217,16 @@ def tile_attend_gmp_tnh_kernel(tc, dyT, hE, wm, offs, offs2, out):
         dz16 = shared.tile([P, E * PLANES], BF16, name="dz16", align_bytes=64, offset=dz16_at)
         nc.scalar.copy(interleaved_runs(w16_first[:], PLANES), row_runs(w_first[:]))
 
-        for j, (t0, e0) in enumerate(TURNS):
-            whole = interleaved_runs(dz16[:, e0 * PLANES : (e0 + P) * PLANES], PLANES)
+        for e0 in CHUNKS:
+            weave_pairs(e0)
+
+        for j, e0 in enumerate(TURNS):
             nc.vector.tensor_tensor(
-                whole if t0 == 0 else pair_runs(t0, e0, e0 + P),
-                row_runs(gathered_part(t0, PLANES, e0, e0 + P)),
-                row_runs(factor_banks[j][:, 0 : blocks[j].stop].rearrange("p (t e) -> p t e", e=P)),
+                interleaved_runs(dz_part(e0, e0 + P), PLANES),
+                row_runs(gathered_part(0, PLANES, e0, e0 + P)),
+                row_runs(factor_banks[j][:].rearrange("p (t e) -> p t e", e=P)),
                 MULT,
             )
-        for e0, e1 in WEAVES:
-            weave_pairs(e0, e1)
 
         def w_codes(d0, d1):
             words = w_codes_first[:] if d0 == 0 else w_codes_rest[:, d0 - P : d1 - P]
@@ -236,10 +235,12 @@ def tile_attend_gmp_tnh_kernel(tc, dyT, hE, wm, offs, offs2, out):
         def quantize_w(d0, d1, interleaved):
             nc.vector.quantize_mx(w_codes(d0, d1), w_scales[:, d0:d1], interleaved)
 
-        def quantize_dz(half):
-            e0, e1 = half * N_PASS, (half + 1) * N_PASS
+        def quantize_dz(c0, c1):
+            first = c0 % N_PASS
             nc.vector.quantize_mx(
-                dz_codes[half][:].bitcast(E5M2), dz_scales[:, e0:e1], dz16[:, e0 * PLANES : e1 * PLANES]
+                dz_codes[c0 // N_PASS][:, first : first + c1 - c0].bitcast(E5M2),
+                dz_scales[:, c0:c1],
+                dz16[:, c0 * PLANES : c1 * PLANES],
             )
 
         def multiply(i, half):
@@ -254,12 +255,16 @@ def tile_attend_gmp_tnh_kernel(tc, dyT, hE, wm, offs, offs2, out):
                 start=True,
                 stop=True,
             )
-            nc.scalar.activation(dm[i][:, edges], bank[:], COPY, scale=-1.0)
+            first, second = (e0 // CHUNK for e0 in PASS_CHUNKS[half])
+            chunks = dm[i][:, 0:E].rearrange("p (c e) -> p c e", e=CHUNK)[:, first : second + 1 : second - first, :]
+            nc.scalar.activation(chunks, bank[:].rearrange("p (c e) -> p c e", e=CHUNK), COPY, scale=-1.0)
 
         quantize_w(0, P, w16_first[:])
-        for half in range(E // N_PASS):
-            quantize_dz(half)
-            multiply(0, half)
+        quantize_dz(0, N_PASS)
+        multiply(0, 0)
+        quantize_dz(N_PASS, N_PASS + CHUNK)
+        quantize_dz(N_PASS + CHUNK, E)
+        multiply(0, 1)
 
         w16_rest = shared.tile([P, (D - P) * PLANES], BF16, name="w16_rest", align_bytes=64, offset=dz16_at)
         nc.vector.tensor_copy(interleaved_runs(w16_rest[:], PLANES), row_runs(w_rest[:]))

@@ -33,13 +33,12 @@ LAST = SPLIT + P
 CHUNKS = range(0, SPLIT, CHUNK)
 PRODUCTS = [(t0, e0) for t0 in (0, PAIR) for e0 in CHUNKS]
 TURNS = [SPLIT, LAST]
-PASS_CHUNKS = [(0, SPLIT), (CHUNK, 2 * CHUNK)]
 
 DY_PAD = 176
 DM_PAD = 352
 REACH = 64
 
-LAST_CUTS = [(0, 448), (448, 384), (832, 192)]
+LAST_CUTS = [(0, 512), (512, 384), (896, 128)]
 
 
 def tile_attend_gmp_tnh_kernel(tc, dyT, hE, wm, offs, offs2, out):
@@ -62,7 +61,8 @@ def tile_attend_gmp_tnh_kernel(tc, dyT, hE, wm, offs, offs2, out):
         late = 4 * (P + 2 * N_PASS)
         h[0, SPLIT] = shared.tile([P, PAIR, CHUNK], F32, name="h_last", align_bytes=64, offset=late)
         w_first = keep.tile([P, PLANES, P], F32, name="w_first")
-        w_rest = keep.tile([P, PLANES, D - P], F32, name="w_rest")
+        w_second = keep.tile([P, PLANES, P], F32, name="w_second")
+        w_rest = keep.tile([P, PLANES, D - 2 * P], F32, name="w_rest")
 
         def load_dy(t):
             nc.sync.dma_start(dy[:, dy_at[t] : dy_at[t] + V], dy_rows[:, t, :])
@@ -85,18 +85,15 @@ def tile_attend_gmp_tnh_kernel(tc, dyT, hE, wm, offs, offs2, out):
         load_h(0, SPLIT)
         nc.sync.dma_start(w_first[:], w_rows[:, :, 0:P])
         nc.sync.dma_start(src[:], offs2)
-        nc.sync.dma_start(w_rest[:], w_rows[:, :, P:D])
+        nc.sync.dma_start(w_second[:], w_rows[:, :, P : 2 * P])
+        nc.sync.dma_start(w_rest[:], w_rows[:, :, 2 * P : D])
 
         gathered = [keep.tile([P, PLANES, N_PASS], F32, name=f"gathered{half}") for half in range(E // N_PASS)]
 
         def gathered_part(t0, t1, e0, e1):
             return gathered[e0 // N_PASS][:, t0:t1, e0 % N_PASS : e0 % N_PASS + e1 - e0]
 
-        def place(e):
-            first = e - e % CHUNK
-            return [e0 for chunks in PASS_CHUNKS for e0 in chunks].index(first) * CHUNK + e - first
-
-        pairs = {e0: keep.tile([P, PLANES // PAIR, CHUNK * PAIR], BF16, name=f"pairs{e0}") for e0 in CHUNKS}
+        pairs = {e0: keep.tile([P, PLANES // PAIR, CHUNK * PAIR], BF16, name=f"pairs{e0}", align_bytes=64) for e0 in CHUNKS}
         dz_scales = keep.tile([P, E], U8, name="dz_scales", align_bytes=64)
         w_scales = keep.tile([P, D], U8, name="w_scales", align_bytes=64)
         dm = [
@@ -149,7 +146,7 @@ def tile_attend_gmp_tnh_kernel(tc, dyT, hE, wm, offs, offs2, out):
             )
 
         def dz_part(e0, e1):
-            return dz16[:, place(e0) * PLANES : (place(e0) + e1 - e0) * PLANES]
+            return dz16[:, e0 * PLANES : e1 * PLANES]
 
         def weave_pairs(e0):
             words = dz_part(e0, e0 + CHUNK).bitcast(U32)
@@ -220,6 +217,9 @@ def tile_attend_gmp_tnh_kernel(tc, dyT, hE, wm, offs, offs2, out):
         for e0 in CHUNKS:
             weave_pairs(e0)
 
+        w16_second = keep.tile([P, P * PLANES], BF16, name="w16_second", tag=f"pairs{CHUNKS[-1]}", align_bytes=64)
+        nc.scalar.copy(interleaved_runs(w16_second[:], PLANES), row_runs(w_second[:]))
+
         for j, e0 in enumerate(TURNS):
             nc.vector.tensor_tensor(
                 interleaved_runs(dz_part(e0, e0 + P), PLANES),
@@ -235,13 +235,9 @@ def tile_attend_gmp_tnh_kernel(tc, dyT, hE, wm, offs, offs2, out):
         def quantize_w(d0, d1, interleaved):
             nc.vector.quantize_mx(w_codes(d0, d1), w_scales[:, d0:d1], interleaved)
 
-        def quantize_dz(c0, c1):
-            first = c0 % N_PASS
-            nc.vector.quantize_mx(
-                dz_codes[c0 // N_PASS][:, first : first + c1 - c0].bitcast(E5M2),
-                dz_scales[:, c0:c1],
-                dz16[:, c0 * PLANES : c1 * PLANES],
-            )
+        def quantize_dz(half):
+            e0, e1 = half * N_PASS, (half + 1) * N_PASS
+            nc.vector.quantize_mx(dz_codes[half][:].bitcast(E5M2), dz_scales[:, e0:e1], dz_part(e0, e1))
 
         def multiply(i, half):
             edges = slice(half * N_PASS, (half + 1) * N_PASS)
@@ -255,21 +251,17 @@ def tile_attend_gmp_tnh_kernel(tc, dyT, hE, wm, offs, offs2, out):
                 start=True,
                 stop=True,
             )
-            first, second = (e0 // CHUNK for e0 in PASS_CHUNKS[half])
-            chunks = dm[i][:, 0:E].rearrange("p (c e) -> p c e", e=CHUNK)[:, first : second + 1 : second - first, :]
-            nc.scalar.activation(chunks, bank[:].rearrange("p (c e) -> p c e", e=CHUNK), COPY, scale=-1.0)
+            nc.scalar.activation(dm[i][:, edges], bank[:], COPY, scale=-1.0)
 
         quantize_w(0, P, w16_first[:])
-        quantize_dz(0, N_PASS)
-        multiply(0, 0)
-        quantize_dz(N_PASS, N_PASS + CHUNK)
-        quantize_dz(N_PASS + CHUNK, E)
-        multiply(0, 1)
+        for half in range(E // N_PASS):
+            quantize_dz(half)
+            multiply(0, half)
 
-        w16_rest = shared.tile([P, (D - P) * PLANES], BF16, name="w16_rest", align_bytes=64, offset=dz16_at)
+        quantize_w(P, 2 * P, w16_second[:])
+        w16_rest = shared.tile([P, (D - 2 * P) * PLANES], BF16, name="w16_rest", align_bytes=64, offset=dz16_at)
         nc.vector.tensor_copy(interleaved_runs(w16_rest[:], PLANES), row_runs(w_rest[:]))
-        quantize_w(P, 2 * P, w16_rest[:, 0 : P * PLANES])
-        quantize_w(2 * P, D, w16_rest[:, P * PLANES :])
+        quantize_w(2 * P, D, w16_rest[:])
         for i in range(1, DM_TILES):
             for half in range(E // N_PASS):
                 multiply(i, half)

@@ -26,19 +26,26 @@ STRIPE = 16
 RUN = 4
 CHUNK = 256
 DM_TILES = D // P
-HALF = E // 2
+HALF = N_PASS
 
 SPLIT = E - CHUNK
-LAST = SPLIT + P
 CHUNKS = range(0, SPLIT, CHUNK)
-PRODUCTS = [(t0, e0) for t0 in (0, PAIR) for e0 in CHUNKS]
-TURNS = [SPLIT, LAST]
+PRODUCTS = [(t0, e0) for t0 in range(0, PLANES, PAIR) for e0 in CHUNKS]
+LAST = SPLIT + P
+OWN = [SPLIT, LAST]
 
 DY_PAD = 176
 DM_PAD = 352
 REACH = 64
 
 LAST_CUTS = [(0, 512), (512, 384), (896, 128)]
+
+CODES_FIRST_AT = 0
+W_CODES_AT = CODES_FIRST_AT + 4 * N_PASS
+SQUARES_AT = W_CODES_AT - 2 * N_PASS
+H_LAST_AT = W_CODES_AT + 4 * (P + N_PASS)
+DZ_FIRST_AT = H_LAST_AT + 2 * PLANES * P
+DZ_SECOND_AT = DZ_FIRST_AT + 2 * PLANES * N_PASS
 
 
 def tile_attend_gmp_tnh_kernel(tc, dyT, hE, wm, offs, offs2, out):
@@ -57,9 +64,11 @@ def tile_attend_gmp_tnh_kernel(tc, dyT, hE, wm, offs, offs2, out):
         dy_at = {2: 0, 0: V, 1: 2 * V + DY_PAD, 3: 3 * V + DY_PAD}
         dy_end = PLANES * V + 2 * DY_PAD
         dy = keep.tile([P, dy_end], F32, name="dy")
-        h = {key: keep.tile([P, PAIR, CHUNK], F32, name=f"h{key[0]}_{key[1]}") for key in PRODUCTS + [(PAIR, SPLIT)]}
-        late = 4 * (P + 2 * N_PASS)
-        h[0, SPLIT] = shared.tile([P, PAIR, CHUNK], F32, name="h_last", align_bytes=64, offset=late)
+        h = {
+            (t0, e0): keep.tile([P, PAIR, CHUNK], F32, name=f"h{t0}_{e0}")
+            for t0, e0 in PRODUCTS + [(PAIR, SPLIT)]
+        }
+        h[0, SPLIT] = shared.tile([P, PAIR, CHUNK], F32, name="h_last", align_bytes=64, offset=H_LAST_AT)
         w_first = keep.tile([P, PLANES, P], F32, name="w_first")
         w_second = keep.tile([P, PLANES, P], F32, name="w_second")
         w_rest = keep.tile([P, PLANES, D - 2 * P], F32, name="w_rest")
@@ -72,15 +81,13 @@ def tile_attend_gmp_tnh_kernel(tc, dyT, hE, wm, offs, offs2, out):
 
         load_dy(0)
         nc.sync.dma_start(dst[:], offs)
-        load_h(0, 0)
-        load_dy(1)
-        load_h(0, CHUNK)
-        load_h(0, 2 * CHUNK)
-        load_dy(2)
-        load_h(PAIR, 0)
-        load_dy(3)
-        load_h(PAIR, CHUNK)
-        load_h(PAIR, 2 * CHUNK)
+        for t0 in range(0, PLANES, PAIR):
+            if t0 > 0:
+                load_dy(t0)
+            load_h(t0, CHUNKS[0])
+            load_dy(t0 + 1)
+            for e0 in CHUNKS[1:]:
+                load_h(t0, e0)
         load_h(PAIR, SPLIT)
         load_h(0, SPLIT)
         nc.sync.dma_start(w_first[:], w_rows[:, :, 0:P])
@@ -93,7 +100,9 @@ def tile_attend_gmp_tnh_kernel(tc, dyT, hE, wm, offs, offs2, out):
         def gathered_part(t0, t1, e0, e1):
             return gathered[e0 // N_PASS][:, t0:t1, e0 % N_PASS : e0 % N_PASS + e1 - e0]
 
-        pairs = {e0: keep.tile([P, PLANES // PAIR, CHUNK * PAIR], BF16, name=f"pairs{e0}", align_bytes=64) for e0 in CHUNKS}
+        pairs = {
+            e0: keep.tile([P, PLANES // PAIR, CHUNK * PAIR], BF16, name=f"pairs{e0}", align_bytes=64) for e0 in CHUNKS
+        }
         dz_scales = keep.tile([P, E], U8, name="dz_scales", align_bytes=64)
         w_scales = keep.tile([P, D], U8, name="w_scales", align_bytes=64)
         dm = [
@@ -111,7 +120,7 @@ def tile_attend_gmp_tnh_kernel(tc, dyT, hE, wm, offs, offs2, out):
         nc.gpsimd.memset(minus_one[:], -1.0)
         blocks = range(0, N_PASS, P)
         factor_banks = [
-            psum.tile([P, N_PASS], F32, name=f"factor{j}", tag=f"bank{4 + j}") for j in range(len(TURNS))
+            psum.tile([P, N_PASS], F32, name=f"factor{j}", tag=f"bank{4 + j}") for j in range(len(OWN))
         ]
         for bank in factor_banks:
             for c0 in blocks:
@@ -146,7 +155,7 @@ def tile_attend_gmp_tnh_kernel(tc, dyT, hE, wm, offs, offs2, out):
             )
 
         def dz_part(e0, e1):
-            return dz16[:, e0 * PLANES : e1 * PLANES]
+            return dz16[e0 // N_PASS][:, e0 % N_PASS * PLANES : (e0 % N_PASS + e1 - e0) * PLANES]
 
         def weave_pairs(e0):
             words = dz_part(e0, e0 + CHUNK).bitcast(U32)
@@ -191,36 +200,35 @@ def tile_attend_gmp_tnh_kernel(tc, dyT, hE, wm, offs, offs2, out):
             multiply_pair(*product)
 
         first_squares = keep.tile([P, N_PASS], F32, name="first_squares")
-        last_squares = shared.tile([P, N_PASS], F32, name="last_squares", align_bytes=64, offset=2 * N_PASS)
+        last_squares = shared.tile([P, N_PASS], F32, name="last_squares", align_bytes=64, offset=SQUARES_AT)
         turned = turn(PAIR)
         nc.scalar.activation(first_squares[:], turned[:], SQUARE)
         turned = turn(0)
-        for j in range(len(TURNS)):
+        for j in range(len(OWN)):
             turn_back(first_squares, PAIR, j)
-        for j in range(len(TURNS)):
+        for j in range(len(OWN)):
             columns = slice(j * PAIR * P, (j + 1) * PAIR * P)
             nc.scalar.activation(last_squares[:, columns], turned[:, columns], SQUARE)
             turn_back(last_squares, 0, j)
 
-        w_codes_first = shared.tile([P, P], U32, name="w_codes_first", align_bytes=64, offset=4 * N_PASS)
+        w_codes_first = shared.tile([P, P], U32, name="w_codes_first", align_bytes=64, offset=W_CODES_AT)
         w_codes_rest = keep.tile([P, D - P], U32, name="w_codes_rest", align_bytes=64)
         dz_codes = [
-            shared.tile([P, N_PASS], U32, name="dz_codes0", align_bytes=64, offset=0),
-            shared.tile([P, N_PASS], U32, name="dz_codes1", align_bytes=64, offset=4 * (N_PASS + P)),
+            shared.tile([P, N_PASS], U32, name=f"dz_codes{half}", align_bytes=64, offset=at)
+            for half, at in enumerate((CODES_FIRST_AT, DZ_FIRST_AT))
         ]
 
-        w16_first = shared.tile([P, P * PLANES], BF16, name="w16_first", align_bytes=64, offset=late)
-        dz16_at = late + 2 * P * PLANES
-        dz16 = shared.tile([P, E * PLANES], BF16, name="dz16", align_bytes=64, offset=dz16_at)
-        nc.scalar.copy(interleaved_runs(w16_first[:], PLANES), row_runs(w_first[:]))
-
-        for e0 in CHUNKS:
+        dz16 = [
+            shared.tile([P, N_PASS * PLANES], BF16, name=f"dz16_{half}", align_bytes=64, offset=at)
+            for half, at in enumerate((DZ_FIRST_AT, DZ_SECOND_AT))
+        ]
+        w16_first = shared.tile([P, P * PLANES], BF16, name="w16_first", align_bytes=64, offset=H_LAST_AT)
+        for e0 in CHUNKS[:-1]:
             weave_pairs(e0)
+        nc.scalar.copy(interleaved_runs(w16_first[:], PLANES), row_runs(w_first[:]))
+        weave_pairs(CHUNKS[-1])
 
-        w16_second = keep.tile([P, P * PLANES], BF16, name="w16_second", tag=f"pairs{CHUNKS[-1]}", align_bytes=64)
-        nc.scalar.copy(interleaved_runs(w16_second[:], PLANES), row_runs(w_second[:]))
-
-        for j, e0 in enumerate(TURNS):
+        for j, e0 in enumerate(OWN):
             nc.vector.tensor_tensor(
                 interleaved_runs(dz_part(e0, e0 + P), PLANES),
                 row_runs(gathered_part(0, PLANES, e0, e0 + P)),
@@ -235,9 +243,9 @@ def tile_attend_gmp_tnh_kernel(tc, dyT, hE, wm, offs, offs2, out):
         def quantize_w(d0, d1, interleaved):
             nc.vector.quantize_mx(w_codes(d0, d1), w_scales[:, d0:d1], interleaved)
 
-        def quantize_dz(half):
-            e0, e1 = half * N_PASS, (half + 1) * N_PASS
-            nc.vector.quantize_mx(dz_codes[half][:].bitcast(E5M2), dz_scales[:, e0:e1], dz_part(e0, e1))
+        def quantize_dz(e0, e1):
+            codes = dz_codes[e0 // N_PASS][:, e0 % N_PASS : e0 % N_PASS + e1 - e0]
+            nc.vector.quantize_mx(codes.bitcast(E5M2), dz_scales[:, e0:e1], dz_part(e0, e1))
 
         def multiply(i, half):
             edges = slice(half * N_PASS, (half + 1) * N_PASS)
@@ -253,14 +261,20 @@ def tile_attend_gmp_tnh_kernel(tc, dyT, hE, wm, offs, offs2, out):
             )
             nc.scalar.activation(dm[i][:, edges], bank[:], COPY, scale=-1.0)
 
+        quantize_dz(0, HALF)
         quantize_w(0, P, w16_first[:])
-        for half in range(E // N_PASS):
-            quantize_dz(half)
-            multiply(0, half)
+        multiply(0, 0)
+        quantize_dz(SPLIT, E)
+        quantize_dz(HALF, SPLIT)
+        multiply(0, 1)
 
-        quantize_w(P, 2 * P, w16_second[:])
-        w16_rest = shared.tile([P, (D - 2 * P) * PLANES], BF16, name="w16_rest", align_bytes=64, offset=dz16_at)
+        w16_second = shared.tile([P, P * PLANES], BF16, name="w16_second", align_bytes=64, offset=DZ_SECOND_AT)
+        w16_rest = shared.tile(
+            [P, (D - 2 * P) * PLANES], BF16, name="w16_rest", align_bytes=64, offset=DZ_SECOND_AT + 2 * PLANES * P
+        )
+        nc.vector.tensor_copy(interleaved_runs(w16_second[:], PLANES), row_runs(w_second[:]))
         nc.vector.tensor_copy(interleaved_runs(w16_rest[:], PLANES), row_runs(w_rest[:]))
+        quantize_w(P, 2 * P, w16_second[:])
         quantize_w(2 * P, D, w16_rest[:])
         for i in range(1, DM_TILES):
             for half in range(E // N_PASS):
@@ -271,7 +285,7 @@ def tile_attend_gmp_tnh_kernel(tc, dyT, hE, wm, offs, offs2, out):
             total = keep.tile([P, V], F32, name=f"total{i}")
             for c0, n in LAST_CUTS if last else [(0, E)]:
                 if i == 0:
-                    picked = shared.tile([P, n], F32, name="picked0", align_bytes=64, offset=dz16_at)
+                    picked = shared.tile([P, n], F32, name="picked0", align_bytes=64, offset=DZ_SECOND_AT)
                 else:
                     picked = keep.tile([P, n], F32, name=f"picked{i}_{c0}")
                 nc.vector.tensor_copy(picked[:], dm[i][:].indirect(src[:, c0 // STRIPE : (c0 + n) // STRIPE]))

@@ -42,10 +42,12 @@ LAST_CUTS = [(0, 512), (512, 384), (896, 128)]
 
 CODES_FIRST_AT = 0
 W_CODES_AT = CODES_FIRST_AT + 4 * N_PASS
+CODES_SECOND_AT = W_CODES_AT + 4 * P
 SQUARES_AT = W_CODES_AT - 2 * N_PASS
-H_LAST_AT = W_CODES_AT + 4 * (P + N_PASS)
-DZ_FIRST_AT = H_LAST_AT + 2 * PLANES * P
-DZ_SECOND_AT = DZ_FIRST_AT + 2 * PLANES * N_PASS
+W16_FIRST_AT = CODES_SECOND_AT + 4 * N_PASS
+W16_SECOND_AT = W16_FIRST_AT + 2 * PLANES * P
+DZ_FIRST_AT = W16_SECOND_AT + 2 * PLANES * P
+H_LAST_AT = W16_SECOND_AT - 2 * PLANES * P // 2
 
 
 def tile_attend_gmp_tnh_kernel(tc, dyT, hE, wm, offs, offs2, out):
@@ -215,18 +217,20 @@ def tile_attend_gmp_tnh_kernel(tc, dyT, hE, wm, offs, offs2, out):
         w_codes_rest = keep.tile([P, D - P], U32, name="w_codes_rest", align_bytes=64)
         dz_codes = [
             shared.tile([P, N_PASS], U32, name=f"dz_codes{half}", align_bytes=64, offset=at)
-            for half, at in enumerate((CODES_FIRST_AT, DZ_FIRST_AT))
+            for half, at in enumerate((CODES_FIRST_AT, CODES_SECOND_AT))
         ]
 
         dz16 = [
-            shared.tile([P, N_PASS * PLANES], BF16, name=f"dz16_{half}", align_bytes=64, offset=at)
-            for half, at in enumerate((DZ_FIRST_AT, DZ_SECOND_AT))
+            shared.tile([P, N_PASS * PLANES], BF16, name="dz16_0", align_bytes=64, offset=DZ_FIRST_AT),
+            keep.tile([P, N_PASS * PLANES], BF16, name="dz16_1", align_bytes=64),
         ]
-        w16_first = shared.tile([P, P * PLANES], BF16, name="w16_first", align_bytes=64, offset=H_LAST_AT)
+        w16_first = shared.tile([P, P * PLANES], BF16, name="w16_first", align_bytes=64, offset=W16_FIRST_AT)
+        w16_second = shared.tile([P, P * PLANES], BF16, name="w16_second", align_bytes=64, offset=W16_SECOND_AT)
         for e0 in CHUNKS[:-1]:
             weave_pairs(e0)
         nc.scalar.copy(interleaved_runs(w16_first[:], PLANES), row_runs(w_first[:]))
         weave_pairs(CHUNKS[-1])
+        nc.scalar.copy(interleaved_runs(w16_second[:], PLANES), row_runs(w_second[:]))
 
         for j, e0 in enumerate(OWN):
             nc.vector.tensor_tensor(
@@ -268,11 +272,7 @@ def tile_attend_gmp_tnh_kernel(tc, dyT, hE, wm, offs, offs2, out):
         quantize_dz(HALF, SPLIT)
         multiply(0, 1)
 
-        w16_second = shared.tile([P, P * PLANES], BF16, name="w16_second", align_bytes=64, offset=DZ_SECOND_AT)
-        w16_rest = shared.tile(
-            [P, (D - 2 * P) * PLANES], BF16, name="w16_rest", align_bytes=64, offset=DZ_SECOND_AT + 2 * PLANES * P
-        )
-        nc.vector.tensor_copy(interleaved_runs(w16_second[:], PLANES), row_runs(w_second[:]))
+        w16_rest = shared.tile([P, (D - 2 * P) * PLANES], BF16, name="w16_rest", align_bytes=64, offset=DZ_FIRST_AT)
         nc.vector.tensor_copy(interleaved_runs(w16_rest[:], PLANES), row_runs(w_rest[:]))
         quantize_w(P, 2 * P, w16_second[:])
         quantize_w(2 * P, D, w16_rest[:])
@@ -284,10 +284,7 @@ def tile_attend_gmp_tnh_kernel(tc, dyT, hE, wm, offs, offs2, out):
             last = i == DM_TILES - 1
             total = keep.tile([P, V], F32, name=f"total{i}")
             for c0, n in LAST_CUTS if last else [(0, E)]:
-                if i == 0:
-                    picked = shared.tile([P, n], F32, name="picked0", align_bytes=64, offset=DZ_SECOND_AT)
-                else:
-                    picked = keep.tile([P, n], F32, name=f"picked{i}_{c0}")
+                picked = keep.tile([P, n], F32, name=f"picked{i}_{c0}")
                 nc.vector.tensor_copy(picked[:], dm[i][:].indirect(src[:, c0 // STRIPE : (c0 + n) // STRIPE]))
                 nodes = slice(c0 // K, (c0 + n) // K)
                 adder = nc.vector if c0 > 0 else nc.gpsimd

@@ -1,7 +1,6 @@
 from contextlib import ExitStack
 
 import concourse.mybir as mybir
-from concourse.masks import make_identity
 
 V, K, E, D, DV = 512, 2, 1024, 512, 512
 FLOPS = 2 * DV * D * E
@@ -16,38 +15,18 @@ E5M2 = mybir.dt.float8_e5m2_x4
 MULT = mybir.AluOpType.mult
 ADD = mybir.AluOpType.add
 COPY = mybir.ActivationFunctionType.Copy
+IDENTITY = mybir.ActivationFunctionType.Identity
 SQUARE = mybir.ActivationFunctionType.Square
 
 P = 128
 PLANES = 4
-PAIR = 2
 N_PASS = 512
 STRIPE = 16
 RUN = 4
 CHUNK = 256
 DM_TILES = D // P
 HALF = N_PASS
-
-SPLIT = E - CHUNK
-CHUNKS = range(0, SPLIT, CHUNK)
-PRODUCTS = [(t0, e0) for t0 in range(0, PLANES, PAIR) for e0 in CHUNKS]
-LAST = SPLIT + P
-OWN = [SPLIT, LAST]
-
-DY_PAD = 176
-DM_PAD = 352
-REACH = 64
-
-LAST_CUTS = [(0, 512), (512, 384), (896, 128)]
-
-CODES_FIRST_AT = 0
-W_CODES_AT = CODES_FIRST_AT + 4 * N_PASS
-CODES_SECOND_AT = W_CODES_AT + 4 * P
-SQUARES_AT = W_CODES_AT - 2 * N_PASS
-W16_FIRST_AT = CODES_SECOND_AT + 4 * N_PASS
-W16_SECOND_AT = W16_FIRST_AT + 2 * PLANES * P
-DZ_FIRST_AT = W16_SECOND_AT + 2 * PLANES * P
-H_LAST_AT = W16_SECOND_AT - 2 * PLANES * P // 2
+DY_PAD = 16
 
 
 def tile_attend_gmp_tnh_kernel(tc, dyT, hE, wm, offs, offs2, out):
@@ -58,235 +37,164 @@ def tile_attend_gmp_tnh_kernel(tc, dyT, hE, wm, offs, offs2, out):
 
     with ExitStack() as ctx:
         keep = ctx.enter_context(tc.tile_pool(name="keep", bufs=1))
-        shared = ctx.enter_context(tc.tile_pool(name="shared", bufs=1))
         psum = ctx.enter_context(tc.psum_pool(name="psum", bufs=1))
 
         dst = keep.tile([P, E // STRIPE], U16, name="dst")
         src = keep.tile([P, E // STRIPE], U16, name="src")
-        dy_at = {2: 0, 0: V, 1: 2 * V + DY_PAD, 3: 3 * V + DY_PAD}
-        dy_end = PLANES * V + 2 * DY_PAD
-        dy = keep.tile([P, dy_end], F32, name="dy")
-        h = {
-            (t0, e0): keep.tile([P, PAIR, CHUNK], F32, name=f"h{t0}_{e0}")
-            for t0, e0 in PRODUCTS + [(PAIR, SPLIT)]
-        }
-        h[0, SPLIT] = shared.tile([P, PAIR, CHUNK], F32, name="h_last", align_bytes=64, offset=H_LAST_AT)
-        w_first = keep.tile([P, PLANES, P], F32, name="w_first")
-        w_second = keep.tile([P, PLANES, P], F32, name="w_second")
-        w_rest = keep.tile([P, PLANES, D - 2 * P], F32, name="w_rest")
+        dy = [keep.tile([P, V + DY_PAD], F32, name=f"dy{t}") for t in range(PLANES)]
+        h = [keep.tile([P, PLANES, CHUNK], F32, name=f"h{c}") for c in range(E // CHUNK)]
+        w = [keep.tile([P, PLANES, 2 * P], F32, name=f"w{j}") for j in range(2)]
 
         def load_dy(t):
-            nc.sync.dma_start(dy[:, dy_at[t] : dy_at[t] + V], dy_rows[:, t, :])
+            nc.sync.dma_start(dy[t][:, 0:V], dy_rows[:, t, :])
 
-        def load_h(t0, e0):
-            nc.sync.dma_start(h[t0, e0][:], h_rows[:, t0 : t0 + PAIR, e0 : e0 + CHUNK])
+        def load_h(c):
+            nc.sync.dma_start(h[c][:], h_rows[:, :, c * CHUNK : (c + 1) * CHUNK])
 
         load_dy(0)
         nc.sync.dma_start(dst[:], offs)
-        for t0 in range(0, PLANES, PAIR):
-            if t0 > 0:
-                load_dy(t0)
-            load_h(t0, CHUNKS[0])
-            load_dy(t0 + 1)
-            for e0 in CHUNKS[1:]:
-                load_h(t0, e0)
-        load_h(PAIR, SPLIT)
-        load_h(0, SPLIT)
-        nc.sync.dma_start(w_first[:], w_rows[:, :, 0:P])
+        nc.sync.dma_start(h[0][:, 0:2, :], h_rows[:, 0:2, 0:CHUNK])
+        load_dy(1)
+        load_dy(2)
+        nc.sync.dma_start(h[0][:, 2:4, :], h_rows[:, 2:4, 0:CHUNK])
+        load_dy(3)
+        load_h(1)
+        nc.sync.dma_start(w[0][:], w_rows[:, :, 0 : 2 * P])
+        load_h(2)
+        load_h(3)
         nc.sync.dma_start(src[:], offs2)
-        nc.sync.dma_start(w_second[:], w_rows[:, :, P : 2 * P])
-        nc.sync.dma_start(w_rest[:], w_rows[:, :, 2 * P : D])
+        nc.sync.dma_start(w[1][:], w_rows[:, :, 2 * P : D])
 
-        gathered = [keep.tile([P, PLANES, N_PASS], F32, name=f"gathered{half}") for half in range(E // N_PASS)]
+        zero = keep.tile([P, 1], F32, name="zero")
+        one = keep.tile([P, 1], F32, name="one")
+        nc.gpsimd.memset(zero[:], 0.0)
+        nc.scalar.activation(one[:], zero[:], COPY, bias=1.0)
+        for t in range(PLANES):
+            nc.gpsimd.memset(dy[t][:, V:], 0.0)
 
-        def gathered_part(t0, t1, e0, e1):
-            return gathered[e0 // N_PASS][:, t0:t1, e0 % N_PASS : e0 % N_PASS + e1 - e0]
+        gathered = [keep.tile([P, PLANES, HALF], F32, name=f"gathered{half}") for half in range(2)]
+        dz16 = [keep.tile([P, CHUNK * PLANES], BF16, name=f"dz16_{c}", align_bytes=64) for c in range(E // CHUNK)]
+        dz_codes = [keep.tile([P, N_PASS], U32, name=f"dz_codes{half}", align_bytes=64) for half in range(2)]
+        dz_scales = [keep.tile([P, N_PASS], U8, name=f"dz_scales{half}", align_bytes=64) for half in range(2)]
+        w16 = [keep.tile([P, 2 * P * PLANES], BF16, name=f"w16_{j}", align_bytes=64) for j in range(2)]
+        w_codes = [keep.tile([P, 2 * P], U32, name=f"w_codes{j}", align_bytes=64) for j in range(2)]
+        w_scales = [keep.tile([P, 2 * P], U8, name=f"w_scales{j}", align_bytes=64) for j in range(2)]
+        dm = [keep.tile([P, E], F32, name=f"dm{i}") for i in range(DM_TILES)]
 
-        pairs = {
-            e0: keep.tile([P, PLANES // PAIR, CHUNK * PAIR], BF16, name=f"pairs{e0}", align_bytes=64) for e0 in CHUNKS
-        }
-        dz_scales = keep.tile([P, E], U8, name="dz_scales", align_bytes=64)
-        w_scales = keep.tile([P, D], U8, name="w_scales", align_bytes=64)
-        dm = [
-            keep.tile([P, E + DM_PAD if i < DM_TILES - 1 else E], F32, name=f"dm{i}")
-            for i in range(DM_TILES)
-        ]
-        for t in (0, 3):
-            nc.vector.memset(dy[:, dy_at[t] + V : dy_at[t] + V + DY_PAD], 0.0)
-        for i in range(DM_TILES - 1):
-            nc.gpsimd.memset(dm[i][:, E:], 0.0)
+        def gather(on_scalar, dest, window, entries):
+            if on_scalar:
+                nc.scalar.activation(dest, window.indirect(entries), COPY)
+            else:
+                nc.vector.tensor_copy(dest, window.indirect(entries))
 
-        identity = keep.tile([P, P], F32, name="identity")
-        make_identity(nc, identity[:])
-        minus_one = keep.tile([P, P], F32, name="minus_one")
-        nc.gpsimd.memset(minus_one[:], -1.0)
-        blocks = range(0, N_PASS, P)
-        factor_banks = [
-            psum.tile([P, N_PASS], F32, name=f"factor{j}", tag=f"bank{4 + j}") for j in range(len(OWN))
-        ]
-        for bank in factor_banks:
-            for c0 in blocks:
-                nc.tensor.matmul(
-                    bank[:, c0 : c0 + P], minus_one[:], identity[:], start=c0 == 0, stop=False, is_transpose=True
-                )
-
-        def gather_dy(t, e0, e1, window_end):
-            nc.vector.tensor_copy(
-                gathered_part(t, t + 1, e0, e1)[:, 0, :],
-                dy[:, dy_at[t] : window_end].indirect(dst[:, e0 // STRIPE : e1 // STRIPE]),
-            )
+        def gather_dy(on_scalar, t, e0, e1):
+            dest = gathered[e0 // HALF][:, t, e0 % HALF : e0 % HALF + e1 - e0]
+            gather(on_scalar, dest, dy[t][:], dst[:, e0 // STRIPE : e1 // STRIPE])
 
         def row_runs(rows):
             return rows.rearrange("p t (c i) -> p c t i", i=RUN)
 
-        def interleaved_runs(interleaved, rows):
-            return interleaved.rearrange("p (c i t) -> p c t i", i=RUN, t=rows)
+        def interleaved_runs(interleaved):
+            return interleaved.rearrange("p (c i t) -> p c t i", i=RUN, t=PLANES)
 
-        def make_factor(parts):
-            for part in parts:
-                nc.scalar.activation(part, part, SQUARE)
-            for part in parts:
-                nc.scalar.activation(part, part, COPY, bias=-1.0)
+        def flat(c):
+            return h[c][:].rearrange("p t e -> p (t e)")
 
-        def multiply_pair(t0, e0):
-            nc.gpsimd.tensor_tensor(
-                interleaved_runs(pairs[e0][:, t0 // PAIR, :], PAIR),
-                row_runs(gathered_part(t0, t0 + PAIR, e0, e0 + CHUNK)),
-                row_runs(h[t0, e0][:]),
-                MULT,
-            )
+        def square_scalar(c):
+            nc.scalar.activation(flat(c), flat(c), SQUARE)
 
-        def dz_part(e0, e1):
-            return dz16[e0 // N_PASS][:, e0 % N_PASS * PLANES : (e0 % N_PASS + e1 - e0) * PLANES]
+        def flip_scalar(c):
+            nc.scalar.activation(flat(c), flat(c), IDENTITY, bias=one[:], scale=-1.0)
 
-        def weave_pairs(e0):
-            words = dz_part(e0, e0 + CHUNK).bitcast(U32)
-            nc.scalar.copy(interleaved_runs(words, PLANES // PAIR), row_runs(pairs[e0][:].bitcast(U32)))
-
-        def turn(t0):
-            turned = psum.tile([P, N_PASS], F32, name=f"turned{t0}", tag=f"bank{6 + t0 // PAIR}")
-            for c0 in blocks:
-                j, t = divmod(c0 // P, PAIR)
-                nc.tensor.transpose(turned[:, c0 : c0 + P], h[t0, SPLIT][:, t, j * P : (j + 1) * P], identity[:])
-            return turned
-
-        def turn_back(squares, t0, j):
-            for t in range(PAIR):
-                c0 = (j * PAIR + t) * P
-                nc.tensor.matmul(
-                    factor_banks[j][:, (t0 + t) * P : (t0 + t + 1) * P],
-                    squares[:, c0 : c0 + P],
-                    identity[:],
-                    start=False,
-                    stop=t0 == 0 and t == PAIR - 1,
-                    is_transpose=True,
-                )
-
-        gather_dy(0, 0, HALF, dy_at[1])
-        gather_dy(0, HALF, HALF + P, dy_at[1])
-        gather_dy(1, 0, CHUNK, dy_at[3])
-        gather_dy(1, CHUNK, HALF, dy_at[3])
-        gather_dy(0, HALF + P, E, dy_at[1] + REACH)
-        gather_dy(1, HALF, SPLIT, dy_at[3])
-        gather_dy(2, 0, HALF, dy_at[1])
-        gather_dy(3, 0, CHUNK, dy_end)
-        gather_dy(3, CHUNK, HALF, dy_end)
-        gather_dy(2, HALF, E, dy_end)
-        gather_dy(3, HALF, LAST, dy_end)
-        gather_dy(1, SPLIT, E, dy_end)
-        gather_dy(3, LAST, E, dy_at[3] + V)
-
-        for product in PRODUCTS:
-            make_factor([h[product][:, t, :] for t in range(PAIR)])
-        for product in PRODUCTS:
-            multiply_pair(*product)
-
-        first_squares = keep.tile([P, N_PASS], F32, name="first_squares")
-        last_squares = shared.tile([P, N_PASS], F32, name="last_squares", align_bytes=64, offset=SQUARES_AT)
-        turned = turn(PAIR)
-        nc.scalar.activation(first_squares[:], turned[:], SQUARE)
-        turned = turn(0)
-        for j in range(len(OWN)):
-            turn_back(first_squares, PAIR, j)
-        for j in range(len(OWN)):
-            columns = slice(j * PAIR * P, (j + 1) * PAIR * P)
-            nc.scalar.activation(last_squares[:, columns], turned[:, columns], SQUARE)
-            turn_back(last_squares, 0, j)
-
-        w_codes_first = shared.tile([P, P], U32, name="w_codes_first", align_bytes=64, offset=W_CODES_AT)
-        w_codes_rest = keep.tile([P, D - P], U32, name="w_codes_rest", align_bytes=64)
-        dz_codes = [
-            shared.tile([P, N_PASS], U32, name=f"dz_codes{half}", align_bytes=64, offset=at)
-            for half, at in enumerate((CODES_FIRST_AT, CODES_SECOND_AT))
-        ]
-
-        dz16 = [
-            shared.tile([P, N_PASS * PLANES], BF16, name="dz16_0", align_bytes=64, offset=DZ_FIRST_AT),
-            keep.tile([P, N_PASS * PLANES], BF16, name="dz16_1", align_bytes=64),
-        ]
-        w16_first = shared.tile([P, P * PLANES], BF16, name="w16_first", align_bytes=64, offset=W16_FIRST_AT)
-        w16_second = shared.tile([P, P * PLANES], BF16, name="w16_second", align_bytes=64, offset=W16_SECOND_AT)
-        for e0 in CHUNKS[:-1]:
-            weave_pairs(e0)
-        nc.scalar.copy(interleaved_runs(w16_first[:], PLANES), row_runs(w_first[:]))
-        weave_pairs(CHUNKS[-1])
-        nc.scalar.copy(interleaved_runs(w16_second[:], PLANES), row_runs(w_second[:]))
-
-        for j, e0 in enumerate(OWN):
+        def product(c):
+            e0 = c * CHUNK % HALF
             nc.vector.tensor_tensor(
-                interleaved_runs(dz_part(e0, e0 + P), PLANES),
-                row_runs(gathered_part(0, PLANES, e0, e0 + P)),
-                row_runs(factor_banks[j][:].rearrange("p (t e) -> p t e", e=P)),
+                interleaved_runs(dz16[c][:]),
+                row_runs(gathered[c * CHUNK // HALF][:, :, e0 : e0 + CHUNK]),
+                row_runs(h[c][:]),
                 MULT,
             )
 
-        def w_codes(d0, d1):
-            words = w_codes_first[:] if d0 == 0 else w_codes_rest[:, d0 - P : d1 - P]
-            return words.bitcast(E4M3)
+        def quantize_dz(c):
+            half, e0 = divmod(c * CHUNK, HALF)
+            nc.vector.quantize_mx(
+                dz_codes[half][:, e0 : e0 + CHUNK].bitcast(E5M2), dz_scales[half][:, e0 : e0 + CHUNK], dz16[c][:]
+            )
 
-        def quantize_w(d0, d1, interleaved):
-            nc.vector.quantize_mx(w_codes(d0, d1), w_scales[:, d0:d1], interleaved)
+        def cast_w(j):
+            nc.vector.tensor_copy(interleaved_runs(w16[j][:]), row_runs(w[j][:]))
 
-        def quantize_dz(e0, e1):
-            codes = dz_codes[e0 // N_PASS][:, e0 % N_PASS : e0 % N_PASS + e1 - e0]
-            nc.vector.quantize_mx(codes.bitcast(E5M2), dz_scales[:, e0:e1], dz_part(e0, e1))
+        def quantize_w(j):
+            nc.vector.quantize_mx(w_codes[j][:].bitcast(E4M3), w_scales[j][:], w16[j][:])
 
         def multiply(i, half):
-            edges = slice(half * N_PASS, (half + 1) * N_PASS)
-            bank = psum.tile([P, N_PASS], F32, name=f"pass{i}_{half}", tag=f"bank{2 * i + half}")
+            j, d0 = divmod(i * P, 2 * P)
+            bank = psum.tile([P, N_PASS], F32, name=f"pass{i}_{half}")
             nc.tensor.matmul_mx(
                 bank[:],
-                lhsT=w_codes(i * P, (i + 1) * P),
-                lhsT_scale=w_scales[:, i * P : (i + 1) * P],
+                lhsT=w_codes[j][:, d0 : d0 + P].bitcast(E4M3),
+                lhsT_scale=w_scales[j][:, d0 : d0 + P],
                 rhs=dz_codes[half][:].bitcast(E5M2),
-                rhs_scale=dz_scales[:, edges],
+                rhs_scale=dz_scales[half][:],
                 start=True,
                 stop=True,
             )
-            nc.scalar.activation(dm[i][:, edges], bank[:], COPY, scale=-1.0)
+            nc.scalar.activation(dm[i][:, half * N_PASS : (half + 1) * N_PASS], bank[:], COPY)
 
-        quantize_dz(0, HALF)
-        quantize_w(0, P, w16_first[:])
+        for t0 in (0, 2):
+            part = h[0][:, t0 : t0 + 2, :].rearrange("p t e -> p (t e)")
+            nc.gpsimd.tensor_tensor(part, part, part, MULT)
+            nc.gpsimd.tensor_scalar(part, part, -1.0, 1.0, MULT, ADD)
+        for t in range(3):
+            gather_dy(False, t, 0, HALF)
+            gather_dy(True, t, HALF, E)
+        gather_dy(False, 3, 0, HALF)
+        gather_dy(True, 3, HALF + CHUNK, E)
+        gather_dy(False, 3, HALF, HALF + CHUNK)
+        square_scalar(1)
+        flip_scalar(1)
+        square_scalar(2)
+        flip_scalar(2)
+        square_scalar(3)
+        flip_scalar(3)
+
+        product(0)
+        quantize_dz(0)
+        product(1)
+        cast_w(0)
+        quantize_dz(1)
+        product(2)
+        quantize_w(0)
         multiply(0, 0)
-        quantize_dz(SPLIT, E)
-        quantize_dz(HALF, SPLIT)
+        multiply(1, 0)
+        quantize_dz(2)
+        product(3)
+        quantize_dz(3)
+        cast_w(1)
         multiply(0, 1)
+        multiply(1, 1)
+        quantize_w(1)
+        for i in range(2, DM_TILES):
+            multiply(i, 0)
+            multiply(i, 1)
 
-        w16_rest = shared.tile([P, (D - 2 * P) * PLANES], BF16, name="w16_rest", align_bytes=64, offset=DZ_FIRST_AT)
-        nc.vector.tensor_copy(interleaved_runs(w16_rest[:], PLANES), row_runs(w_rest[:]))
-        quantize_w(P, 2 * P, w16_second[:])
-        quantize_w(2 * P, D, w16_rest[:])
-        for i in range(1, DM_TILES):
-            for half in range(E // N_PASS):
-                multiply(i, half)
-
-        for i in range(DM_TILES):
-            last = i == DM_TILES - 1
-            total = keep.tile([P, V], F32, name=f"total{i}")
-            for c0, n in LAST_CUTS if last else [(0, E)]:
-                picked = keep.tile([P, n], F32, name=f"picked{i}_{c0}")
-                nc.vector.tensor_copy(picked[:], dm[i][:].indirect(src[:, c0 // STRIPE : (c0 + n) // STRIPE]))
-                nodes = slice(c0 // K, (c0 + n) // K)
-                adder = nc.vector if c0 > 0 else nc.gpsimd
-                adder.tensor_tensor(total[:, nodes], picked[:, 0:n:K], picked[:, 1:n:K], ADD)
-                nc.sync.dma_start(out[i * P : (i + 1) * P, nodes], total[:, nodes])
+        cuts = [
+            (False, 0, 0, 512, True),
+            (False, 0, 512, 512, True),
+            (False, 1, 0, 512, True),
+            (True, 2, 0, 512, True),
+            (False, 1, 512, 512, True),
+            (True, 2, 512, 512, False),
+            (False, 3, 512, 256, False),
+            (False, 3, 768, 256, False),
+            (True, 3, 0, 512, False),
+        ]
+        picked = {}
+        for on_scalar, i, c0, n, on_gpsimd in cuts:
+            picked[i, c0] = keep.tile([P, n], F32, name=f"picked{i}_{c0}")
+            gather(on_scalar, picked[i, c0][:], dm[i][:], src[:, c0 // STRIPE : (c0 + n) // STRIPE])
+        for on_scalar, i, c0, n, on_gpsimd in cuts:
+            total = keep.tile([P, n // K], F32, name=f"total{i}_{c0}")
+            adder = nc.gpsimd if on_gpsimd else nc.vector
+            adder.tensor_tensor(total[:], picked[i, c0][:, 0:n:K], picked[i, c0][:, 1:n:K], ADD)
+            nc.sync.dma_start(out[i * P : (i + 1) * P, c0 // K : (c0 + n) // K], total[:])

@@ -1,6 +1,7 @@
 from contextlib import ExitStack
 
 import concourse.mybir as mybir
+from concourse.masks import make_identity
 
 V, K, E, D, DV = 512, 2, 1024, 512, 512
 FLOPS = 2 * DV * D * E
@@ -15,18 +16,22 @@ E5M2 = mybir.dt.float8_e5m2_x4
 MULT = mybir.AluOpType.mult
 ADD = mybir.AluOpType.add
 COPY = mybir.ActivationFunctionType.Copy
-IDENTITY = mybir.ActivationFunctionType.Identity
 SQUARE = mybir.ActivationFunctionType.Square
 
 P = 128
 PLANES = 4
+PAIR = 2
 N_PASS = 512
 STRIPE = 16
 RUN = 4
 CHUNK = 256
+CHUNKS = E // CHUNK
 DM_TILES = D // P
 HALF = N_PASS
-DY_PAD = 16
+LAST = E - CHUNK
+TURNED = (1, 2)
+SCALAR_EDGES = 384
+DY_PAD = 144
 
 
 def tile_attend_gmp_tnh_kernel(tc, dyT, hE, wm, offs, offs2, out):
@@ -37,49 +42,74 @@ def tile_attend_gmp_tnh_kernel(tc, dyT, hE, wm, offs, offs2, out):
 
     with ExitStack() as ctx:
         keep = ctx.enter_context(tc.tile_pool(name="keep", bufs=1))
+        shared = ctx.enter_context(tc.tile_pool(name="shared", bufs=1))
         psum = ctx.enter_context(tc.psum_pool(name="psum", bufs=1))
 
         dst = keep.tile([P, E // STRIPE], U16, name="dst")
         src = keep.tile([P, E // STRIPE], U16, name="src")
         dy = [keep.tile([P, V + DY_PAD], F32, name=f"dy{t}") for t in range(PLANES)]
-        h = [keep.tile([P, PLANES, CHUNK], F32, name=f"h{c}") for c in range(E // CHUNK)]
+        h_first = keep.tile([P, PLANES, CHUNK], F32, name="h_first")
+        h = {
+            (c, t0): keep.tile([P, PAIR, CHUNK], F32, name=f"h{c}_{t0}")
+            for c in TURNED
+            for t0 in range(0, PLANES, PAIR)
+        }
+        h_last = keep.tile([P, PLANES, CHUNK], F32, name="h_last")
         w = [keep.tile([P, PLANES, 2 * P], F32, name=f"w{j}") for j in range(2)]
 
         def load_dy(t):
             nc.sync.dma_start(dy[t][:, 0:V], dy_rows[:, t, :])
 
-        def load_h(c):
-            nc.sync.dma_start(h[c][:], h_rows[:, :, c * CHUNK : (c + 1) * CHUNK])
+        def load_h(c, t0):
+            tile = h_first[:, t0 : t0 + PAIR, :] if c == 0 else h[c, t0][:]
+            nc.sync.dma_start(tile, h_rows[:, t0 : t0 + PAIR, c * CHUNK : (c + 1) * CHUNK])
 
         load_dy(0)
         nc.sync.dma_start(dst[:], offs)
-        nc.sync.dma_start(h[0][:, 0:2, :], h_rows[:, 0:2, 0:CHUNK])
+        load_h(0, 0)
         load_dy(1)
+        load_h(0, PAIR)
         load_dy(2)
-        nc.sync.dma_start(h[0][:, 2:4, :], h_rows[:, 2:4, 0:CHUNK])
         load_dy(3)
-        load_h(1)
+        for c in TURNED:
+            load_h(c, 0)
+            load_h(c, PAIR)
+        nc.sync.dma_start(h_last[:], h_rows[:, :, LAST:E])
         nc.sync.dma_start(w[0][:], w_rows[:, :, 0 : 2 * P])
-        load_h(2)
-        load_h(3)
         nc.sync.dma_start(src[:], offs2)
         nc.sync.dma_start(w[1][:], w_rows[:, :, 2 * P : D])
 
-        zero = keep.tile([P, 1], F32, name="zero")
-        one = keep.tile([P, 1], F32, name="one")
-        nc.gpsimd.memset(zero[:], 0.0)
-        nc.scalar.activation(one[:], zero[:], COPY, bias=1.0)
+        zero = keep.tile([P, P], F32, name="zero")
+        nc.vector.memset(zero[:], 0.0)
+        minus_one = keep.tile([P, P], F32, name="minus_one")
+        nc.scalar.activation(minus_one[:], zero[:], COPY, bias=-1.0)
+        identity = keep.tile([P, P], F32, name="identity")
+        make_identity(nc, identity[:])
         for t in range(PLANES):
             nc.gpsimd.memset(dy[t][:, V:], 0.0)
 
-        gathered = [keep.tile([P, PLANES, HALF], F32, name=f"gathered{half}") for half in range(2)]
-        dz16 = [keep.tile([P, CHUNK * PLANES], BF16, name=f"dz16_{c}", align_bytes=64) for c in range(E // CHUNK)]
+        blocks = range(0, N_PASS, P)
+        factor = {}
+        for c in TURNED:
+            for j in range(CHUNK // P):
+                factor[c, j] = psum.tile([P, N_PASS], F32, name=f"factor{c}_{j}", tag=f"bank{2 * c + 2 + j}")
+                for c0 in blocks:
+                    nc.tensor.matmul(
+                        factor[c, j][:, c0 : c0 + P],
+                        minus_one[:],
+                        identity[:],
+                        start=c0 == 0,
+                        stop=False,
+                        is_transpose=True,
+                    )
+
+        gathered_first = keep.tile([P, PLANES, SCALAR_EDGES], F32, name="gathered_first")
+        gathered_rest = keep.tile([P, PLANES, E - SCALAR_EDGES], F32, name="gathered_rest")
+        dz16 = [keep.tile([P, HALF * PLANES], BF16, name=f"dz16_{half}", align_bytes=64) for half in range(2)]
         dz_codes = [keep.tile([P, N_PASS], U32, name=f"dz_codes{half}", align_bytes=64) for half in range(2)]
         dz_scales = [keep.tile([P, N_PASS], U8, name=f"dz_scales{half}", align_bytes=64) for half in range(2)]
-        w16 = [keep.tile([P, 2 * P * PLANES], BF16, name=f"w16_{j}", align_bytes=64) for j in range(2)]
-        w_codes = [keep.tile([P, 2 * P], U32, name=f"w_codes{j}", align_bytes=64) for j in range(2)]
-        w_scales = [keep.tile([P, 2 * P], U8, name=f"w_scales{j}", align_bytes=64) for j in range(2)]
-        dm = [keep.tile([P, E], F32, name=f"dm{i}") for i in range(DM_TILES)]
+        w_scales = [keep.tile([P, n], U8, name=f"w_scales{n}", align_bytes=64) for n in (P, D - P)]
+        dm = [keep.tile([P, E], F32, name=f"dm{i}", tag=f"dm{i}") for i in range(DM_TILES)]
 
         def gather(on_scalar, dest, window, entries):
             if on_scalar:
@@ -87,9 +117,13 @@ def tile_attend_gmp_tnh_kernel(tc, dyT, hE, wm, offs, offs2, out):
             else:
                 nc.vector.tensor_copy(dest, window.indirect(entries))
 
+        def gathered_part(e0, e1):
+            if e0 < SCALAR_EDGES:
+                return gathered_first[:, :, e0:e1]
+            return gathered_rest[:, :, e0 - SCALAR_EDGES : e1 - SCALAR_EDGES]
+
         def gather_dy(on_scalar, t, e0, e1):
-            dest = gathered[e0 // HALF][:, t, e0 % HALF : e0 % HALF + e1 - e0]
-            gather(on_scalar, dest, dy[t][:], dst[:, e0 // STRIPE : e1 // STRIPE])
+            gather(on_scalar, gathered_part(e0, e1)[:, t, :], dy[t][:], dst[:, e0 // STRIPE : e1 // STRIPE])
 
         def row_runs(rows):
             return rows.rearrange("p t (c i) -> p c t i", i=RUN)
@@ -97,39 +131,48 @@ def tile_attend_gmp_tnh_kernel(tc, dyT, hE, wm, offs, offs2, out):
         def interleaved_runs(interleaved):
             return interleaved.rearrange("p (c i t) -> p c t i", i=RUN, t=PLANES)
 
-        def flat(c):
-            return h[c][:].rearrange("p t e -> p (t e)")
+        squares = {}
 
-        def square_scalar(c):
-            nc.scalar.activation(flat(c), flat(c), SQUARE)
+        def turn_and_square(c, t0):
+            turned = psum.tile([P, N_PASS], F32, name=f"turned{c}_{t0}", tag=f"bank{2 * c - 2 + t0 // PAIR}")
+            for c0 in blocks:
+                j, t = divmod(c0 // P, PAIR)
+                nc.tensor.transpose(turned[:, c0 : c0 + P], h[c, t0][:, t, j * P : (j + 1) * P], identity[:])
+            if (c, t0) == (TURNED[-1], 0):
+                squares[c, t0] = shared.tile([P, N_PASS], F32, name="held_squares", align_bytes=64, offset=0)[:]
+            else:
+                squares[c, t0] = keep.tile([P, N_PASS], F32, name=f"squares{c}_{t0}")[:]
+            nc.scalar.activation(squares[c, t0], turned[:], SQUARE)
 
-        def flip_scalar(c):
-            nc.scalar.activation(flat(c), flat(c), IDENTITY, bias=one[:], scale=-1.0)
+        def turn_back(c, t0):
+            for c0 in blocks:
+                j, t = divmod(c0 // P, PAIR)
+                nc.tensor.matmul(
+                    factor[c, j][:, (t0 + t) * P : (t0 + t + 1) * P],
+                    squares[c, t0][:, c0 : c0 + P],
+                    identity[:],
+                    start=False,
+                    stop=t0 + t == PLANES - 1,
+                    is_transpose=True,
+                )
 
-        def product(c):
-            e0 = c * CHUNK % HALF
-            nc.vector.tensor_tensor(
-                interleaved_runs(dz16[c][:]),
-                row_runs(gathered[c * CHUNK // HALF][:, :, e0 : e0 + CHUNK]),
-                row_runs(h[c][:]),
+        def product(engine, c, e0, e1, rows):
+            engine.tensor_tensor(
+                interleaved_runs(dz16[c // 2][:, (c % 2 * CHUNK + e0) * PLANES : (c % 2 * CHUNK + e1) * PLANES]),
+                row_runs(gathered_part(c * CHUNK + e0, c * CHUNK + e1)),
+                row_runs(rows),
                 MULT,
             )
 
-        def quantize_dz(c):
-            half, e0 = divmod(c * CHUNK, HALF)
-            nc.vector.quantize_mx(
-                dz_codes[half][:, e0 : e0 + CHUNK].bitcast(E5M2), dz_scales[half][:, e0 : e0 + CHUNK], dz16[c][:]
-            )
+        def product_psum(c, j):
+            product(nc.vector, c, j * P, (j + 1) * P, factor[c, j][:].rearrange("p (t e) -> p t e", e=P))
 
-        def cast_w(j):
-            nc.vector.tensor_copy(interleaved_runs(w16[j][:]), row_runs(w[j][:]))
+        def quantize_dz(half):
+            nc.vector.quantize_mx(dz_codes[half][:].bitcast(E5M2), dz_scales[half][:], dz16[half][:])
 
-        def quantize_w(j):
-            nc.vector.quantize_mx(w_codes[j][:].bitcast(E4M3), w_scales[j][:], w16[j][:])
-
-        def multiply(i, half):
-            j, d0 = divmod(i * P, 2 * P)
-            bank = psum.tile([P, N_PASS], F32, name=f"pass{i}_{half}")
+        def multiply(i, half, bank_number, on_scalar):
+            j, d0 = (0, 0) if i == 0 else (1, (i - 1) * P)
+            bank = psum.tile([P, N_PASS], F32, name=f"pass{i}_{half}", tag=f"bank{bank_number}")
             nc.tensor.matmul_mx(
                 bank[:],
                 lhsT=w_codes[j][:, d0 : d0 + P].bitcast(E4M3),
@@ -139,44 +182,58 @@ def tile_attend_gmp_tnh_kernel(tc, dyT, hE, wm, offs, offs2, out):
                 start=True,
                 stop=True,
             )
-            nc.scalar.activation(dm[i][:, half * N_PASS : (half + 1) * N_PASS], bank[:], COPY)
+            part = dm[i][:, half * N_PASS : (half + 1) * N_PASS]
+            if on_scalar:
+                nc.scalar.activation(part, bank[:], COPY, scale=-1.0)
+            else:
+                nc.vector.tensor_scalar(part, bank[:], -1.0, 0.0, MULT, ADD)
 
-        for t0 in (0, 2):
-            part = h[0][:, t0 : t0 + 2, :].rearrange("p t e -> p (t e)")
+        for t0 in range(0, PLANES, PAIR):
+            part = h_first[:, t0 : t0 + PAIR, :].rearrange("p t e -> p (t e)")
             nc.gpsimd.tensor_tensor(part, part, part, MULT)
-            nc.gpsimd.tensor_scalar(part, part, -1.0, 1.0, MULT, ADD)
-        for t in range(3):
-            gather_dy(False, t, 0, HALF)
-            gather_dy(True, t, HALF, E)
-        gather_dy(False, 3, 0, HALF)
-        gather_dy(True, 3, HALF + CHUNK, E)
-        gather_dy(False, 3, HALF, HALF + CHUNK)
-        square_scalar(1)
-        flip_scalar(1)
-        square_scalar(2)
-        flip_scalar(2)
-        square_scalar(3)
-        flip_scalar(3)
+            nc.gpsimd.tensor_scalar(part, part, 1.0, -1.0, MULT, ADD)
 
-        product(0)
+        for t in range(PLANES):
+            gather_dy(True, t, 0, SCALAR_EDGES)
+            gather_dy(False, t, SCALAR_EDGES, E)
+        product(nc.gpsimd, 0, 0, CHUNK, h_first[:])
+
+        loads = [(c, t0) for c in TURNED for t0 in range(0, PLANES, PAIR)]
+        for load in loads:
+            turn_and_square(*load)
+        for load in loads:
+            turn_back(*load)
+        last_squares = shared.tile([P, PLANES, CHUNK], F32, name="last_squares", align_bytes=64, offset=0)
+        last_factor = shared.tile([P, PLANES, CHUNK], F32, name="last_factor", align_bytes=64, offset=4096)
+        for t0 in range(0, PLANES, PAIR):
+            nc.scalar.activation(last_squares[:, t0 : t0 + PAIR, :], h_last[:, t0 : t0 + PAIR, :], SQUARE)
+        for t0 in range(0, PLANES, PAIR):
+            nc.scalar.activation(last_factor[:, t0 : t0 + PAIR, :], last_squares[:, t0 : t0 + PAIR, :], COPY, bias=-1.0)
+        w16_first = shared.tile([P, P * PLANES], BF16, name="w16_first", align_bytes=64, offset=0)
+        w16_rest = shared.tile([P, (D - P) * PLANES], BF16, name="w16_rest", align_bytes=64, offset=1024)
+        nc.scalar.copy(interleaved_runs(w16_first[:]), row_runs(w[0][:, :, 0:P]))
+        nc.scalar.copy(interleaved_runs(w16_rest[:, 0 : P * PLANES]), row_runs(w[0][:, :, P : 2 * P]))
+        nc.scalar.copy(interleaved_runs(w16_rest[:, P * PLANES :]), row_runs(w[1][:]))
+
+        for c in TURNED:
+            for j in range(CHUNK // P):
+                product_psum(c, j)
         quantize_dz(0)
-        product(1)
-        cast_w(0)
+        product(nc.vector, CHUNKS - 1, 0, CHUNK, last_factor[:])
+        w_codes = [
+            keep.tile([P, P], U32, name="w_codes_first", align_bytes=64),
+            shared.tile([P, D - P], U32, name="w_codes_rest", align_bytes=64, offset=4096),
+        ]
+        nc.vector.quantize_mx(w_codes[0][:].bitcast(E4M3), w_scales[0][:], w16_first[:])
         quantize_dz(1)
-        product(2)
-        quantize_w(0)
-        multiply(0, 0)
-        multiply(1, 0)
-        quantize_dz(2)
-        product(3)
-        quantize_dz(3)
-        cast_w(1)
-        multiply(0, 1)
-        multiply(1, 1)
-        quantize_w(1)
+        nc.vector.quantize_mx(w_codes[1][:].bitcast(E4M3), w_scales[1][:], w16_rest[:])
+        multiply(0, 0, 0, True)
+        multiply(0, 1, 2, False)
+        multiply(1, 0, 1, True)
+        multiply(1, 1, 3, True)
         for i in range(2, DM_TILES):
-            multiply(i, 0)
-            multiply(i, 1)
+            multiply(i, 0, 2 * i, True)
+            multiply(i, 1, 2 * i + 1, True)
 
         cuts = [
             (False, 0, 0, 512, True),
@@ -185,8 +242,8 @@ def tile_attend_gmp_tnh_kernel(tc, dyT, hE, wm, offs, offs2, out):
             (True, 2, 0, 512, True),
             (False, 1, 512, 512, True),
             (True, 2, 512, 512, False),
-            (False, 3, 512, 256, False),
-            (False, 3, 768, 256, False),
+            (False, 3, 512, 384, False),
+            (False, 3, 896, 128, False),
             (True, 3, 0, 512, False),
         ]
         picked = {}

@@ -28,10 +28,14 @@ CHUNK = 256
 CHUNKS = E // CHUNK
 DM_TILES = D // P
 HALF = N_PASS
-LAST = E - CHUNK
-TURNED = (1, 2)
-SCALAR_EDGES = 384
-DY_PAD = 144
+TURNED = 1
+DY_PAD = 16
+H_TURNED_AT = 0
+LAST_SQUARES_AT = 0
+H_LAST_AT = 4096
+TURNED_SQUARES_AT = 8192
+FIRST_SQUARES_AT = 12288
+DZ_AT = {TURNED: 16384, CHUNKS - 1: H_LAST_AT}
 
 
 def tile_attend_gmp_tnh_kernel(tc, dyT, hE, wm, offs, offs2, out):
@@ -48,21 +52,16 @@ def tile_attend_gmp_tnh_kernel(tc, dyT, hE, wm, offs, offs2, out):
         dst = keep.tile([P, E // STRIPE], U16, name="dst")
         src = keep.tile([P, E // STRIPE], U16, name="src")
         dy = [keep.tile([P, V + DY_PAD], F32, name=f"dy{t}") for t in range(PLANES)]
-        h_first = keep.tile([P, PLANES, CHUNK], F32, name="h_first")
-        h = {
-            (c, t0): keep.tile([P, PAIR, CHUNK], F32, name=f"h{c}_{t0}")
-            for c in TURNED
-            for t0 in range(0, PLANES, PAIR)
-        }
-        h_last = keep.tile([P, PLANES, CHUNK], F32, name="h_last")
+        h = {c: keep.tile([P, PLANES, CHUNK], F32, name=f"h{c}") for c in (0, 2)}
+        for c, at in ((TURNED, H_TURNED_AT), (CHUNKS - 1, H_LAST_AT)):
+            h[c] = shared.tile([P, PLANES, CHUNK], F32, name=f"h{c}", align_bytes=64, offset=at)
         w = [keep.tile([P, PLANES, 2 * P], F32, name=f"w{j}") for j in range(2)]
 
         def load_dy(t):
             nc.sync.dma_start(dy[t][:, 0:V], dy_rows[:, t, :])
 
         def load_h(c, t0):
-            tile = h_first[:, t0 : t0 + PAIR, :] if c == 0 else h[c, t0][:]
-            nc.sync.dma_start(tile, h_rows[:, t0 : t0 + PAIR, c * CHUNK : (c + 1) * CHUNK])
+            nc.sync.dma_start(h[c][:, t0 : t0 + PAIR, :], h_rows[:, t0 : t0 + PAIR, c * CHUNK : (c + 1) * CHUNK])
 
         load_dy(0)
         nc.sync.dma_start(dst[:], offs)
@@ -71,10 +70,9 @@ def tile_attend_gmp_tnh_kernel(tc, dyT, hE, wm, offs, offs2, out):
         load_h(0, PAIR)
         load_dy(2)
         load_dy(3)
-        for c in TURNED:
+        for c in (2, TURNED, 3):
             load_h(c, 0)
             load_h(c, PAIR)
-        nc.sync.dma_start(h_last[:], h_rows[:, :, LAST:E])
         nc.sync.dma_start(w[0][:], w_rows[:, :, 0 : 2 * P])
         nc.sync.dma_start(src[:], offs2)
         nc.sync.dma_start(w[1][:], w_rows[:, :, 2 * P : D])
@@ -89,26 +87,19 @@ def tile_attend_gmp_tnh_kernel(tc, dyT, hE, wm, offs, offs2, out):
             nc.gpsimd.memset(dy[t][:, V:], 0.0)
 
         blocks = range(0, N_PASS, P)
-        factor = {}
-        for c in TURNED:
-            for j in range(CHUNK // P):
-                factor[c, j] = psum.tile([P, N_PASS], F32, name=f"factor{c}_{j}", tag=f"bank{2 * c + 2 + j}")
-                for c0 in blocks:
-                    nc.tensor.matmul(
-                        factor[c, j][:, c0 : c0 + P],
-                        minus_one[:],
-                        identity[:],
-                        start=c0 == 0,
-                        stop=False,
-                        is_transpose=True,
-                    )
+        factor_banks = [
+            psum.tile([P, N_PASS], F32, name=f"factor{j}", tag=f"bank{2 + j}") for j in range(CHUNK // P)
+        ]
+        for bank in factor_banks:
+            for c0 in blocks:
+                nc.tensor.matmul(
+                    bank[:, c0 : c0 + P], minus_one[:], identity[:], start=c0 == 0, stop=False, is_transpose=True
+                )
 
-        gathered_first = keep.tile([P, PLANES, SCALAR_EDGES], F32, name="gathered_first")
-        gathered_rest = keep.tile([P, PLANES, E - SCALAR_EDGES], F32, name="gathered_rest")
-        dz16 = [keep.tile([P, HALF * PLANES], BF16, name=f"dz16_{half}", align_bytes=64) for half in range(2)]
-        dz_codes = [keep.tile([P, N_PASS], U32, name=f"dz_codes{half}", align_bytes=64) for half in range(2)]
-        dz_scales = [keep.tile([P, N_PASS], U8, name=f"dz_scales{half}", align_bytes=64) for half in range(2)]
-        w_scales = [keep.tile([P, n], U8, name=f"w_scales{n}", align_bytes=64) for n in (P, D - P)]
+        gathered = [keep.tile([P, PLANES, HALF], F32, name=f"gathered{half}") for half in range(2)]
+        dz16 = {}
+        dz_scales = keep.tile([P, E], U8, name="dz_scales", align_bytes=64)
+        w_scales = keep.tile([P, D], U8, name="w_scales", align_bytes=64)
         dm = [keep.tile([P, E], F32, name=f"dm{i}", tag=f"dm{i}") for i in range(DM_TILES)]
 
         def gather(on_scalar, dest, window, entries):
@@ -118,9 +109,7 @@ def tile_attend_gmp_tnh_kernel(tc, dyT, hE, wm, offs, offs2, out):
                 nc.vector.tensor_copy(dest, window.indirect(entries))
 
         def gathered_part(e0, e1):
-            if e0 < SCALAR_EDGES:
-                return gathered_first[:, :, e0:e1]
-            return gathered_rest[:, :, e0 - SCALAR_EDGES : e1 - SCALAR_EDGES]
+            return gathered[e0 // HALF][:, :, e0 % HALF : e0 % HALF + e1 - e0]
 
         def gather_dy(on_scalar, t, e0, e1):
             gather(on_scalar, gathered_part(e0, e1)[:, t, :], dy[t][:], dst[:, e0 // STRIPE : e1 // STRIPE])
@@ -131,109 +120,125 @@ def tile_attend_gmp_tnh_kernel(tc, dyT, hE, wm, offs, offs2, out):
         def interleaved_runs(interleaved):
             return interleaved.rearrange("p (c i t) -> p c t i", i=RUN, t=PLANES)
 
-        squares = {}
+        def pair_of(tile, t0):
+            return tile[:, t0 : t0 + PAIR, :].rearrange("p t e -> p (t e)")
 
-        def turn_and_square(c, t0):
-            turned = psum.tile([P, N_PASS], F32, name=f"turned{c}_{t0}", tag=f"bank{2 * c - 2 + t0 // PAIR}")
+        def product(c, e0, e1, rows):
+            if e0 == 0 and c in DZ_AT:
+                dz16[c] = shared.tile([P, CHUNK * PLANES], BF16, name=f"dz16_{c}", align_bytes=64, offset=DZ_AT[c])
+            elif e0 == 0:
+                dz16[c] = keep.tile([P, CHUNK * PLANES], BF16, name=f"dz16_{c}", align_bytes=64)
+            nc.vector.tensor_tensor(
+                interleaved_runs(dz16[c][:, e0 * PLANES : e1 * PLANES]),
+                row_runs(gathered_part(c * CHUNK + e0, c * CHUNK + e1)),
+                row_runs(rows),
+                MULT,
+            )
+
+        def quantize_dz(c, codes):
+            nc.vector.quantize_mx(codes.bitcast(E5M2), dz_scales[:, c * CHUNK : (c + 1) * CHUNK], dz16[c][:])
+
+        def multiply(i, e0, parts, bank_number, on_scalar=True):
+            width = sum(codes.shape[1] for codes in parts)
+            bank = psum.tile([P, width], F32, name=f"pass{i}_{e0}", tag=f"bank{bank_number}")
+            c0 = 0
+            for codes in parts:
+                n = codes.shape[1]
+                nc.tensor.matmul_mx(
+                    bank[:, c0 : c0 + n],
+                    lhsT=w_codes[:, i * P : (i + 1) * P].bitcast(E4M3),
+                    lhsT_scale=w_scales[:, i * P : (i + 1) * P],
+                    rhs=codes.bitcast(E5M2),
+                    rhs_scale=dz_scales[:, e0 + c0 : e0 + c0 + n],
+                    start=True,
+                    stop=True,
+                )
+                c0 = c0 + n
+            if on_scalar:
+                nc.scalar.activation(dm[i][:, e0 : e0 + width], bank[:], COPY, scale=-1.0)
+            else:
+                nc.vector.tensor_scalar(dm[i][:, e0 : e0 + width], bank[:], -1.0, 0.0, MULT, ADD)
+
+        pairs = range(0, PLANES, PAIR)
+        for t0 in pairs:
+            part = pair_of(h[0], t0)
+            first_squares = shared.tile([P, N_PASS], F32, name=f"first_squares{t0}", align_bytes=64, offset=FIRST_SQUARES_AT)
+            nc.gpsimd.tensor_tensor(first_squares[:], part, part, MULT)
+            nc.gpsimd.tensor_scalar(part, first_squares[:], 1.0, -1.0, MULT, ADD)
+
+        for t in range(PLANES):
+            gather_dy(False, t, 0, HALF)
+            gather_dy(True, t, HALF, E)
+
+        for t0 in pairs:
+            nc.scalar.activation(pair_of(h[2], t0), pair_of(h[2], t0), SQUARE)
+        turned_squares = {
+            0: keep.tile([P, N_PASS], F32, name="turned_squares0"),
+            PAIR: shared.tile([P, N_PASS], F32, name="turned_squares2", align_bytes=64, offset=TURNED_SQUARES_AT),
+        }
+        for t0 in pairs:
+            turned = psum.tile([P, N_PASS], F32, name=f"turned{t0}", tag=f"bank{t0 // PAIR}")
             for c0 in blocks:
                 j, t = divmod(c0 // P, PAIR)
-                nc.tensor.transpose(turned[:, c0 : c0 + P], h[c, t0][:, t, j * P : (j + 1) * P], identity[:])
-            if (c, t0) == (TURNED[-1], 0):
-                squares[c, t0] = shared.tile([P, N_PASS], F32, name="held_squares", align_bytes=64, offset=0)[:]
-            else:
-                squares[c, t0] = keep.tile([P, N_PASS], F32, name=f"squares{c}_{t0}")[:]
-            nc.scalar.activation(squares[c, t0], turned[:], SQUARE)
-
-        def turn_back(c, t0):
+                nc.tensor.transpose(turned[:, c0 : c0 + P], h[TURNED][:, t0 + t, j * P : (j + 1) * P], identity[:])
+            nc.scalar.activation(turned_squares[t0][:], turned[:], SQUARE)
+        for t0 in pairs:
             for c0 in blocks:
                 j, t = divmod(c0 // P, PAIR)
                 nc.tensor.matmul(
-                    factor[c, j][:, (t0 + t) * P : (t0 + t + 1) * P],
-                    squares[c, t0][:, c0 : c0 + P],
+                    factor_banks[j][:, (t0 + t) * P : (t0 + t + 1) * P],
+                    turned_squares[t0][:, c0 : c0 + P],
                     identity[:],
                     start=False,
                     stop=t0 + t == PLANES - 1,
                     is_transpose=True,
                 )
 
-        def product(engine, c, e0, e1, rows):
-            engine.tensor_tensor(
-                interleaved_runs(dz16[c // 2][:, (c % 2 * CHUNK + e0) * PLANES : (c % 2 * CHUNK + e1) * PLANES]),
-                row_runs(gathered_part(c * CHUNK + e0, c * CHUNK + e1)),
-                row_runs(rows),
-                MULT,
-            )
-
-        def product_psum(c, j):
-            product(nc.vector, c, j * P, (j + 1) * P, factor[c, j][:].rearrange("p (t e) -> p t e", e=P))
-
-        def quantize_dz(half):
-            nc.vector.quantize_mx(dz_codes[half][:].bitcast(E5M2), dz_scales[half][:], dz16[half][:])
-
-        def multiply(i, half, bank_number, on_scalar):
-            j, d0 = (0, 0) if i == 0 else (1, (i - 1) * P)
-            bank = psum.tile([P, N_PASS], F32, name=f"pass{i}_{half}", tag=f"bank{bank_number}")
-            nc.tensor.matmul_mx(
-                bank[:],
-                lhsT=w_codes[j][:, d0 : d0 + P].bitcast(E4M3),
-                lhsT_scale=w_scales[j][:, d0 : d0 + P],
-                rhs=dz_codes[half][:].bitcast(E5M2),
-                rhs_scale=dz_scales[half][:],
-                start=True,
-                stop=True,
-            )
-            part = dm[i][:, half * N_PASS : (half + 1) * N_PASS]
-            if on_scalar:
-                nc.scalar.activation(part, bank[:], COPY, scale=-1.0)
-            else:
-                nc.vector.tensor_scalar(part, bank[:], -1.0, 0.0, MULT, ADD)
-
-        for t0 in range(0, PLANES, PAIR):
-            part = h_first[:, t0 : t0 + PAIR, :].rearrange("p t e -> p (t e)")
-            nc.gpsimd.tensor_tensor(part, part, part, MULT)
-            nc.gpsimd.tensor_scalar(part, part, 1.0, -1.0, MULT, ADD)
-
-        for t in range(PLANES):
-            gather_dy(True, t, 0, SCALAR_EDGES)
-            gather_dy(False, t, SCALAR_EDGES, E)
-        product(nc.gpsimd, 0, 0, CHUNK, h_first[:])
-
-        loads = [(c, t0) for c in TURNED for t0 in range(0, PLANES, PAIR)]
-        for load in loads:
-            turn_and_square(*load)
-        for load in loads:
-            turn_back(*load)
-        last_squares = shared.tile([P, PLANES, CHUNK], F32, name="last_squares", align_bytes=64, offset=0)
-        last_factor = shared.tile([P, PLANES, CHUNK], F32, name="last_factor", align_bytes=64, offset=4096)
-        for t0 in range(0, PLANES, PAIR):
-            nc.scalar.activation(last_squares[:, t0 : t0 + PAIR, :], h_last[:, t0 : t0 + PAIR, :], SQUARE)
-        for t0 in range(0, PLANES, PAIR):
-            nc.scalar.activation(last_factor[:, t0 : t0 + PAIR, :], last_squares[:, t0 : t0 + PAIR, :], COPY, bias=-1.0)
-        w16_first = shared.tile([P, P * PLANES], BF16, name="w16_first", align_bytes=64, offset=0)
-        w16_rest = shared.tile([P, (D - P) * PLANES], BF16, name="w16_rest", align_bytes=64, offset=1024)
-        nc.scalar.copy(interleaved_runs(w16_first[:]), row_runs(w[0][:, :, 0:P]))
-        nc.scalar.copy(interleaved_runs(w16_rest[:, 0 : P * PLANES]), row_runs(w[0][:, :, P : 2 * P]))
-        nc.scalar.copy(interleaved_runs(w16_rest[:, P * PLANES :]), row_runs(w[1][:]))
-
-        for c in TURNED:
-            for j in range(CHUNK // P):
-                product_psum(c, j)
-        quantize_dz(0)
-        product(nc.vector, CHUNKS - 1, 0, CHUNK, last_factor[:])
-        w_codes = [
-            keep.tile([P, P], U32, name="w_codes_first", align_bytes=64),
-            shared.tile([P, D - P], U32, name="w_codes_rest", align_bytes=64, offset=4096),
+        last_squares = shared.tile([P, PLANES, CHUNK], F32, name="last_squares", align_bytes=64, offset=LAST_SQUARES_AT)
+        last_factor = keep.tile([P, PLANES, CHUNK], F32, name="last_factor")
+        for t0 in pairs:
+            nc.scalar.activation(pair_of(last_squares, t0), pair_of(h[3], t0), SQUARE)
+        for t0 in pairs:
+            nc.gpsimd.tensor_scalar(pair_of(last_factor, t0), pair_of(last_squares, t0), 1.0, -1.0, MULT, ADD)
+        w16 = [
+            shared.tile([P, 2 * P * PLANES], BF16, name=f"w16_{j}", align_bytes=64, offset=H_LAST_AT + 2048 * j)
+            for j in range(2)
         ]
-        nc.vector.quantize_mx(w_codes[0][:].bitcast(E4M3), w_scales[0][:], w16_first[:])
-        quantize_dz(1)
-        nc.vector.quantize_mx(w_codes[1][:].bitcast(E4M3), w_scales[1][:], w16_rest[:])
-        multiply(0, 0, 0, True)
-        multiply(0, 1, 2, False)
-        multiply(1, 0, 1, True)
-        multiply(1, 1, 3, True)
-        for i in range(2, DM_TILES):
-            multiply(i, 0, 2 * i, True)
-            multiply(i, 1, 2 * i + 1, True)
+        for j in range(2):
+            nc.scalar.copy(interleaved_runs(w16[j][:]), row_runs(w[j][:]))
+
+        w_codes = shared.tile([P, D], U32, name="w_codes", align_bytes=64, offset=TURNED_SQUARES_AT)
+
+        def quantize_w(d0, d1):
+            nc.vector.quantize_mx(w_codes[:, d0:d1].bitcast(E4M3), w_scales[:, d0:d1], w16[d0 // (2 * P)][:])
+
+        codes_first = keep.tile([P, HALF], U32, name="codes_first", align_bytes=64)
+        product(0, 0, CHUNK, h[0][:])
+        third_factor = shared.tile([P, PLANES, CHUNK], F32, name="third_factor", align_bytes=64, offset=FIRST_SQUARES_AT)
+        nc.vector.tensor_scalar(
+            third_factor[:].rearrange("p t e -> p (t e)"), h[2][:].rearrange("p t e -> p (t e)"), 1.0, -1.0, MULT, ADD
+        )
+        quantize_dz(0, codes_first[:, 0:CHUNK])
+        product(2, 0, CHUNK, third_factor[:])
+        for j, bank in enumerate(factor_banks):
+            product(TURNED, j * P, (j + 1) * P, bank[:].rearrange("p (t e) -> p t e", e=P))
+        quantize_w(0, 2 * P)
+        quantize_dz(1, codes_first[:, CHUNK:HALF])
+        product(3, 0, CHUNK, last_factor[:])
+        codes_rest = shared.tile([P, HALF], U32, name="codes_rest", align_bytes=64, offset=DZ_AT[TURNED])
+        quantize_dz(2, codes_rest[:, 0:CHUNK])
+        quantize_dz(3, codes_rest[:, CHUNK:HALF])
+        quantize_w(2 * P, D)
+        first_half = [codes_first[:]]
+        multiply(0, 0, first_half, 4)
+        multiply(1, 0, first_half, 7)
+        multiply(0, HALF, [codes_rest[:, 0:CHUNK]], 5, on_scalar=False)
+        multiply(0, HALF + CHUNK, [codes_rest[:, CHUNK:HALF]], 6)
+        multiply(1, HALF, [codes_rest[:]], 0)
+        multiply(2, 0, first_half, 1)
+        multiply(2, HALF, [codes_rest[:]], 2)
+        multiply(3, 0, first_half, 3)
+        multiply(3, HALF, [codes_rest[:]], 4)
 
         cuts = [
             (False, 0, 0, 512, True),

@@ -30,12 +30,13 @@ DM_TILES = D // P
 HALF = N_PASS
 TURNED = 1
 DY_PAD = 16
+W_PARTS = ((0, P), (P, 2 * P), (2 * P, D))
 H_TURNED_AT = 0
 LAST_SQUARES_AT = 0
 H_LAST_AT = 4096
 TURNED_SQUARES_AT = 8192
 FIRST_SQUARES_AT = 12288
-DZ_AT = {TURNED: 16384, CHUNKS - 1: H_LAST_AT}
+DZ_AT = {TURNED: 16384, CHUNKS - 1: H_LAST_AT - 1024}
 
 
 def tile_attend_gmp_tnh_kernel(tc, dyT, hE, wm, offs, offs2, out):
@@ -55,7 +56,7 @@ def tile_attend_gmp_tnh_kernel(tc, dyT, hE, wm, offs, offs2, out):
         h = {c: keep.tile([P, PLANES, CHUNK], F32, name=f"h{c}") for c in (0, 2)}
         for c, at in ((TURNED, H_TURNED_AT), (CHUNKS - 1, H_LAST_AT)):
             h[c] = shared.tile([P, PLANES, CHUNK], F32, name=f"h{c}", align_bytes=64, offset=at)
-        w = [keep.tile([P, PLANES, 2 * P], F32, name=f"w{j}") for j in range(2)]
+        w = {d0: keep.tile([P, PLANES, d1 - d0], F32, name=f"w{d0}") for d0, d1 in W_PARTS}
 
         def load_dy(t):
             nc.sync.dma_start(dy[t][:, 0:V], dy_rows[:, t, :])
@@ -67,15 +68,15 @@ def tile_attend_gmp_tnh_kernel(tc, dyT, hE, wm, offs, offs2, out):
         nc.sync.dma_start(dst[:], offs)
         load_h(0, 0)
         load_dy(1)
-        load_h(0, PAIR)
         load_dy(2)
+        load_h(0, PAIR)
         load_dy(3)
         for c in (2, TURNED, 3):
             load_h(c, 0)
             load_h(c, PAIR)
-        nc.sync.dma_start(w[0][:], w_rows[:, :, 0 : 2 * P])
+        for d0, d1 in W_PARTS:
+            nc.sync.dma_start(w[d0][:], w_rows[:, :, d0:d1])
         nc.sync.dma_start(src[:], offs2)
-        nc.sync.dma_start(w[1][:], w_rows[:, :, 2 * P : D])
 
         zero = keep.tile([P, P], F32, name="zero")
         nc.vector.memset(zero[:], 0.0)
@@ -200,17 +201,19 @@ def tile_attend_gmp_tnh_kernel(tc, dyT, hE, wm, offs, offs2, out):
             nc.scalar.activation(pair_of(last_squares, t0), pair_of(h[3], t0), SQUARE)
         for t0 in pairs:
             nc.gpsimd.tensor_scalar(pair_of(last_factor, t0), pair_of(last_squares, t0), 1.0, -1.0, MULT, ADD)
-        w16 = [
-            shared.tile([P, 2 * P * PLANES], BF16, name=f"w16_{j}", align_bytes=64, offset=H_LAST_AT + 2048 * j)
-            for j in range(2)
-        ]
-        for j in range(2):
-            nc.scalar.copy(interleaved_runs(w16[j][:]), row_runs(w[j][:]))
+        w16 = {
+            d0: shared.tile(
+                [P, (d1 - d0) * PLANES], BF16, name=f"w16_{d0}", align_bytes=64, offset=H_LAST_AT + 2 * PLANES * d0
+            )
+            for d0, d1 in W_PARTS
+        }
+        for d0, d1 in W_PARTS:
+            nc.scalar.copy(interleaved_runs(w16[d0][:]), row_runs(w[d0][:]))
 
         w_codes = shared.tile([P, D], U32, name="w_codes", align_bytes=64, offset=TURNED_SQUARES_AT)
 
         def quantize_w(d0, d1):
-            nc.vector.quantize_mx(w_codes[:, d0:d1].bitcast(E4M3), w_scales[:, d0:d1], w16[d0 // (2 * P)][:])
+            nc.vector.quantize_mx(w_codes[:, d0:d1].bitcast(E4M3), w_scales[:, d0:d1], w16[d0][:])
 
         codes_first = keep.tile([P, HALF], U32, name="codes_first", align_bytes=64)
         product(0, 0, CHUNK, h[0][:])
@@ -222,8 +225,9 @@ def tile_attend_gmp_tnh_kernel(tc, dyT, hE, wm, offs, offs2, out):
         product(2, 0, CHUNK, third_factor[:])
         for j, bank in enumerate(factor_banks):
             product(TURNED, j * P, (j + 1) * P, bank[:].rearrange("p (t e) -> p t e", e=P))
-        quantize_w(0, 2 * P)
+        quantize_w(0, P)
         quantize_dz(1, codes_first[:, CHUNK:HALF])
+        quantize_w(P, 2 * P)
         product(3, 0, CHUNK, last_factor[:])
         codes_rest = shared.tile([P, HALF], U32, name="codes_rest", align_bytes=64, offset=DZ_AT[TURNED])
         quantize_dz(2, codes_rest[:, 0:CHUNK])
@@ -235,28 +239,28 @@ def tile_attend_gmp_tnh_kernel(tc, dyT, hE, wm, offs, offs2, out):
         multiply(0, HALF, [codes_rest[:, 0:CHUNK]], 5, on_scalar=False)
         multiply(0, HALF + CHUNK, [codes_rest[:, CHUNK:HALF]], 6)
         multiply(1, HALF, [codes_rest[:]], 0)
+        picked = {}
+
+        def gather_dm(on_scalar, i, c0, n):
+            picked[i, c0] = keep.tile([P, n], F32, name=f"picked{i}_{c0}")
+            gather(on_scalar, picked[i, c0][:], dm[i][:], src[:, c0 // STRIPE : (c0 + n) // STRIPE])
+
+        gather_dm(False, 0, 0, 512)
+        gather_dm(True, 0, 512, 512)
         multiply(2, 0, first_half, 1)
         multiply(2, HALF, [codes_rest[:]], 2)
         multiply(3, 0, first_half, 3)
         multiply(3, HALF, [codes_rest[:]], 4)
-
-        cuts = [
-            (False, 0, 0, 512, True),
-            (False, 0, 512, 512, True),
-            (False, 1, 0, 512, True),
-            (True, 2, 0, 512, True),
-            (False, 1, 512, 512, True),
-            (True, 2, 512, 512, False),
-            (False, 3, 512, 384, False),
-            (False, 3, 896, 128, False),
-            (True, 3, 0, 512, False),
-        ]
-        picked = {}
-        for on_scalar, i, c0, n, on_gpsimd in cuts:
-            picked[i, c0] = keep.tile([P, n], F32, name=f"picked{i}_{c0}")
-            gather(on_scalar, picked[i, c0][:], dm[i][:], src[:, c0 // STRIPE : (c0 + n) // STRIPE])
-        for on_scalar, i, c0, n, on_gpsimd in cuts:
+        gather_dm(False, 1, 0, 512)
+        gather_dm(False, 1, 512, 512)
+        gather_dm(False, 2, 0, 512)
+        gather_dm(False, 2, 512, 384)
+        gather_dm(True, 3, 0, 512)
+        gather_dm(True, 3, 512, 512)
+        gather_dm(True, 2, 896, 128)
+        for number, ((i, c0), tile) in enumerate(picked.items()):
+            n = tile.shape[1]
             total = keep.tile([P, n // K], F32, name=f"total{i}_{c0}")
-            adder = nc.gpsimd if on_gpsimd else nc.vector
-            adder.tensor_tensor(total[:], picked[i, c0][:, 0:n:K], picked[i, c0][:, 1:n:K], ADD)
+            adder = nc.gpsimd if number < 5 else nc.vector
+            adder.tensor_tensor(total[:], tile[:, 0:n:K], tile[:, 1:n:K], ADD)
             nc.sync.dma_start(out[i * P : (i + 1) * P, c0 // K : (c0 + n) // K], total[:])

@@ -21,22 +21,28 @@ SQUARE = mybir.ActivationFunctionType.Square
 P = 128
 PLANES = 4
 PAIR = 2
-N_PASS = 512
+BANK = 512
 STRIPE = 16
 RUN = 4
 CHUNK = 256
-CHUNKS = E // CHUNK
+HALF = E // 2
 DM_TILES = D // P
-HALF = N_PASS
-TURNED = 1
 DY_PAD = 16
+SHORT_CUT = 128
+GPSIMD_CUTS = 5
+
+FIRST, TURNED, THIRD, LAST = range(E // CHUNK)
 W_PARTS = ((0, P), (P, 2 * P), (2 * P, D))
+
+PAIR_BYTES = 4 * PAIR * CHUNK
+W16_BYTES = 2 * PLANES * P
 H_TURNED_AT = 0
-LAST_SQUARES_AT = 0
-H_LAST_AT = 4096
-TURNED_SQUARES_AT = 8192
-FIRST_SQUARES_AT = 12288
-DZ_AT = {TURNED: 16384, CHUNKS - 1: H_LAST_AT - 1024}
+H_LAST_AT = H_TURNED_AT + 2 * PAIR_BYTES
+DZ_LAST_AT = H_LAST_AT - W16_BYTES
+TURNED_SQUARES_AT = H_LAST_AT + 2 * PAIR_BYTES
+FIRST_SQUARES_AT = TURNED_SQUARES_AT + 2 * PAIR_BYTES
+DZ_TURNED_AT = FIRST_SQUARES_AT + 2 * PAIR_BYTES
+LAST_FACTOR_AT = DZ_TURNED_AT + 2 * PAIR_BYTES
 
 
 def tile_attend_gmp_tnh_kernel(tc, dyT, hE, wm, offs, offs2, out):
@@ -44,36 +50,44 @@ def tile_attend_gmp_tnh_kernel(tc, dyT, hE, wm, offs, offs2, out):
     dy_rows = dyT.rearrange("(p t) v -> p t v", t=PLANES)
     h_rows = hE.rearrange("(p t) e -> p t e", t=PLANES)
     w_rows = wm.rearrange("(p t) d -> p t d", t=PLANES)
+    pairs = range(0, PLANES, PAIR)
+    blocks = range(0, BANK, P)
 
     with ExitStack() as ctx:
         keep = ctx.enter_context(tc.tile_pool(name="keep", bufs=1))
         shared = ctx.enter_context(tc.tile_pool(name="shared", bufs=1))
         psum = ctx.enter_context(tc.psum_pool(name="psum", bufs=1))
 
+        def shared_tile(name, shape, dtype, at):
+            return shared.tile(shape, dtype, name=name, align_bytes=64, offset=at)
+
         dst = keep.tile([P, E // STRIPE], U16, name="dst")
         src = keep.tile([P, E // STRIPE], U16, name="src")
         dy = [keep.tile([P, V + DY_PAD], F32, name=f"dy{t}") for t in range(PLANES)]
-        h = {c: keep.tile([P, PLANES, CHUNK], F32, name=f"h{c}") for c in (0, 2)}
-        for c, at in ((TURNED, H_TURNED_AT), (CHUNKS - 1, H_LAST_AT)):
-            h[c] = shared.tile([P, PLANES, CHUNK], F32, name=f"h{c}", align_bytes=64, offset=at)
+        h = {c: keep.tile([P, PLANES, CHUNK], F32, name=f"h{c}") for c in (FIRST, THIRD)}
+        h[TURNED] = shared_tile("h_turned", [P, PLANES, CHUNK], F32, H_TURNED_AT)
+        h_last = {
+            t0: shared_tile(f"h_last{t0}", [P, PAIR, CHUNK], F32, H_LAST_AT + PAIR_BYTES * t0 // PAIR) for t0 in pairs
+        }
         w = {d0: keep.tile([P, PLANES, d1 - d0], F32, name=f"w{d0}") for d0, d1 in W_PARTS}
 
         def load_dy(t):
             nc.sync.dma_start(dy[t][:, 0:V], dy_rows[:, t, :])
 
         def load_h(c, t0):
-            nc.sync.dma_start(h[c][:, t0 : t0 + PAIR, :], h_rows[:, t0 : t0 + PAIR, c * CHUNK : (c + 1) * CHUNK])
+            planes = h_last[t0][:] if c == LAST else h[c][:, t0 : t0 + PAIR, :]
+            nc.sync.dma_start(planes, h_rows[:, t0 : t0 + PAIR, c * CHUNK : (c + 1) * CHUNK])
 
         load_dy(0)
         nc.sync.dma_start(dst[:], offs)
-        load_h(0, 0)
+        load_h(FIRST, 0)
         load_dy(1)
         load_dy(2)
-        load_h(0, PAIR)
+        load_h(FIRST, PAIR)
         load_dy(3)
-        for c in (2, TURNED, 3):
-            load_h(c, 0)
-            load_h(c, PAIR)
+        for c in (THIRD, TURNED, LAST):
+            for t0 in pairs:
+                load_h(c, t0)
         for d0, d1 in W_PARTS:
             nc.sync.dma_start(w[d0][:], w_rows[:, :, d0:d1])
         nc.sync.dma_start(src[:], offs2)
@@ -87,33 +101,29 @@ def tile_attend_gmp_tnh_kernel(tc, dyT, hE, wm, offs, offs2, out):
         for t in range(PLANES):
             nc.gpsimd.memset(dy[t][:, V:], 0.0)
 
-        blocks = range(0, N_PASS, P)
-        factor_banks = [
-            psum.tile([P, N_PASS], F32, name=f"factor{j}", tag=f"bank{2 + j}") for j in range(CHUNK // P)
-        ]
+        factor_banks = [psum.tile([P, BANK], F32, name=f"factor{j}", tag=f"bank{2 + j}") for j in range(CHUNK // P)]
         for bank in factor_banks:
             for c0 in blocks:
                 nc.tensor.matmul(
                     bank[:, c0 : c0 + P], minus_one[:], identity[:], start=c0 == 0, stop=False, is_transpose=True
                 )
 
-        gathered = [keep.tile([P, PLANES, HALF], F32, name=f"gathered{half}") for half in range(2)]
-        dz16 = {}
+        gathered = [keep.tile([P, PLANES, HALF], F32, name=f"gathered{half}") for half in range(E // HALF)]
         dz_scales = keep.tile([P, E], U8, name="dz_scales", align_bytes=64)
         w_scales = keep.tile([P, D], U8, name="w_scales", align_bytes=64)
-        dm = [keep.tile([P, E], F32, name=f"dm{i}", tag=f"dm{i}") for i in range(DM_TILES)]
+        dm = [keep.tile([P, E], F32, name=f"dm{i}") for i in range(DM_TILES)]
 
-        def gather(on_scalar, dest, window, entries):
-            if on_scalar:
-                nc.scalar.activation(dest, window.indirect(entries), COPY)
+        def gather(engine, picked, window, entries):
+            if engine == "scalar":
+                nc.scalar.activation(picked, window.indirect(entries), COPY)
             else:
-                nc.vector.tensor_copy(dest, window.indirect(entries))
+                nc.vector.tensor_copy(picked, window.indirect(entries))
 
-        def gathered_part(e0, e1):
-            return gathered[e0 // HALF][:, :, e0 % HALF : e0 % HALF + e1 - e0]
+        def flat(planes):
+            return planes.rearrange("p t e -> p (t e)")
 
-        def gather_dy(on_scalar, t, e0, e1):
-            gather(on_scalar, gathered_part(e0, e1)[:, t, :], dy[t][:], dst[:, e0 // STRIPE : e1 // STRIPE])
+        def pair_of(tile, t0):
+            return flat(tile[:, t0 : t0 + PAIR, :])
 
         def row_runs(rows):
             return rows.rearrange("p t (c i) -> p c t i", i=RUN)
@@ -121,64 +131,26 @@ def tile_attend_gmp_tnh_kernel(tc, dyT, hE, wm, offs, offs2, out):
         def interleaved_runs(interleaved):
             return interleaved.rearrange("p (c i t) -> p c t i", i=RUN, t=PLANES)
 
-        def pair_of(tile, t0):
-            return tile[:, t0 : t0 + PAIR, :].rearrange("p t e -> p (t e)")
-
-        def product(c, e0, e1, rows):
-            if e0 == 0 and c in DZ_AT:
-                dz16[c] = shared.tile([P, CHUNK * PLANES], BF16, name=f"dz16_{c}", align_bytes=64, offset=DZ_AT[c])
-            elif e0 == 0:
-                dz16[c] = keep.tile([P, CHUNK * PLANES], BF16, name=f"dz16_{c}", align_bytes=64)
-            nc.vector.tensor_tensor(
-                interleaved_runs(dz16[c][:, e0 * PLANES : e1 * PLANES]),
-                row_runs(gathered_part(c * CHUNK + e0, c * CHUNK + e1)),
-                row_runs(rows),
-                MULT,
-            )
-
-        def quantize_dz(c, codes):
-            nc.vector.quantize_mx(codes.bitcast(E5M2), dz_scales[:, c * CHUNK : (c + 1) * CHUNK], dz16[c][:])
-
-        def multiply(i, e0, parts, bank_number, on_scalar=True):
-            width = sum(codes.shape[1] for codes in parts)
-            bank = psum.tile([P, width], F32, name=f"pass{i}_{e0}", tag=f"bank{bank_number}")
-            c0 = 0
-            for codes in parts:
-                n = codes.shape[1]
-                nc.tensor.matmul_mx(
-                    bank[:, c0 : c0 + n],
-                    lhsT=w_codes[:, i * P : (i + 1) * P].bitcast(E4M3),
-                    lhsT_scale=w_scales[:, i * P : (i + 1) * P],
-                    rhs=codes.bitcast(E5M2),
-                    rhs_scale=dz_scales[:, e0 + c0 : e0 + c0 + n],
-                    start=True,
-                    stop=True,
-                )
-                c0 = c0 + n
-            if on_scalar:
-                nc.scalar.activation(dm[i][:, e0 : e0 + width], bank[:], COPY, scale=-1.0)
-            else:
-                nc.vector.tensor_scalar(dm[i][:, e0 : e0 + width], bank[:], -1.0, 0.0, MULT, ADD)
-
-        pairs = range(0, PLANES, PAIR)
         for t0 in pairs:
-            part = pair_of(h[0], t0)
-            first_squares = shared.tile([P, N_PASS], F32, name=f"first_squares{t0}", align_bytes=64, offset=FIRST_SQUARES_AT)
-            nc.gpsimd.tensor_tensor(first_squares[:], part, part, MULT)
-            nc.gpsimd.tensor_scalar(part, first_squares[:], 1.0, -1.0, MULT, ADD)
+            planes = pair_of(h[FIRST], t0)
+            first_squares = shared_tile(f"first_squares{t0}", [P, PAIR * CHUNK], F32, FIRST_SQUARES_AT)
+            nc.gpsimd.tensor_tensor(first_squares[:], planes, planes, MULT)
+            nc.gpsimd.tensor_scalar(planes, first_squares[:], 1.0, -1.0, MULT, ADD)
 
         for t in range(PLANES):
-            gather_dy(False, t, 0, HALF)
-            gather_dy(True, t, HALF, E)
+            for half, engine in enumerate(("vector", "scalar")):
+                entries = dst[:, half * HALF // STRIPE : (half + 1) * HALF // STRIPE]
+                gather(engine, gathered[half][:, t, :], dy[t][:], entries)
 
         for t0 in pairs:
-            nc.scalar.activation(pair_of(h[2], t0), pair_of(h[2], t0), SQUARE)
+            nc.scalar.activation(pair_of(h[THIRD], t0), pair_of(h[THIRD], t0), SQUARE)
+
         turned_squares = {
-            0: keep.tile([P, N_PASS], F32, name="turned_squares0"),
-            PAIR: shared.tile([P, N_PASS], F32, name="turned_squares2", align_bytes=64, offset=TURNED_SQUARES_AT),
+            0: keep.tile([P, BANK], F32, name="turned_squares0"),
+            PAIR: shared_tile("turned_squares2", [P, BANK], F32, TURNED_SQUARES_AT),
         }
         for t0 in pairs:
-            turned = psum.tile([P, N_PASS], F32, name=f"turned{t0}", tag=f"bank{t0 // PAIR}")
+            turned = psum.tile([P, BANK], F32, name=f"turned{t0}", tag=f"bank{t0 // PAIR}")
             for c0 in blocks:
                 j, t = divmod(c0 // P, PAIR)
                 nc.tensor.transpose(turned[:, c0 : c0 + P], h[TURNED][:, t0 + t, j * P : (j + 1) * P], identity[:])
@@ -195,72 +167,111 @@ def tile_attend_gmp_tnh_kernel(tc, dyT, hE, wm, offs, offs2, out):
                     is_transpose=True,
                 )
 
-        last_squares = shared.tile([P, PLANES, CHUNK], F32, name="last_squares", align_bytes=64, offset=LAST_SQUARES_AT)
-        last_factor = keep.tile([P, PLANES, CHUNK], F32, name="last_factor")
+        last_squares = shared_tile("last_squares", [P, PLANES, CHUNK], F32, H_TURNED_AT)
+        last_factor = shared_tile("last_factor", [P, PLANES, CHUNK], F32, LAST_FACTOR_AT)
         for t0 in pairs:
-            nc.scalar.activation(pair_of(last_squares, t0), pair_of(h[3], t0), SQUARE)
+            nc.scalar.activation(pair_of(last_squares, t0), flat(h_last[t0][:]), SQUARE)
         for t0 in pairs:
             nc.gpsimd.tensor_scalar(pair_of(last_factor, t0), pair_of(last_squares, t0), 1.0, -1.0, MULT, ADD)
-        w16 = {
-            d0: shared.tile(
-                [P, (d1 - d0) * PLANES], BF16, name=f"w16_{d0}", align_bytes=64, offset=H_LAST_AT + 2 * PLANES * d0
-            )
-            for d0, d1 in W_PARTS
-        }
-        for d0, d1 in W_PARTS:
-            nc.scalar.copy(interleaved_runs(w16[d0][:]), row_runs(w[d0][:]))
 
-        w_codes = shared.tile([P, D], U32, name="w_codes", align_bytes=64, offset=TURNED_SQUARES_AT)
+        def w_tile(i):
+            d0 = max(first for first, end in W_PARTS if first <= i * P)
+            return w[d0][:, :, i * P - d0 : (i + 1) * P - d0]
 
-        def quantize_w(d0, d1):
-            nc.vector.quantize_mx(w_codes[:, d0:d1].bitcast(E4M3), w_scales[:, d0:d1], w16[d0][:])
+        w16 = {}
+        for i in range(DM_TILES - 1):
+            w16[i] = shared_tile(f"w16_{i}", [P, P * PLANES], BF16, H_LAST_AT + W16_BYTES * i)
+            nc.scalar.copy(interleaved_runs(w16[i][:]), row_runs(w_tile(i)))
+
+        w_codes = shared_tile("w_codes", [P, D], U32, TURNED_SQUARES_AT)
+
+        def quantize_w(i):
+            columns = slice(i * P, (i + 1) * P)
+            nc.vector.quantize_mx(w_codes[:, columns].bitcast(E4M3), w_scales[:, columns], w16[i][:])
+
+        def product(dz16, e0, e1, factor):
+            planes = gathered[e0 // HALF][:, :, e0 % HALF : e0 % HALF + e1 - e0]
+            place = dz16[:, e0 % CHUNK * PLANES : (e0 % CHUNK + e1 - e0) * PLANES]
+            nc.vector.tensor_tensor(interleaved_runs(place), row_runs(planes), row_runs(factor), MULT)
+
+        def quantize_dz(c, codes, dz16):
+            nc.vector.quantize_mx(codes.bitcast(E5M2), dz_scales[:, c * CHUNK : (c + 1) * CHUNK], dz16[:])
 
         codes_first = keep.tile([P, HALF], U32, name="codes_first", align_bytes=64)
-        product(0, 0, CHUNK, h[0][:])
-        third_factor = shared.tile([P, PLANES, CHUNK], F32, name="third_factor", align_bytes=64, offset=FIRST_SQUARES_AT)
-        nc.vector.tensor_scalar(
-            third_factor[:].rearrange("p t e -> p (t e)"), h[2][:].rearrange("p t e -> p (t e)"), 1.0, -1.0, MULT, ADD
-        )
-        quantize_dz(0, codes_first[:, 0:CHUNK])
-        product(2, 0, CHUNK, third_factor[:])
+        dz_first = keep.tile([P, CHUNK * PLANES], BF16, name="dz_first", align_bytes=64)
+        product(dz_first, FIRST * CHUNK, (FIRST + 1) * CHUNK, h[FIRST][:])
+        third_factor = shared_tile("third_factor", [P, PLANES, CHUNK], F32, FIRST_SQUARES_AT)
+        nc.vector.tensor_scalar(flat(third_factor[:]), flat(h[THIRD][:]), 1.0, -1.0, MULT, ADD)
+        quantize_dz(FIRST, codes_first[:, 0:CHUNK], dz_first)
+        dz_third = keep.tile([P, CHUNK * PLANES], BF16, name="dz_third", align_bytes=64)
+        product(dz_third, THIRD * CHUNK, (THIRD + 1) * CHUNK, third_factor[:])
+        dz_turned = shared_tile("dz_turned", [P, CHUNK * PLANES], BF16, DZ_TURNED_AT)
         for j, bank in enumerate(factor_banks):
-            product(TURNED, j * P, (j + 1) * P, bank[:].rearrange("p (t e) -> p t e", e=P))
-        quantize_w(0, P)
-        quantize_dz(1, codes_first[:, CHUNK:HALF])
-        quantize_w(P, 2 * P)
-        product(3, 0, CHUNK, last_factor[:])
-        codes_rest = shared.tile([P, HALF], U32, name="codes_rest", align_bytes=64, offset=DZ_AT[TURNED])
-        quantize_dz(2, codes_rest[:, 0:CHUNK])
-        quantize_dz(3, codes_rest[:, CHUNK:HALF])
-        quantize_w(2 * P, D)
-        first_half = [codes_first[:]]
-        multiply(0, 0, first_half, 4)
-        multiply(1, 0, first_half, 7)
-        multiply(0, HALF, [codes_rest[:, 0:CHUNK]], 5, on_scalar=False)
-        multiply(0, HALF + CHUNK, [codes_rest[:, CHUNK:HALF]], 6)
-        multiply(1, HALF, [codes_rest[:]], 0)
+            e0 = TURNED * CHUNK + j * P
+            product(dz_turned, e0, e0 + P, bank[:].rearrange("p (t e) -> p t e", e=P))
+        quantize_w(0)
+        quantize_dz(TURNED, codes_first[:, CHUNK:HALF], dz_turned)
+        quantize_w(1)
+        dz_last = shared_tile("dz_last", [P, CHUNK * PLANES], BF16, DZ_LAST_AT)
+        product(dz_last, LAST * CHUNK, (LAST + 1) * CHUNK, last_factor[:])
+        codes_rest = shared_tile("codes_rest", [P, HALF], U32, DZ_TURNED_AT)
+        quantize_dz(THIRD, codes_rest[:, 0:CHUNK], dz_third)
+        quantize_dz(LAST, codes_rest[:, CHUNK:HALF], dz_last)
+        quantize_w(2)
+        w16[3] = shared_tile("w16_3", [P, P * PLANES], BF16, LAST_FACTOR_AT)
+        nc.vector.tensor_copy(interleaved_runs(w16[3][:]), row_runs(w_tile(3)))
+
+        def multiply(i, e0, parts, bank_number, engine="scalar"):
+            width = sum(codes.shape[1] for codes in parts)
+            bank = psum.tile([P, width], F32, name=f"pass{i}_{e0}", tag=f"bank{bank_number}")
+            c0 = 0
+            for codes in parts:
+                n = codes.shape[1]
+                nc.tensor.matmul_mx(
+                    bank[:, c0 : c0 + n],
+                    lhsT=w_codes[:, i * P : (i + 1) * P].bitcast(E4M3),
+                    lhsT_scale=w_scales[:, i * P : (i + 1) * P],
+                    rhs=codes.bitcast(E5M2),
+                    rhs_scale=dz_scales[:, e0 + c0 : e0 + c0 + n],
+                    start=True,
+                    stop=True,
+                )
+                c0 = c0 + n
+            if engine == "scalar":
+                nc.scalar.activation(dm[i][:, e0 : e0 + width], bank[:], COPY, scale=-1.0)
+            else:
+                nc.vector.tensor_scalar(dm[i][:, e0 : e0 + width], bank[:], -1.0, 0.0, MULT, ADD)
+
         picked = {}
 
-        def gather_dm(on_scalar, i, c0, n):
-            picked[i, c0] = keep.tile([P, n], F32, name=f"picked{i}_{c0}")
-            gather(on_scalar, picked[i, c0][:], dm[i][:], src[:, c0 // STRIPE : (c0 + n) // STRIPE])
+        def gather_dm(engine, i, c0, c1):
+            picked[i, c0] = keep.tile([P, c1 - c0], F32, name=f"picked{i}_{c0}")
+            gather(engine, picked[i, c0][:], dm[i][:], src[:, c0 // STRIPE : c1 // STRIPE])
 
-        gather_dm(False, 0, 0, 512)
-        gather_dm(True, 0, 512, 512)
-        multiply(2, 0, first_half, 1)
+        multiply(0, 0, [codes_first[:, 0:CHUNK], codes_first[:, CHUNK:HALF]], 4)
+        multiply(1, 0, [codes_first[:]], 7)
+        multiply(0, THIRD * CHUNK, [codes_rest[:, 0:CHUNK]], 5, engine="vector")
+        quantize_w(3)
+        multiply(0, LAST * CHUNK, [codes_rest[:, CHUNK:HALF]], 6)
+        multiply(1, HALF, [codes_rest[:]], 0)
+
+        gather_dm("vector", 0, 0, HALF)
+        gather_dm("scalar", 0, HALF, E)
+        multiply(2, 0, [codes_first[:]], 1)
         multiply(2, HALF, [codes_rest[:]], 2)
-        multiply(3, 0, first_half, 3)
+        multiply(3, 0, [codes_first[:]], 3)
         multiply(3, HALF, [codes_rest[:]], 4)
-        gather_dm(False, 1, 0, 512)
-        gather_dm(False, 1, 512, 512)
-        gather_dm(False, 2, 0, 512)
-        gather_dm(False, 2, 512, 384)
-        gather_dm(True, 3, 0, 512)
-        gather_dm(True, 3, 512, 512)
-        gather_dm(True, 2, 896, 128)
-        for number, ((i, c0), tile) in enumerate(picked.items()):
-            n = tile.shape[1]
+        gather_dm("vector", 1, 0, HALF)
+        gather_dm("vector", 1, HALF, E)
+        gather_dm("vector", 2, 0, HALF)
+        gather_dm("vector", 2, HALF, E - SHORT_CUT)
+        gather_dm("scalar", 3, 0, HALF)
+        gather_dm("scalar", 3, HALF, E)
+        gather_dm("scalar", 2, E - SHORT_CUT, E)
+
+        for number, ((i, c0), columns) in enumerate(picked.items()):
+            n = columns.shape[1]
             total = keep.tile([P, n // K], F32, name=f"total{i}_{c0}")
-            adder = nc.gpsimd if number < 5 else nc.vector
-            adder.tensor_tensor(total[:], tile[:, 0:n:K], tile[:, 1:n:K], ADD)
+            adder = nc.gpsimd if number < GPSIMD_CUTS else nc.vector
+            adder.tensor_tensor(total[:], columns[:, 0:n:K], columns[:, 1:n:K], ADD)
             nc.sync.dma_start(out[i * P : (i + 1) * P, c0 // K : (c0 + n) // K], total[:])

from contextlib import ExitStack

import concourse.mybir as mybir
from concourse.masks import make_identity

V, K, E, D, DV = 512, 2, 1024, 512, 512
FLOPS = 2 * DV * D * E

F32 = mybir.dt.float32
BF16 = mybir.dt.bfloat16
U32 = mybir.dt.uint32
U16 = mybir.dt.uint16
U8 = mybir.dt.uint8
E4M3 = mybir.dt.float8_e4m3fn_x4
E5M2 = mybir.dt.float8_e5m2_x4
MULT = mybir.AluOpType.mult
ADD = mybir.AluOpType.add
COPY = mybir.ActivationFunctionType.Copy
SQUARE = mybir.ActivationFunctionType.Square

P = 128
PLANES = 4
PAIR = 2
BANK = 512
STRIPE = 16
RUN = 4
CHUNK = 256
HALF = E // 2
DM_TILES = D // P
DY_PAD = 16
SHORT_CUT = 128
GPSIMD_CUTS = 5

FIRST, TURNED, THIRD, LAST = range(E // CHUNK)
W_PARTS = ((0, P), (P, 2 * P), (2 * P, D))

PAIR_BYTES = 4 * PAIR * CHUNK
W16_BYTES = 2 * PLANES * P
H_TURNED_AT = 0
H_LAST_AT = H_TURNED_AT + 2 * PAIR_BYTES
DZ_LAST_AT = H_LAST_AT - W16_BYTES
TURNED_SQUARES_AT = H_LAST_AT + 2 * PAIR_BYTES
FIRST_SQUARES_AT = TURNED_SQUARES_AT + 2 * PAIR_BYTES
DZ_TURNED_AT = FIRST_SQUARES_AT + 2 * PAIR_BYTES
LAST_FACTOR_AT = DZ_TURNED_AT + 2 * PAIR_BYTES


def tile_attend_gmp_tnh_kernel(tc, dyT, hE, wm, offs, offs2, out):
    nc = tc.nc
    dy_rows = dyT.rearrange("(p t) v -> p t v", t=PLANES)
    h_rows = hE.rearrange("(p t) e -> p t e", t=PLANES)
    w_rows = wm.rearrange("(p t) d -> p t d", t=PLANES)
    pairs = range(0, PLANES, PAIR)
    blocks = range(0, BANK, P)

    with ExitStack() as ctx:
        keep = ctx.enter_context(tc.tile_pool(name="keep", bufs=1))
        shared = ctx.enter_context(tc.tile_pool(name="shared", bufs=1))
        psum = ctx.enter_context(tc.psum_pool(name="psum", bufs=1))

        def shared_tile(name, shape, dtype, at):
            return shared.tile(shape, dtype, name=name, align_bytes=64, offset=at)

        dst = keep.tile([P, E // STRIPE], U16, name="dst")
        src = keep.tile([P, E // STRIPE], U16, name="src")
        dy = [keep.tile([P, V + DY_PAD], F32, name=f"dy{t}") for t in range(PLANES)]
        h = {c: keep.tile([P, PLANES, CHUNK], F32, name=f"h{c}") for c in (FIRST, THIRD)}
        h[TURNED] = shared_tile("h_turned", [P, PLANES, CHUNK], F32, H_TURNED_AT)
        h_last = {
            t0: shared_tile(f"h_last{t0}", [P, PAIR, CHUNK], F32, H_LAST_AT + PAIR_BYTES * t0 // PAIR) for t0 in pairs
        }
        w = {d0: keep.tile([P, PLANES, d1 - d0], F32, name=f"w{d0}") for d0, d1 in W_PARTS}

        def load_dy(t):
            nc.sync.dma_start(dy[t][:, 0:V], dy_rows[:, t, :])

        def load_h(c, t0):
            planes = h_last[t0][:] if c == LAST else h[c][:, t0 : t0 + PAIR, :]
            nc.sync.dma_start(planes, h_rows[:, t0 : t0 + PAIR, c * CHUNK : (c + 1) * CHUNK])

        load_dy(0)
        nc.sync.dma_start(dst[:], offs)
        load_h(FIRST, 0)
        load_dy(1)
        load_dy(2)
        load_h(FIRST, PAIR)
        load_dy(3)
        for c in (THIRD, TURNED, LAST):
            for t0 in pairs:
                load_h(c, t0)
        for d0, d1 in W_PARTS:
            nc.sync.dma_start(w[d0][:], w_rows[:, :, d0:d1])
        nc.sync.dma_start(src[:], offs2)

        zero = keep.tile([P, P], F32, name="zero")
        nc.vector.memset(zero[:], 0.0)
        minus_one = keep.tile([P, P], F32, name="minus_one")
        nc.scalar.activation(minus_one[:], zero[:], COPY, bias=-1.0)
        identity = keep.tile([P, P], F32, name="identity")
        make_identity(nc, identity[:])
        for t in range(PLANES):
            nc.gpsimd.memset(dy[t][:, V:], 0.0)

        factor_banks = [psum.tile([P, BANK], F32, name=f"factor{j}", tag=f"bank{2 + j}") for j in range(CHUNK // P)]
        for bank in factor_banks:
            for c0 in blocks:
                nc.tensor.matmul(
                    bank[:, c0 : c0 + P], minus_one[:], identity[:], start=c0 == 0, stop=False, is_transpose=True
                )

        gathered = [keep.tile([P, PLANES, HALF], F32, name=f"gathered{half}") for half in range(E // HALF)]
        dz_scales = keep.tile([P, E], U8, name="dz_scales", align_bytes=64)
        w_scales = keep.tile([P, D], U8, name="w_scales", align_bytes=64)
        dm = [keep.tile([P, E], F32, name=f"dm{i}") for i in range(DM_TILES)]

        def gather(engine, picked, window, entries):
            if engine == "scalar":
                nc.scalar.activation(picked, window.indirect(entries), COPY)
            else:
                nc.vector.tensor_copy(picked, window.indirect(entries))

        def flat(planes):
            return planes.rearrange("p t e -> p (t e)")

        def pair_of(tile, t0):
            return flat(tile[:, t0 : t0 + PAIR, :])

        def row_runs(rows):
            return rows.rearrange("p t (c i) -> p c t i", i=RUN)

        def interleaved_runs(interleaved):
            return interleaved.rearrange("p (c i t) -> p c t i", i=RUN, t=PLANES)

        for t0 in pairs:
            planes = pair_of(h[FIRST], t0)
            first_squares = shared_tile(f"first_squares{t0}", [P, PAIR * CHUNK], F32, FIRST_SQUARES_AT)
            nc.gpsimd.tensor_tensor(first_squares[:], planes, planes, MULT)
            nc.gpsimd.tensor_scalar(planes, first_squares[:], 1.0, -1.0, MULT, ADD)

        for t in range(PLANES):
            for half, engine in enumerate(("vector", "scalar")):
                entries = dst[:, half * HALF // STRIPE : (half + 1) * HALF // STRIPE]
                gather(engine, gathered[half][:, t, :], dy[t][:], entries)

        for t0 in pairs:
            nc.scalar.activation(pair_of(h[THIRD], t0), pair_of(h[THIRD], t0), SQUARE)

        turned_squares = {
            0: keep.tile([P, BANK], F32, name="turned_squares0"),
            PAIR: shared_tile("turned_squares2", [P, BANK], F32, TURNED_SQUARES_AT),
        }
        for t0 in pairs:
            turned = psum.tile([P, BANK], F32, name=f"turned{t0}", tag=f"bank{t0 // PAIR}")
            for c0 in blocks:
                j, t = divmod(c0 // P, PAIR)
                nc.tensor.transpose(turned[:, c0 : c0 + P], h[TURNED][:, t0 + t, j * P : (j + 1) * P], identity[:])
            nc.scalar.activation(turned_squares[t0][:], turned[:], SQUARE)
        for t0 in pairs:
            for c0 in blocks:
                j, t = divmod(c0 // P, PAIR)
                nc.tensor.matmul(
                    factor_banks[j][:, (t0 + t) * P : (t0 + t + 1) * P],
                    turned_squares[t0][:, c0 : c0 + P],
                    identity[:],
                    start=False,
                    stop=t0 + t == PLANES - 1,
                    is_transpose=True,
                )

        last_squares = shared_tile("last_squares", [P, PLANES, CHUNK], F32, H_TURNED_AT)
        last_factor = shared_tile("last_factor", [P, PLANES, CHUNK], F32, LAST_FACTOR_AT)
        for t0 in pairs:
            nc.scalar.activation(pair_of(last_squares, t0), flat(h_last[t0][:]), SQUARE)
        for t0 in pairs:
            nc.gpsimd.tensor_scalar(pair_of(last_factor, t0), pair_of(last_squares, t0), 1.0, -1.0, MULT, ADD)

        def w_tile(i):
            d0 = max(first for first, end in W_PARTS if first <= i * P)
            return w[d0][:, :, i * P - d0 : (i + 1) * P - d0]

        w16 = {}
        for i in range(DM_TILES - 1):
            w16[i] = shared_tile(f"w16_{i}", [P, P * PLANES], BF16, H_LAST_AT + W16_BYTES * i)
            nc.scalar.copy(interleaved_runs(w16[i][:]), row_runs(w_tile(i)))

        w_codes = shared_tile("w_codes", [P, D], U32, TURNED_SQUARES_AT)

        def quantize_w(i):
            columns = slice(i * P, (i + 1) * P)
            nc.vector.quantize_mx(w_codes[:, columns].bitcast(E4M3), w_scales[:, columns], w16[i][:])

        def product(dz16, e0, e1, factor):
            planes = gathered[e0 // HALF][:, :, e0 % HALF : e0 % HALF + e1 - e0]
            place = dz16[:, e0 % CHUNK * PLANES : (e0 % CHUNK + e1 - e0) * PLANES]
            nc.vector.tensor_tensor(interleaved_runs(place), row_runs(planes), row_runs(factor), MULT)

        def quantize_dz(c, codes, dz16):
            nc.vector.quantize_mx(codes.bitcast(E5M2), dz_scales[:, c * CHUNK : (c + 1) * CHUNK], dz16[:])

        codes_first = keep.tile([P, HALF], U32, name="codes_first", align_bytes=64)
        dz_first = keep.tile([P, CHUNK * PLANES], BF16, name="dz_first", align_bytes=64)
        product(dz_first, FIRST * CHUNK, (FIRST + 1) * CHUNK, h[FIRST][:])
        third_factor = shared_tile("third_factor", [P, PLANES, CHUNK], F32, FIRST_SQUARES_AT)
        nc.vector.tensor_scalar(flat(third_factor[:]), flat(h[THIRD][:]), 1.0, -1.0, MULT, ADD)
        quantize_dz(FIRST, codes_first[:, 0:CHUNK], dz_first)
        dz_third = keep.tile([P, CHUNK * PLANES], BF16, name="dz_third", align_bytes=64)
        product(dz_third, THIRD * CHUNK, (THIRD + 1) * CHUNK, third_factor[:])
        dz_turned = shared_tile("dz_turned", [P, CHUNK * PLANES], BF16, DZ_TURNED_AT)
        for j, bank in enumerate(factor_banks):
            e0 = TURNED * CHUNK + j * P
            product(dz_turned, e0, e0 + P, bank[:].rearrange("p (t e) -> p t e", e=P))
        quantize_w(0)
        quantize_dz(TURNED, codes_first[:, CHUNK:HALF], dz_turned)
        quantize_w(1)
        dz_last = shared_tile("dz_last", [P, CHUNK * PLANES], BF16, DZ_LAST_AT)
        product(dz_last, LAST * CHUNK, (LAST + 1) * CHUNK, last_factor[:])
        codes_rest = shared_tile("codes_rest", [P, HALF], U32, DZ_TURNED_AT)
        quantize_dz(THIRD, codes_rest[:, 0:CHUNK], dz_third)
        quantize_dz(LAST, codes_rest[:, CHUNK:HALF], dz_last)
        quantize_w(2)
        w16[3] = shared_tile("w16_3", [P, P * PLANES], BF16, LAST_FACTOR_AT)
        nc.vector.tensor_copy(interleaved_runs(w16[3][:]), row_runs(w_tile(3)))

        def multiply(i, e0, parts, bank_number, engine="scalar"):
            width = sum(codes.shape[1] for codes in parts)
            bank = psum.tile([P, width], F32, name=f"pass{i}_{e0}", tag=f"bank{bank_number}")
            c0 = 0
            for codes in parts:
                n = codes.shape[1]
                nc.tensor.matmul_mx(
                    bank[:, c0 : c0 + n],
                    lhsT=w_codes[:, i * P : (i + 1) * P].bitcast(E4M3),
                    lhsT_scale=w_scales[:, i * P : (i + 1) * P],
                    rhs=codes.bitcast(E5M2),
                    rhs_scale=dz_scales[:, e0 + c0 : e0 + c0 + n],
                    start=True,
                    stop=True,
                )
                c0 = c0 + n
            if engine == "scalar":
                nc.scalar.activation(dm[i][:, e0 : e0 + width], bank[:], COPY, scale=-1.0)
            else:
                nc.vector.tensor_scalar(dm[i][:, e0 : e0 + width], bank[:], -1.0, 0.0, MULT, ADD)

        picked = {}

        def gather_dm(engine, i, c0, c1):
            picked[i, c0] = keep.tile([P, c1 - c0], F32, name=f"picked{i}_{c0}")
            gather(engine, picked[i, c0][:], dm[i][:], src[:, c0 // STRIPE : c1 // STRIPE])

        multiply(0, 0, [codes_first[:, 0:CHUNK], codes_first[:, CHUNK:HALF]], 4)
        multiply(1, 0, [codes_first[:]], 7)
        multiply(0, THIRD * CHUNK, [codes_rest[:, 0:CHUNK]], 5, engine="vector")
        quantize_w(3)
        multiply(0, LAST * CHUNK, [codes_rest[:, CHUNK:HALF]], 6)
        multiply(1, HALF, [codes_rest[:]], 0)

        gather_dm("vector", 0, 0, HALF)
        gather_dm("scalar", 0, HALF, E)
        multiply(2, 0, [codes_first[:]], 1)
        multiply(2, HALF, [codes_rest[:]], 2)
        multiply(3, 0, [codes_first[:]], 3)
        multiply(3, HALF, [codes_rest[:]], 4)
        gather_dm("vector", 1, 0, HALF)
        gather_dm("vector", 1, HALF, E)
        gather_dm("vector", 2, 0, HALF)
        gather_dm("vector", 2, HALF, E - SHORT_CUT)
        gather_dm("scalar", 3, 0, HALF)
        gather_dm("scalar", 3, HALF, E)
        gather_dm("scalar", 2, E - SHORT_CUT, E)

        for number, ((i, c0), columns) in enumerate(picked.items()):
            n = columns.shape[1]
            total = keep.tile([P, n // K], F32, name=f"total{i}_{c0}")
            adder = nc.gpsimd if number < GPSIMD_CUTS else nc.vector
            adder.tensor_tensor(total[:], columns[:, 0:n:K], columns[:, 1:n:K], ADD)
            nc.sync.dma_start(out[i * P : (i + 1) * P, c0 // K : (c0 + n) // K], total[:])
